import numpy as np
import ml_dtypes


def mxq(x, axis, fmt="e4m3"):
    dtype, down = {"e4m3": (ml_dtypes.float8_e4m3fn, 7), "e5m2": (ml_dtypes.float8_e5m2, 14)}[fmt]
    v = np.moveaxis(np.asarray(x, np.float32).astype(ml_dtypes.bfloat16).astype(np.float64), axis, -1)
    blocks = v.reshape(v.shape[:-1] + (-1, 32))
    amax = np.abs(blocks).max(-1, keepdims=True)
    byte = np.maximum(np.where(amax > 0, np.frexp(amax)[1] - 1 + 127, 0) - down, 1)
    scale = np.exp2(byte - 127.0)
    codes = (blocks / scale).astype(np.float32).astype(dtype).astype(np.float64)
    return np.moveaxis((codes * scale).reshape(v.shape), -1, axis)


WIDE = False


def mx_kscale(k):
    if not WIDE:
        return np.ones(k)
    levels = np.array([10, -10, 5, -5, 0])
    if k % 512:
        return np.exp2(np.random.permutation(np.resize(levels, k // 32))).repeat(32)
    a = np.empty((k // 512, 16))
    for p in range(k // 512):
        a[p, :8] = np.random.permutation(np.resize(levels, 8))
        for g in range(8):
            far = levels[np.abs(levels - a[p, g]) >= 10]
            a[p, g + 8] = far[np.random.randint(len(far))]
    return np.exp2(a.ravel()).repeat(32)


def f64(x):
    return np.asarray(x).astype(np.float64)


def striped(idx):
    return np.tile(np.asarray(idx).reshape(-1, 16).T, (8, 1)).astype(np.uint16)


def unstriped(offs):
    return offs[:16].T.reshape(-1).astype(np.int64)


E2M1 = np.array([0.0, 0.5, 1.0, 1.5, 2.0, 3.0, 4.0, 6.0, -0.0, -0.5, -1.0, -1.5, -2.0, -3.0, -4.0, -6.0])


def pack_weight(w, fmt):
    k, n = w.shape
    w = f64(np.asarray(w, np.float32).astype(ml_dtypes.bfloat16)).reshape(k // 32, 32, n)
    amax = np.abs(w).max(1)
    if fmt == "e4m3":
        byte = np.frexp(amax)[1] - 1 + 127 - 7
    else:
        mant, ex = np.frexp(amax / 6.0)
        byte = np.where(mant > 0.5, ex, ex - 1) + 127
    byte = np.clip(np.where(amax > 0, byte, 1), 1, 254)
    scaled = (w * np.exp2(127.0 - byte)[:, None, :]).reshape(k, n).astype(np.float32)
    by_word = np.ascontiguousarray(scaled.reshape(k // 512, 128, 4, n).transpose(0, 1, 3, 2))
    if fmt == "e4m3":
        words = by_word.astype(ml_dtypes.float8_e4m3fn).view(np.uint8)
    else:
        c = by_word.astype(ml_dtypes.float4_e2m1fn).view(np.uint8) & 0xF
        words = (c[..., 0::2] | (c[..., 1::2] << 4)).reshape(k // 512, 128, 2 * n)
    return np.ascontiguousarray(words), np.ascontiguousarray(byte.astype(np.uint8).reshape(k // 512, 16, n))


def unpack_weight(words, scales, fmt):
    g, _, n = scales.shape
    words = np.ascontiguousarray(words).reshape(g, 128, n, -1)
    if fmt == "e4m3":
        vals = words.view(ml_dtypes.float8_e4m3fn).astype(np.float64)
    else:
        nib = np.empty((g, 128, n, 4), np.uint8)
        nib[..., 0::2] = words & 0xF
        nib[..., 1::2] = words >> 4
        vals = E2M1[nib]
    vals = vals * np.repeat(np.exp2(scales.astype(np.float64) - 127.0), 8, axis=1)[..., None]
    return vals.transpose(0, 1, 3, 2).reshape(g * 512, n)


B, N, T, D, DV, NQ = 2, 512, 2048, 512, 256, 128
PAGE = 64


def setup_inputs():
    n = np.random.standard_normal
    pages = np.random.permutation(T // PAGE)[:B * N // PAGE]
    idx = (pages[:, None] * PAGE + np.arange(PAGE)[None, :]).reshape(-1)
    s = mx_kscale(D)[:, None]
    u = np.ones(T)
    u[idx] = mx_kscale(B * N)
    r = np.random.uniform(0.5, 2.0, T)
    k = n((D, T)) / s
    v = n((DV, T)) / (u * r)
    kp = pack_weight(k, "e4m3")
    return {
        "qT": (n((B, D, NQ)) * s * (0.60 / np.sqrt(D))).astype(np.float32),
        "k_words": kp[0],
        "k_scales": kp[1],
        "vT": v.astype(np.float32),
        "vs": np.tile(u * r, (128, 1)).astype(np.float32),
        "sink": (2.0 + 3.0 * n((B, NQ, 1))).astype(np.float32),
        "offs": striped(idx),
    }


def reference(qT, k_words, k_scales, vT, vs, sink, offs):
    idx = unstriped(offs)
    k = unpack_weight(k_words, k_scales, "e4m3")
    v = f64(vT)
    pick = lambda x: x[:, idx].reshape(x.shape[0], B, N).transpose(1, 0, 2)
    q = f64(qT)
    score = mxq(q, 1, "e4m3").transpose(0, 2, 1) @ pick(k)
    m = np.maximum(score.max(-1, keepdims=True), f64(sink))
    p = np.exp(score - m)
    total = p.sum(-1, keepdims=True) + np.exp(f64(sink) - m)
    w = p * pick(f64(vs))[:, :1, :]
    y = mxq(w, 2, "e4m3") @ mxq(pick(v).transpose(0, 2, 1), 1, "e4m3")
    y = y / total
    return y

@@ -1,0 +1,209 @@
+from contextlib import ExitStack
+
+import concourse.mybir as mybir
+from concourse.masks import make_identity
+
+B, N, T, D, DV, NQ = 2, 512, 2048, 512, 256, 128
+FLOPS = 2 * B * NQ * N * (D + DV)
+
+F32 = mybir.dt.float32
+BF16 = mybir.dt.bfloat16
+I32 = mybir.dt.int32
+U32 = mybir.dt.uint32
+U16 = mybir.dt.uint16
+U8 = mybir.dt.uint8
+FP8X4 = mybir.dt.float8_e4m3fn_x4
+ALU = mybir.AluOpType
+ACT = mybir.ActivationFunctionType
+
+P = 128
+PACK = 4
+LIST_COLS = N // 16
+BLOCKS = DV // P
+
+
+def tile_attend_sink_kernel(tc, qT, k_words, k_scales, vT, vs, sink, offs, out):
+    nc = tc.nc
+    with ExitStack() as ctx:
+        held = ctx.enter_context(tc.tile_pool(name="held", bufs=1))
+        psum = ctx.enter_context(tc.psum_pool(name="psum", bufs=1))
+
+        def sb(name, shape, dtype):
+            return held.tile(shape, dtype, name=name, align_bytes=64)
+
+        def bank(index, name):
+            return psum.tile([P, 512], F32, name=name, tag="bank%d" % index)
+
+        offsets = held.tile([P, B * LIST_COLS], U16, name="offsets")
+        nc.sync.dma_start(offsets[:], offs)
+
+        def listed(b):
+            return offsets[:, b * LIST_COLS : (b + 1) * LIST_COLS]
+
+        ks_pool = sb("ks_pool", [P, T // 4], I32)
+        vs_pool = sb("vs_pool", [P, T], F32)
+        nc.vector.memset(ks_pool[:], 0)
+        nc.vector.memset(vs_pool[:], 0.0)
+
+        q_raw = sb("q_raw", [P, B, PACK, NQ], F32)
+        nc.sync.dma_start(
+            q_raw[:].rearrange("p b j q -> p b (j q)"),
+            qT.rearrange("b (p j) q -> p b (j q)", j=PACK),
+        )
+        kw_pool = sb("kw_pool", [P, T], U32)
+        nc.sync.dma_start(kw_pool[:].bitcast(I32), k_words[0].rearrange("p n r -> p (n r)").bitcast(I32))
+        v_pool = [sb("v_pool%d" % h, [P, T], F32) for h in range(BLOCKS)]
+        for h in range(BLOCKS):
+            nc.sync.dma_start(v_pool[h][:], vT[h * P : (h + 1) * P, :])
+
+        ks_rows = k_scales[0].bitcast(I32)
+        for r in range(4):
+            nc.scalar.dma_start(ks_pool[r:P:32, :], ks_rows[r:16:4, :])
+
+        sink_raw = sb("sink_raw", [P, B], F32)
+        with nc.allow_non_contiguous_dma(reason="one logit a query row and sequence"):
+            nc.gpsimd.dma_start(sink_raw[:], sink.rearrange("b q o -> q (b o)"))
+        ident = sb("ident", [P, P], F32)
+        make_identity(nc, ident[:])
+        nc.gpsimd.dma_start(vs_pool[0:1, :], vs[0:1, :])
+
+        warm = sb("warm", [P, 1], F32)
+        nc.scalar.activation(warm[:], ident[:, 0:1], ACT.Exp)
+
+        ks_got = sb("ks_got", [P, B * N], U8)
+        nc.vector.tensor_copy(ks_got[:], ks_pool[:].bitcast(U8).indirect(offsets[:]))
+
+        q_codes = sb("q_codes", [P, B, NQ], U32)
+        q_scales = sb("q_scales", [P, B, NQ], U8)
+        neg = [sb("neg%d" % b, [P, N + 1], F32) for b in range(B)]
+        for b in range(B):
+            q_bf = sb("q_bf%d" % b, [P, NQ, PACK], BF16)
+            nc.scalar.copy(q_bf[:], q_raw[:, b].rearrange("p j q -> p q j"))
+            nc.vector.tensor_scalar(neg[b][:, N : N + 1], sink_raw[:, b : b + 1], -1.0, None, ALU.mult)
+            nc.vector.quantize_mx(
+                out=q_codes[:, b, :].bitcast(FP8X4),
+                scales=q_scales[:, b, :],
+                in_=q_bf[:].rearrange("p q j -> p (q j)"),
+            )
+
+        vs_got = sb("vs_got", [P, B * N], F32)
+        nc.vector.tensor_copy(vs_got[:], vs_pool[:].indirect(offsets[:]))
+
+        kw_got = [sb("kw_got%d" % b, [P, N], U32) for b in range(B)]
+        scores = []
+        for b in range(B):
+            nc.vector.tensor_copy(kw_got[b][:], kw_pool[:].indirect(listed(b)))
+            acc = bank(b, "scores%d" % b)
+            nc.tensor.matmul_mx(
+                out=acc[:],
+                lhsT=q_codes[:, b, :].bitcast(FP8X4),
+                lhsT_scale=q_scales[:, b, :],
+                rhs=kw_got[b][:].bitcast(FP8X4),
+                rhs_scale=ks_got[:, b * N : (b + 1) * N],
+                start=True,
+                stop=True,
+            )
+            scores.append(acc)
+
+        vs_col = []
+        for b in range(B):
+            turned = bank(2 + b, "vs_turned%d" % b)
+            for t in range(PACK):
+                nc.tensor.transpose(
+                    turned[:, t * P : (t + 1) * P], vs_got[:, b * N + t : (b + 1) * N : PACK], ident[:]
+                )
+            col = sb("vs_col%d" % b, [P, PACK], F32)
+            nc.scalar.copy(col[:], turned[:, 0 : PACK * P : P])
+            vs_col.append(col)
+
+        probs, totals, p_turned = [], [], []
+        for b in range(B):
+            neg_max = sb("neg_max%d" % b, [P, 1], F32)
+            nc.vector.tensor_scalar(
+                neg[b][:, 0:N].rearrange("p (t s) -> p t s", t=PACK),
+                scores[b][:].rearrange("p (s t) -> p t s", t=PACK),
+                -1.0,
+                neg[b][:, N : N + 1],
+                ALU.mult,
+                ALU.min,
+                accum_out=neg_max[:],
+            )
+            p = sb("p%d" % b, [P, N + 1], F32)
+            total = sb("total%d" % b, [P, 1], F32)
+            nc.scalar.activation(p[:], neg[b][:], ACT.Exp, bias=neg_max[:], scale=-1.0, accum_out=total[:])
+            turned = bank(4 + b, "p_turned%d" % b)
+            for t in range(PACK):
+                nc.tensor.transpose(turned[:, t * P : (t + 1) * P], p[:, t * P : (t + 1) * P], ident[:])
+            totals.append(total)
+            p_turned.append(turned)
+
+        def gather_values(h, b, bank_index):
+            got = sb("v_got%d%d" % (h, b), [P, 2, P, 2], BF16)
+            nc.vector.tensor_copy(got[:].rearrange("e u s i -> e s u i"), v_pool[h][:].indirect(listed(b)))
+            words = got[:].rearrange("e u s i -> e (u s i)").bitcast(F32)
+            turned = bank(bank_index, "v_turned%d%d" % (h, b))
+            for u in range(2):
+                nc.tensor.transpose(turned[:, u * P : (u + 1) * P], words[:, u * P : (u + 1) * P], ident[:])
+            v_bf = sb("v_bf%d%d" % (h, b), [P, P * PACK], BF16)
+            nc.scalar.copy(
+                v_bf[:].bitcast(F32).rearrange("s (e u) -> s e u", u=2),
+                turned[:, 0 : 2 * P].rearrange("s (u e) -> s e u", u=2),
+            )
+            return v_bf
+
+        def quantize(name, values):
+            codes = sb(name + "_codes", [P, P], U32)
+            scales = sb(name + "_scales", [P, P], U8)
+            nc.vector.quantize_mx(out=codes[:].bitcast(FP8X4), scales=scales[:], in_=values[:])
+            return codes, scales
+
+        def weigh(b):
+            w_bf = sb("w_bf%d" % b, [P, NQ * PACK], BF16)
+            nc.vector.tensor_tensor(
+                w_bf[:].rearrange("s (q t) -> s q t", t=PACK),
+                p_turned[b][:].rearrange("s (t q) -> s q t", t=PACK),
+                vs_col[b][:].unsqueeze(1).to_broadcast([P, NQ, PACK]),
+                ALU.mult,
+            )
+            return w_bf
+
+        def finish(h, b, w, v, inverse, bank_index, on_vector):
+            acc = bank(bank_index, "y%d%d" % (h, b))
+            nc.tensor.matmul_mx(
+                out=acc[:, 0:P],
+                lhsT=w[0][:].bitcast(FP8X4),
+                lhsT_scale=w[1][:],
+                rhs=v[0][:].bitcast(FP8X4),
+                rhs_scale=v[1][:],
+                start=True,
+                stop=True,
+            )
+            y = sb("y_out%d%d" % (h, b), [P, P], F32)
+            if on_vector:
+                nc.vector.tensor_scalar(y[:], acc[:, 0:P], inverse[:], None, ALU.mult)
+            else:
+                nc.scalar.activation(y[:], acc[:, 0:P], ACT.Copy, scale=inverse[:])
+            nc.sync.dma_start(out[b, :, h * P : (h + 1) * P], y[:])
+
+        v_bf = {}
+        v_bf[0, 0] = gather_values(0, 0, 6)
+        w_bf0 = weigh(0)
+        v_bf[0, 1] = gather_values(0, 1, 7)
+        w_bf1 = weigh(1)
+        inverse = []
+        for b in range(B):
+            inv = sb("inverse%d" % b, [P, 1], F32)
+            nc.vector.reciprocal(inv[:], totals[b][:])
+            inverse.append(inv)
+        w = [quantize("w0", w_bf0)]
+        v00 = quantize("v00", v_bf[0, 0])
+        w.append(quantize("w1", w_bf1))
+        v01 = quantize("v01", v_bf[0, 1])
+        v_bf[1, 0] = gather_values(1, 0, 2)
+        v_bf[1, 1] = gather_values(1, 1, 3)
+        finish(0, 0, w[0], v00, inverse[0], 0, False)
+        finish(0, 1, w[1], v01, inverse[1], 1, False)
+        v10 = quantize("v10", v_bf[1, 0])
+        v11 = quantize("v11", v_bf[1, 1])
+        finish(1, 0, w[0], v10, inverse[0], 4, False)
+        finish(1, 1, w[1], v11, inverse[1], 5, True)

@@ -28,8 +28,8 @@ def tile_attend_sink_kernel(tc, qT, k_words, k_scales, vT, vs, sink, offs, out):
         held = ctx.enter_context(tc.tile_pool(name="held", bufs=1))
         psum = ctx.enter_context(tc.psum_pool(name="psum", bufs=1))
 
-        def sb(name, shape, dtype):
-            return held.tile(shape, dtype, name=name, align_bytes=64)
+        def sb(name, shape, dtype, tag=None):
+            return held.tile(shape, dtype, name=name, tag=tag or name, align_bytes=64)
 
         def bank(index, name):
             return psum.tile([P, 512], F32, name=name, tag="bank%d" % index)
@@ -42,33 +42,32 @@ def tile_attend_sink_kernel(tc, qT, k_words, k_scales, vT, vs, sink, offs, out):
 
         ks_pool = sb("ks_pool", [P, T // 4], I32)
         vs_pool = sb("vs_pool", [P, T], F32)
+        sink_rows = sb("sink_rows", [P, NQ], F32)
         nc.vector.memset(ks_pool[:], 0)
         nc.vector.memset(vs_pool[:], 0.0)
+
+        ident = sb("ident", [P, P], F32)
+        nc.gpsimd.memset(sink_rows[:], 0.0)
+        make_identity(nc, ident[:])
 
         q_raw = sb("q_raw", [P, B, PACK, NQ], F32)
         nc.sync.dma_start(
             q_raw[:].rearrange("p b j q -> p b (j q)"),
             qT.rearrange("b (p j) q -> p b (j q)", j=PACK),
         )
+        ks_rows = k_scales[0].bitcast(I32)
+        for r in range(4):
+            nc.sync.dma_start(ks_pool[r:P:32, :], ks_rows[r:16:4, :])
+        nc.sync.dma_start(vs_pool[0:1, :], vs[0:1, :])
         kw_pool = sb("kw_pool", [P, T], U32)
         nc.sync.dma_start(kw_pool[:].bitcast(I32), k_words[0].rearrange("p n r -> p (n r)").bitcast(I32))
+        nc.sync.dma_start(sink_rows[0:B, :], sink.rearrange("b q o -> b (q o)"))
         v_pool = [sb("v_pool%d" % h, [P, T], F32) for h in range(BLOCKS)]
         for h in range(BLOCKS):
             nc.sync.dma_start(v_pool[h][:], vT[h * P : (h + 1) * P, :])
 
-        ks_rows = k_scales[0].bitcast(I32)
-        for r in range(4):
-            nc.scalar.dma_start(ks_pool[r:P:32, :], ks_rows[r:16:4, :])
-
-        sink_raw = sb("sink_raw", [P, B], F32)
-        with nc.allow_non_contiguous_dma(reason="one logit a query row and sequence"):
-            nc.gpsimd.dma_start(sink_raw[:], sink.rearrange("b q o -> q (b o)"))
-        ident = sb("ident", [P, P], F32)
-        make_identity(nc, ident[:])
-        nc.gpsimd.dma_start(vs_pool[0:1, :], vs[0:1, :])
-
         warm = sb("warm", [P, 1], F32)
-        nc.scalar.activation(warm[:], ident[:, 0:1], ACT.Exp)
+        nc.scalar.activation(warm[64:P, :], sink_rows[64:P, 0:1], ACT.Exp)
 
         ks_got = sb("ks_got", [P, B * N], U8)
         nc.vector.tensor_copy(ks_got[:], ks_pool[:].bitcast(U8).indirect(offsets[:]))
@@ -79,7 +78,6 @@ def tile_attend_sink_kernel(tc, qT, k_words, k_scales, vT, vs, sink, offs, out):
         for b in range(B):
             q_bf = sb("q_bf%d" % b, [P, NQ, PACK], BF16)
             nc.scalar.copy(q_bf[:], q_raw[:, b].rearrange("p j q -> p q j"))
-            nc.vector.tensor_scalar(neg[b][:, N : N + 1], sink_raw[:, b : b + 1], -1.0, None, ALU.mult)
             nc.vector.quantize_mx(
                 out=q_codes[:, b, :].bitcast(FP8X4),
                 scales=q_scales[:, b, :],
@@ -89,7 +87,12 @@ def tile_attend_sink_kernel(tc, qT, k_words, k_scales, vT, vs, sink, offs, out):
         vs_got = sb("vs_got", [P, B * N], F32)
         nc.vector.tensor_copy(vs_got[:], vs_pool[:].indirect(offsets[:]))
 
-        kw_got = [sb("kw_got%d" % b, [P, N], U32) for b in range(B)]
+        sink_turned = bank(6, "sink_turned")
+        nc.tensor.transpose(sink_turned[:, 0:P], sink_rows[:], ident[:])
+        for b in range(B):
+            nc.scalar.activation(neg[b][:, N : N + 1], sink_turned[:, b : b + 1], ACT.Copy, scale=-1.0)
+
+        kw_got = [sb("kw_got%d" % b, [P, N], U32, "first%d" % b) for b in range(B)]
         scores = []
         for b in range(B):
             nc.vector.tensor_copy(kw_got[b][:], kw_pool[:].indirect(listed(b)))
@@ -112,7 +115,7 @@ def tile_attend_sink_kernel(tc, qT, k_words, k_scales, vT, vs, sink, offs, out):
                 nc.tensor.transpose(
                     turned[:, t * P : (t + 1) * P], vs_got[:, b * N + t : (b + 1) * N : PACK], ident[:]
                 )
-            col = sb("vs_col%d" % b, [P, PACK], F32)
+            col = sb("vs_col%d" % b, [P, PACK], F32, "second%d" % b)
             nc.scalar.copy(col[:], turned[:, 0 : PACK * P : P])
             vs_col.append(col)
 
@@ -138,7 +141,7 @@ def tile_attend_sink_kernel(tc, qT, k_words, k_scales, vT, vs, sink, offs, out):
             p_turned.append(turned)
 
         def gather_values(h, b, bank_index):
-            got = sb("v_got%d%d" % (h, b), [P, 2, P, 2], BF16)
+            got = sb("v_got%d%d" % (h, b), [P, 2, P, 2], BF16, ("first%d", "second%d")[h] % b)
             nc.vector.tensor_copy(got[:].rearrange("e u s i -> e s u i"), v_pool[h][:].indirect(listed(b)))
             words = got[:].rearrange("e u s i -> e (u s i)").bitcast(F32)
             turned = bank(bank_index, "v_turned%d%d" % (h, b))

@@ -43,54 +43,113 @@ def tile_attend_sink_kernel(tc, qT, k_words, k_scales, vT, vs, sink, offs, out):
         ks_pool = sb("ks_pool", [P, T // 4], I32)
         vs_pool = sb("vs_pool", [P, T], F32)
         sink_rows = sb("sink_rows", [P, NQ], F32)
-        nc.vector.memset(ks_pool[:], 0)
-        nc.vector.memset(vs_pool[:], 0.0)
-
+        zeros = sb("zeros", [P, NQ], F32, "keys")
         ident = sb("ident", [P, P], F32)
-        nc.gpsimd.memset(sink_rows[:], 0.0)
+        nc.vector.memset(ks_pool[:], 0)
+        seed = sb("seed", [P, 1], F32)
+        nc.vector.memset(seed[:], 0.0)
+        nc.vector.memset(zeros[:], 0.0)
+        nc.vector.memset(vs_pool[:], 0.0)
+        nc.vector.tensor_copy(sink_rows[:], zeros[:])
         make_identity(nc, ident[:])
 
-        q_raw = sb("q_raw", [P, B, PACK, NQ], F32)
+        v_pool = [sb("v_pool0", [P, T], F32, "late")]
+        pieces = [
+            [slice(0, 512), slice(512, 1280), slice(1280, T)],
+            [slice(0, T // 2), slice(T // 2, T)],
+        ]
+        nc.sync.dma_start(v_pool[0][:, pieces[0][0]], vT[0:P, pieces[0][0]])
+        ks_rows = k_scales[0].bitcast(I32)
+        for r in range(4):
+            queue = nc.sync if r < 2 else nc.scalar
+            queue.dma_start(ks_pool[r:P:32, :], ks_rows[r:16:4, :])
+        for cols in pieces[0][1:]:
+            nc.sync.dma_start(v_pool[0][:, cols], vT[0:P, cols])
+        warm = sb("warm", [P, 1], F32)
+        nc.scalar.activation(warm[:], seed[:], ACT.Exp)
+        q_raw = sb("q_raw", [P, B, PACK, NQ], F32, "first0")
         nc.sync.dma_start(
             q_raw[:].rearrange("p b j q -> p b (j q)"),
             qT.rearrange("b (p j) q -> p b (j q)", j=PACK),
         )
-        ks_rows = k_scales[0].bitcast(I32)
-        for r in range(4):
-            nc.sync.dma_start(ks_pool[r:P:32, :], ks_rows[r:16:4, :])
         nc.sync.dma_start(vs_pool[0:1, :], vs[0:1, :])
-        kw_pool = sb("kw_pool", [P, T], U32)
+        kw_pool = sb("kw_pool", [P, T], U32, "keys")
         nc.sync.dma_start(kw_pool[:].bitcast(I32), k_words[0].rearrange("p n r -> p (n r)").bitcast(I32))
         nc.sync.dma_start(sink_rows[0:B, :], sink.rearrange("b q o -> b (q o)"))
-        v_pool = [sb("v_pool%d" % h, [P, T], F32) for h in range(BLOCKS)]
-        for h in range(BLOCKS):
-            nc.sync.dma_start(v_pool[h][:], vT[h * P : (h + 1) * P, :])
 
-        warm = sb("warm", [P, 1], F32)
-        nc.scalar.activation(warm[64:P, :], sink_rows[64:P, 0:1], ACT.Exp)
+        v_pool_bf = [sb("v_pool_bf%d" % h, [P, T], BF16) for h in range(BLOCKS)]
+
+        def round_pool(h):
+            for cols in pieces[h]:
+                nc.scalar.activation(v_pool_bf[h][:, cols], v_pool[h][:, cols], ACT.Copy)
+
+        def gather_values(h, b, bank_index, on_vector, tag=None):
+            got = sb("v_got%d%d" % (h, b), [P, 2, P, 2], BF16, tag)
+            stepped = got[:].rearrange("e u s i -> e s u i")
+            if on_vector:
+                nc.vector.tensor_copy(stepped, v_pool[h][:].indirect(listed(b)))
+            else:
+                nc.scalar.activation(stepped, v_pool_bf[h][:].indirect(listed(b)), ACT.Copy)
+            words = got[:].rearrange("e u s i -> e (u s i)").bitcast(F32)
+            turned = bank(bank_index, "v_turned%d%d" % (h, b))
+            for u in range(2):
+                nc.tensor.transpose(turned[:, u * P : (u + 1) * P], words[:, u * P : (u + 1) * P], ident[:])
+            return turned
+
+        def interleave_values(h, b, turned):
+            v_bf = sb("v_bf%d%d" % (h, b), [P, P * PACK], BF16)
+            nc.scalar.copy(
+                v_bf[:].bitcast(F32).rearrange("s (e u) -> s e u", u=2),
+                turned[:, 0 : 2 * P].rearrange("s (u e) -> s e u", u=2),
+            )
+            return v_bf
+
+        def quantize(name, values, tag=None):
+            codes = sb(name + "_codes", [P, P], U32, tag)
+            scales = sb(name + "_scales", [P, P], U8)
+            nc.vector.quantize_mx(out=codes[:].bitcast(FP8X4), scales=scales[:], in_=values[:])
+            return codes, scales
 
         ks_got = sb("ks_got", [P, B * N], U8)
         nc.vector.tensor_copy(ks_got[:], ks_pool[:].bitcast(U8).indirect(offsets[:]))
+        q_bf = sb("q_bf", [P, B, NQ, PACK], BF16)
+        nc.vector.tensor_copy(q_bf[:], q_raw[:].rearrange("p b j q -> p b q j"))
+        vs_got = sb("vs_got", [P, B, PACK, P], F32)
+        nc.vector.tensor_copy(
+            vs_got[:].bitcast(U32).rearrange("p b t s -> p b s t"), vs_pool[:].bitcast(U32).indirect(offsets[:])
+        )
 
-        q_codes = sb("q_codes", [P, B, NQ], U32)
-        q_scales = sb("q_scales", [P, B, NQ], U8)
-        neg = [sb("neg%d" % b, [P, N + 1], F32) for b in range(B)]
+        round_pool(0)
+        v_pool.append(sb("v_pool1", [P, T], F32, "late"))
+        for cols in pieces[1]:
+            nc.sync.dma_start(v_pool[1][:, cols], vT[P : 2 * P, cols])
+        v_bf = {}
+        turned00 = gather_values(0, 0, 6, False)
+        turned01 = gather_values(0, 1, 7, False)
+        v_bf[0, 0] = interleave_values(0, 0, turned00)
+        v_bf[0, 1] = interleave_values(0, 1, turned01)
+
+        q_codes = sb("q_codes", [P, B * NQ], U32)
+        q_scales = sb("q_scales", [P, B * NQ], U8)
+        nc.vector.quantize_mx(
+            out=q_codes[:].bitcast(FP8X4), scales=q_scales[:], in_=q_bf[:].rearrange("p b q j -> p (b q j)")
+        )
+
+        vs_col = []
         for b in range(B):
-            q_bf = sb("q_bf%d" % b, [P, NQ, PACK], BF16)
-            nc.scalar.copy(q_bf[:], q_raw[:, b].rearrange("p j q -> p q j"))
-            nc.vector.quantize_mx(
-                out=q_codes[:, b, :].bitcast(FP8X4),
-                scales=q_scales[:, b, :],
-                in_=q_bf[:].rearrange("p q j -> p (q j)"),
-            )
+            turned = bank(2 + b, "vs_turned%d" % b)
+            for t in range(PACK):
+                nc.tensor.transpose(turned[:, t * P : (t + 1) * P], vs_got[:, b, t, :], ident[:])
+            col = sb("vs_col%d" % b, [P, PACK], F32, "fourth%d" % b)
+            nc.scalar.copy(col[:], turned[:, 0 : PACK * P : P])
+            vs_col.append(col)
 
-        vs_got = sb("vs_got", [P, B * N], F32)
-        nc.vector.tensor_copy(vs_got[:], vs_pool[:].indirect(offsets[:]))
-
-        sink_turned = bank(6, "sink_turned")
+        neg = sb("neg", [P, B, N + 16], F32, "second")
+        sink_turned = bank(4, "sink_turned")
         nc.tensor.transpose(sink_turned[:, 0:P], sink_rows[:], ident[:])
-        for b in range(B):
-            nc.scalar.activation(neg[b][:, N : N + 1], sink_turned[:, b : b + 1], ACT.Copy, scale=-1.0)
+        neg_sink = sb("neg_sink", [P, B], F32, "third")
+        nc.scalar.activation(neg_sink[:], sink_turned[:, 0:B], ACT.Copy, scale=-1.0)
+        nc.scalar.activation(neg[:, :, N], sink_turned[:, 0:B], ACT.Copy, scale=-1.0)
 
         kw_got = [sb("kw_got%d" % b, [P, N], U32, "first%d" % b) for b in range(B)]
         scores = []
@@ -99,8 +158,8 @@ def tile_attend_sink_kernel(tc, qT, k_words, k_scales, vT, vs, sink, offs, out):
             acc = bank(b, "scores%d" % b)
             nc.tensor.matmul_mx(
                 out=acc[:],
-                lhsT=q_codes[:, b, :].bitcast(FP8X4),
-                lhsT_scale=q_scales[:, b, :],
+                lhsT=q_codes[:, b * NQ : (b + 1) * NQ].bitcast(FP8X4),
+                lhsT_scale=q_scales[:, b * NQ : (b + 1) * NQ],
                 rhs=kw_got[b][:].bitcast(FP8X4),
                 rhs_scale=ks_got[:, b * N : (b + 1) * N],
                 start=True,
@@ -108,57 +167,29 @@ def tile_attend_sink_kernel(tc, qT, k_words, k_scales, vT, vs, sink, offs, out):
             )
             scores.append(acc)
 
-        vs_col = []
-        for b in range(B):
-            turned = bank(2 + b, "vs_turned%d" % b)
-            for t in range(PACK):
-                nc.tensor.transpose(
-                    turned[:, t * P : (t + 1) * P], vs_got[:, b * N + t : (b + 1) * N : PACK], ident[:]
-                )
-            col = sb("vs_col%d" % b, [P, PACK], F32, "second%d" % b)
-            nc.scalar.copy(col[:], turned[:, 0 : PACK * P : P])
-            vs_col.append(col)
+        round_pool(1)
 
-        probs, totals, p_turned = [], [], []
+        totals, p_turned, maxes = [], [], []
         for b in range(B):
             neg_max = sb("neg_max%d" % b, [P, 1], F32)
             nc.vector.tensor_scalar(
-                neg[b][:, 0:N].rearrange("p (t s) -> p t s", t=PACK),
+                neg[:, b, 0:N].rearrange("p (t s) -> p t s", t=PACK),
                 scores[b][:].rearrange("p (s t) -> p t s", t=PACK),
                 -1.0,
-                neg[b][:, N : N + 1],
+                neg_sink[:, b : b + 1],
                 ALU.mult,
                 ALU.min,
                 accum_out=neg_max[:],
             )
             p = sb("p%d" % b, [P, N + 1], F32)
             total = sb("total%d" % b, [P, 1], F32)
-            nc.scalar.activation(p[:], neg[b][:], ACT.Exp, bias=neg_max[:], scale=-1.0, accum_out=total[:])
+            nc.scalar.activation(p[:], neg[:, b, 0 : N + 1], ACT.Exp, bias=neg_max[:], scale=-1.0, accum_out=total[:])
             turned = bank(4 + b, "p_turned%d" % b)
             for t in range(PACK):
                 nc.tensor.transpose(turned[:, t * P : (t + 1) * P], p[:, t * P : (t + 1) * P], ident[:])
             totals.append(total)
+            maxes.append(neg_max)
             p_turned.append(turned)
-
-        def gather_values(h, b, bank_index):
-            got = sb("v_got%d%d" % (h, b), [P, 2, P, 2], BF16, ("first%d", "second%d")[h] % b)
-            nc.vector.tensor_copy(got[:].rearrange("e u s i -> e s u i"), v_pool[h][:].indirect(listed(b)))
-            words = got[:].rearrange("e u s i -> e (u s i)").bitcast(F32)
-            turned = bank(bank_index, "v_turned%d%d" % (h, b))
-            for u in range(2):
-                nc.tensor.transpose(turned[:, u * P : (u + 1) * P], words[:, u * P : (u + 1) * P], ident[:])
-            v_bf = sb("v_bf%d%d" % (h, b), [P, P * PACK], BF16)
-            nc.scalar.copy(
-                v_bf[:].bitcast(F32).rearrange("s (e u) -> s e u", u=2),
-                turned[:, 0 : 2 * P].rearrange("s (u e) -> s e u", u=2),
-            )
-            return v_bf
-
-        def quantize(name, values):
-            codes = sb(name + "_codes", [P, P], U32)
-            scales = sb(name + "_scales", [P, P], U8)
-            nc.vector.quantize_mx(out=codes[:].bitcast(FP8X4), scales=scales[:], in_=values[:])
-            return codes, scales
 
         def weigh(b):
             w_bf = sb("w_bf%d" % b, [P, NQ * PACK], BF16)
@@ -188,25 +219,23 @@ def tile_attend_sink_kernel(tc, qT, k_words, k_scales, vT, vs, sink, offs, out):
                 nc.scalar.activation(y[:], acc[:, 0:P], ACT.Copy, scale=inverse[:])
             nc.sync.dma_start(out[b, :, h * P : (h + 1) * P], y[:])
 
-        v_bf = {}
-        v_bf[0, 0] = gather_values(0, 0, 6)
-        w_bf0 = weigh(0)
-        v_bf[0, 1] = gather_values(0, 1, 7)
-        w_bf1 = weigh(1)
+        v00 = quantize("v00", v_bf[0, 0], "first0")
+        v01 = quantize("v01", v_bf[0, 1], "first1")
+        turned11 = gather_values(1, 1, 3, True, "third")
         inverse = []
         for b in range(B):
             inv = sb("inverse%d" % b, [P, 1], F32)
             nc.vector.reciprocal(inv[:], totals[b][:])
             inverse.append(inv)
-        w = [quantize("w0", w_bf0)]
-        v00 = quantize("v00", v_bf[0, 0])
-        w.append(quantize("w1", w_bf1))
-        v01 = quantize("v01", v_bf[0, 1])
-        v_bf[1, 0] = gather_values(1, 0, 2)
-        v_bf[1, 1] = gather_values(1, 1, 3)
+        w_bf0 = weigh(0)
+        w_bf1 = weigh(1)
+        turned10 = gather_values(1, 0, 2, False, "second")
+        w = [quantize("w0", w_bf0), quantize("w1", w_bf1)]
+        v_bf[1, 1] = interleave_values(1, 1, turned11)
+        v_bf[1, 0] = interleave_values(1, 0, turned10)
+        v11 = quantize("v11", v_bf[1, 1], "fourth1")
+        v10 = quantize("v10", v_bf[1, 0], "fourth0")
         finish(0, 0, w[0], v00, inverse[0], 0, False)
         finish(0, 1, w[1], v01, inverse[1], 1, False)
-        v10 = quantize("v10", v_bf[1, 0])
-        v11 = quantize("v11", v_bf[1, 1])
-        finish(1, 0, w[0], v10, inverse[0], 4, False)
-        finish(1, 1, w[1], v11, inverse[1], 5, True)
+        finish(1, 1, w[1], v11, inverse[1], 6, False)
+        finish(1, 0, w[0], v10, inverse[0], 7, True)

@@ -41,7 +41,7 @@ def tile_attend_sink_kernel(tc, qT, k_words, k_scales, vT, vs, sink, offs, out):
             return offsets[:, b * LIST_COLS : (b + 1) * LIST_COLS]
 
         ks_pool = sb("ks_pool", [P, T // 4], I32)
-        vs_pool = sb("vs_pool", [P, T], F32)
+        vs_pool = sb("vs_pool", [P, T], F32, "second")
         sink_rows = sb("sink_rows", [P, NQ], F32)
         zeros = sb("zeros", [P, NQ], F32, "keys")
         ident = sb("ident", [P, P], F32)
@@ -54,34 +54,27 @@ def tile_attend_sink_kernel(tc, qT, k_words, k_scales, vT, vs, sink, offs, out):
         make_identity(nc, ident[:])
 
         v_pool = [sb("v_pool0", [P, T], F32, "late")]
-        pieces = [
-            [slice(0, 512), slice(512, 1280), slice(1280, T)],
-            [slice(0, T // 2), slice(T // 2, T)],
-        ]
-        nc.sync.dma_start(v_pool[0][:, pieces[0][0]], vT[0:P, pieces[0][0]])
+        pieces = [slice(0, 512), slice(512, 1280), slice(1280, T)]
+        nc.sync.dma_start(v_pool[0][:, pieces[0]], vT[0:P, pieces[0]])
         ks_rows = k_scales[0].bitcast(I32)
         for r in range(4):
             queue = nc.sync if r < 2 else nc.scalar
             queue.dma_start(ks_pool[r:P:32, :], ks_rows[r:16:4, :])
-        for cols in pieces[0][1:]:
+        for cols in pieces[1:]:
             nc.sync.dma_start(v_pool[0][:, cols], vT[0:P, cols])
         warm = sb("warm", [P, 1], F32)
         nc.scalar.activation(warm[:], seed[:], ACT.Exp)
-        q_raw = sb("q_raw", [P, B, PACK, NQ], F32, "first0")
+        q_raw = sb("q_raw", [P, B, PACK, NQ], F32)
         nc.sync.dma_start(
             q_raw[:].rearrange("p b j q -> p b (j q)"),
             qT.rearrange("b (p j) q -> p b (j q)", j=PACK),
         )
         nc.sync.dma_start(vs_pool[0:1, :], vs[0:1, :])
+        nc.sync.dma_start(sink_rows[0:B, :], sink.rearrange("b q o -> b (q o)"))
         kw_pool = sb("kw_pool", [P, T], U32, "keys")
         nc.sync.dma_start(kw_pool[:].bitcast(I32), k_words[0].rearrange("p n r -> p (n r)").bitcast(I32))
-        nc.sync.dma_start(sink_rows[0:B, :], sink.rearrange("b q o -> b (q o)"))
 
-        v_pool_bf = [sb("v_pool_bf%d" % h, [P, T], BF16) for h in range(BLOCKS)]
-
-        def round_pool(h):
-            for cols in pieces[h]:
-                nc.scalar.activation(v_pool_bf[h][:, cols], v_pool[h][:, cols], ACT.Copy)
+        v_pool_bf = sb("v_pool_bf", [P, T], BF16)
 
         def gather_values(h, b, bank_index, on_vector, tag=None):
             got = sb("v_got%d%d" % (h, b), [P, 2, P, 2], BF16, tag)
@@ -89,47 +82,55 @@ def tile_attend_sink_kernel(tc, qT, k_words, k_scales, vT, vs, sink, offs, out):
             if on_vector:
                 nc.vector.tensor_copy(stepped, v_pool[h][:].indirect(listed(b)))
             else:
-                nc.scalar.activation(stepped, v_pool_bf[h][:].indirect(listed(b)), ACT.Copy)
+                nc.scalar.activation(stepped, v_pool_bf[:].indirect(listed(b)), ACT.Copy)
             words = got[:].rearrange("e u s i -> e (u s i)").bitcast(F32)
             turned = bank(bank_index, "v_turned%d%d" % (h, b))
             for u in range(2):
                 nc.tensor.transpose(turned[:, u * P : (u + 1) * P], words[:, u * P : (u + 1) * P], ident[:])
             return turned
 
+        v_bf = [sb("v_bf%d" % h, [P, B * N], BF16) for h in range(BLOCKS)]
+
         def interleave_values(h, b, turned):
-            v_bf = sb("v_bf%d%d" % (h, b), [P, P * PACK], BF16)
             nc.scalar.copy(
-                v_bf[:].bitcast(F32).rearrange("s (e u) -> s e u", u=2),
+                v_bf[h][:, b * N : (b + 1) * N].bitcast(F32).rearrange("s (e u) -> s e u", u=2),
                 turned[:, 0 : 2 * P].rearrange("s (u e) -> s e u", u=2),
             )
-            return v_bf
 
         def quantize(name, values, tag=None):
-            codes = sb(name + "_codes", [P, P], U32, tag)
-            scales = sb(name + "_scales", [P, P], U8)
+            width = values.shape[1] // PACK
+            codes = sb(name + "_codes", [P, width], U32, tag)
+            scales = sb(name + "_scales", [P, width], U8)
             nc.vector.quantize_mx(out=codes[:].bitcast(FP8X4), scales=scales[:], in_=values[:])
             return codes, scales
 
         ks_got = sb("ks_got", [P, B * N], U8)
         nc.vector.tensor_copy(ks_got[:], ks_pool[:].bitcast(U8).indirect(offsets[:]))
-        q_bf = sb("q_bf", [P, B, NQ, PACK], BF16)
-        nc.vector.tensor_copy(q_bf[:], q_raw[:].rearrange("p b j q -> p b q j"))
         vs_got = sb("vs_got", [P, B, PACK, P], F32)
         nc.vector.tensor_copy(
             vs_got[:].bitcast(U32).rearrange("p b t s -> p b s t"), vs_pool[:].bitcast(U32).indirect(offsets[:])
         )
 
-        round_pool(0)
+        for cols in pieces:
+            nc.scalar.activation(v_pool_bf[:, cols], v_pool[0][:, cols], ACT.Copy)
         v_pool.append(sb("v_pool1", [P, T], F32, "late"))
-        for cols in pieces[1]:
-            nc.sync.dma_start(v_pool[1][:, cols], vT[P : 2 * P, cols])
-        v_bf = {}
+        nc.sync.dma_start(v_pool[1][:], vT[P : 2 * P, :])
+        q_bf = sb("q_bf", [P, B, NQ, PACK], BF16, "first1")
+        nc.scalar.copy(q_bf[:], q_raw[:].rearrange("p b j q -> p b q j"))
+
+        neg = sb("neg", [P, B, N + 16], F32)
+        sink_turned = bank(4, "sink_turned")
+        nc.tensor.transpose(sink_turned[:, 0:P], sink_rows[:], ident[:])
+        neg_sink = sb("neg_sink", [P, B], F32, "third")
+        nc.scalar.activation(neg_sink[:], sink_turned[:, 0:B], ACT.Copy, scale=-1.0)
+        nc.scalar.activation(neg[:, :, N], sink_turned[:, 0:B], ACT.Copy, scale=-1.0)
+
         turned00 = gather_values(0, 0, 6, False)
         turned01 = gather_values(0, 1, 7, False)
-        v_bf[0, 0] = interleave_values(0, 0, turned00)
-        v_bf[0, 1] = interleave_values(0, 1, turned01)
+        interleave_values(0, 0, turned00)
+        interleave_values(0, 1, turned01)
 
-        q_codes = sb("q_codes", [P, B * NQ], U32)
+        q_codes = sb("q_codes", [P, B * NQ], U32, "second")
         q_scales = sb("q_scales", [P, B * NQ], U8)
         nc.vector.quantize_mx(
             out=q_codes[:].bitcast(FP8X4), scales=q_scales[:], in_=q_bf[:].rearrange("p b q j -> p (b q j)")
@@ -140,16 +141,9 @@ def tile_attend_sink_kernel(tc, qT, k_words, k_scales, vT, vs, sink, offs, out):
             turned = bank(2 + b, "vs_turned%d" % b)
             for t in range(PACK):
                 nc.tensor.transpose(turned[:, t * P : (t + 1) * P], vs_got[:, b, t, :], ident[:])
-            col = sb("vs_col%d" % b, [P, PACK], F32, "fourth%d" % b)
+            col = sb("vs_col%d" % b, [P, PACK], F32, "fourth" if b == 1 else None)
             nc.scalar.copy(col[:], turned[:, 0 : PACK * P : P])
             vs_col.append(col)
-
-        neg = sb("neg", [P, B, N + 16], F32, "second")
-        sink_turned = bank(4, "sink_turned")
-        nc.tensor.transpose(sink_turned[:, 0:P], sink_rows[:], ident[:])
-        neg_sink = sb("neg_sink", [P, B], F32, "third")
-        nc.scalar.activation(neg_sink[:], sink_turned[:, 0:B], ACT.Copy, scale=-1.0)
-        nc.scalar.activation(neg[:, :, N], sink_turned[:, 0:B], ACT.Copy, scale=-1.0)
 
         kw_got = [sb("kw_got%d" % b, [P, N], U32, "first%d" % b) for b in range(B)]
         scores = []
@@ -166,8 +160,6 @@ def tile_attend_sink_kernel(tc, qT, k_words, k_scales, vT, vs, sink, offs, out):
                 stop=True,
             )
             scores.append(acc)
-
-        round_pool(1)
 
         totals, p_turned, maxes = [], [], []
         for b in range(B):
@@ -201,27 +193,31 @@ def tile_attend_sink_kernel(tc, qT, k_words, k_scales, vT, vs, sink, offs, out):
             )
             return w_bf
 
-        def finish(h, b, w, v, inverse, bank_index, on_vector):
-            acc = bank(bank_index, "y%d%d" % (h, b))
-            nc.tensor.matmul_mx(
-                out=acc[:, 0:P],
-                lhsT=w[0][:].bitcast(FP8X4),
-                lhsT_scale=w[1][:],
-                rhs=v[0][:].bitcast(FP8X4),
-                rhs_scale=v[1][:],
-                start=True,
-                stop=True,
-            )
-            y = sb("y_out%d%d" % (h, b), [P, P], F32)
-            if on_vector:
-                nc.vector.tensor_scalar(y[:], acc[:, 0:P], inverse[:], None, ALU.mult)
+        def finish(b, w, inverse):
+            acc = bank(b, "y%d" % b)
+            cols = slice(b * P, (b + 1) * P)
+            for h in range(BLOCKS):
+                nc.tensor.matmul_mx(
+                    out=acc[:, h * P : (h + 1) * P],
+                    lhsT=w[0][:].bitcast(FP8X4),
+                    lhsT_scale=w[1][:],
+                    rhs=v[h][0][:, cols].bitcast(FP8X4),
+                    rhs_scale=v[h][1][:, cols],
+                    start=True,
+                    stop=True,
+                )
+            y = sb("y_out%d" % b, [P, DV], F32)
+            if b == 1:
+                nc.vector.tensor_scalar(y[:], acc[:, 0:DV], inverse[:], None, ALU.mult)
             else:
-                nc.scalar.activation(y[:], acc[:, 0:P], ACT.Copy, scale=inverse[:])
-            nc.sync.dma_start(out[b, :, h * P : (h + 1) * P], y[:])
+                nc.scalar.activation(y[:], acc[:, 0:DV], ACT.Copy, scale=inverse[:])
+            nc.sync.dma_start(out[b], y[:])
 
-        v00 = quantize("v00", v_bf[0, 0], "first0")
-        v01 = quantize("v01", v_bf[0, 1], "first1")
-        turned11 = gather_values(1, 1, 3, True, "third")
+        v = [quantize("v0", v_bf[0], "first0")]
+        turned10 = gather_values(1, 0, 2, True, "third")
+        turned11 = gather_values(1, 1, 3, True, "first1")
+        interleave_values(1, 0, turned10)
+        interleave_values(1, 1, turned11)
         inverse = []
         for b in range(B):
             inv = sb("inverse%d" % b, [P, 1], F32)
@@ -229,13 +225,8 @@ def tile_attend_sink_kernel(tc, qT, k_words, k_scales, vT, vs, sink, offs, out):
             inverse.append(inv)
         w_bf0 = weigh(0)
         w_bf1 = weigh(1)
-        turned10 = gather_values(1, 0, 2, False, "second")
-        w = [quantize("w0", w_bf0), quantize("w1", w_bf1)]
-        v_bf[1, 1] = interleave_values(1, 1, turned11)
-        v_bf[1, 0] = interleave_values(1, 0, turned10)
-        v11 = quantize("v11", v_bf[1, 1], "fourth1")
-        v10 = quantize("v10", v_bf[1, 0], "fourth0")
-        finish(0, 0, w[0], v00, inverse[0], 0, False)
-        finish(0, 1, w[1], v01, inverse[1], 1, False)
-        finish(1, 1, w[1], v11, inverse[1], 6, False)
-        finish(1, 0, w[0], v10, inverse[0], 7, True)
+        w0 = quantize("w0", w_bf0)
+        v.append(quantize("v1", v_bf[1], "fourth"))
+        w1 = quantize("w1", w_bf1)
+        finish(0, w0, inverse[0])
+        finish(1, w1, inverse[1])

@@ -19,13 +19,16 @@ ACT = mybir.ActivationFunctionType
 P = 128
 PACK = 4
 LIST_COLS = N // 16
-BLOCKS = DV // P
+GROUPS = 16
+RUN = 16
+FIRST = 512
 
 
 def tile_attend_sink_kernel(tc, qT, k_words, k_scales, vT, vs, sink, offs, out):
     nc = tc.nc
     with ExitStack() as ctx:
         held = ctx.enter_context(tc.tile_pool(name="held", bufs=1))
+        shared = ctx.enter_context(tc.tile_pool(name="shared", bufs=1))
         psum = ctx.enter_context(tc.psum_pool(name="psum", bufs=1))
 
         def sb(name, shape, dtype, tag=None):
@@ -41,59 +44,77 @@ def tile_attend_sink_kernel(tc, qT, k_words, k_scales, vT, vs, sink, offs, out):
             return offsets[:, b * LIST_COLS : (b + 1) * LIST_COLS]
 
         ks_pool = sb("ks_pool", [P, T // 4], I32)
-        vs_pool = sb("vs_pool", [P, T], F32, "second")
-        sink_rows = sb("sink_rows", [P, NQ], F32)
-        zeros = sb("zeros", [P, NQ], F32, "keys")
-        ident = sb("ident", [P, P], F32)
-        nc.vector.memset(ks_pool[:], 0)
+        vs_pool = sb("vs_pool", [P, T], F32, "scale_pool")
+        nc.vector.memset(ks_pool[:, 0 : T // 8], 0)
+        nc.gpsimd.memset(ks_pool[:, T // 8 : T // 4], 0)
         seed = sb("seed", [P, 1], F32)
         nc.vector.memset(seed[:], 0.0)
-        nc.vector.memset(zeros[:], 0.0)
-        nc.vector.memset(vs_pool[:], 0.0)
-        nc.vector.tensor_copy(sink_rows[:], zeros[:])
+        nc.vector.memset(vs_pool[:, 0 : T // 2], 0.0)
+        nc.gpsimd.memset(vs_pool[:, T // 2 : T], 0.0)
+        ident = sb("ident", [P, P], F32)
         make_identity(nc, ident[:])
 
-        v_pool = [sb("v_pool0", [P, T], F32, "late")]
-        pieces = [slice(0, 512), slice(512, 1280), slice(1280, T)]
-        nc.sync.dma_start(v_pool[0][:, pieces[0]], vT[0:P, pieces[0]])
+        v_pool0 = sb("v_pool0", [P, T], F32)
+        pieces = [slice(0, FIRST), slice(FIRST, (FIRST + T) // 2), slice((FIRST + T) // 2, T)]
+        nc.sync.dma_start(v_pool0[:, pieces[0]], vT[0:P, pieces[0]])
         ks_rows = k_scales[0].bitcast(I32)
         for r in range(4):
             queue = nc.sync if r < 2 else nc.scalar
             queue.dma_start(ks_pool[r:P:32, :], ks_rows[r:16:4, :])
         for cols in pieces[1:]:
-            nc.sync.dma_start(v_pool[0][:, cols], vT[0:P, cols])
+            nc.sync.dma_start(v_pool0[:, cols], vT[0:P, cols])
         warm = sb("warm", [P, 1], F32)
         nc.scalar.activation(warm[:], seed[:], ACT.Exp)
-        q_raw = sb("q_raw", [P, B, PACK, NQ], F32)
+        nc.sync.dma_start(vs_pool[0:1, :], vs[0:1, :])
+        q_raw = shared.tile([P, B, PACK, NQ], F32, name="q_raw", offset=0, align_bytes=64)
         nc.sync.dma_start(
             q_raw[:].rearrange("p b j q -> p b (j q)"),
             qT.rearrange("b (p j) q -> p b (j q)", j=PACK),
         )
-        nc.sync.dma_start(vs_pool[0:1, :], vs[0:1, :])
-        nc.sync.dma_start(sink_rows[0:B, :], sink.rearrange("b q o -> b (q o)"))
-        kw_pool = sb("kw_pool", [P, T], U32, "keys")
+        sink_cols = sb("sink_cols", [P, B], F32)
+        with nc.allow_non_contiguous_dma(reason="one logit a partition"):
+            nc.sync.dma_start(sink_cols[:], sink.rearrange("b q o -> q (b o)"))
+        kw_pool = sb("kw_pool", [P, T], U32)
         nc.sync.dma_start(kw_pool[:].bitcast(I32), k_words[0].rearrange("p n r -> p (n r)").bitcast(I32))
+        v_pool1 = sb("v_pool1", [P, T], F32, "last_pool")
+        nc.sync.dma_start(v_pool1[:], vT[P : 2 * P, :])
 
-        v_pool_bf = sb("v_pool_bf", [P, T], BF16)
+        ks_got = sb("ks_got", [P, B * N], U8)
+        nc.vector.tensor_copy(ks_got[:], ks_pool[:].bitcast(U8).indirect(offsets[:]))
+        vs_got = sb("vs_got", [P, 2, B * GROUPS, RUN], F32)
+        nc.vector.tensor_copy(
+            vs_got[:].bitcast(U32).rearrange("p u g x -> p g u x"), vs_pool[:].bitcast(U32).indirect(offsets[:])
+        )
 
-        def gather_values(h, b, bank_index, on_vector, tag=None):
-            got = sb("v_got%d%d" % (h, b), [P, 2, P, 2], BF16, tag)
-            stepped = got[:].rearrange("e u s i -> e s u i")
-            if on_vector:
-                nc.vector.tensor_copy(stepped, v_pool[h][:].indirect(listed(b)))
+        v_pool_bf = sb("v_pool_bf", [P, T], BF16, "first_pool")
+        for cols in pieces:
+            nc.scalar.activation(v_pool_bf[:, cols], v_pool0[:, cols], ACT.Copy)
+        neg = sb("neg", [P, B, N + 16], F32)
+        nc.scalar.activation(neg[:, :, N], sink_cols[:], ACT.Copy, scale=-1.0)
+        q_bf = sb("q_bf", [P, B, NQ, PACK], BF16)
+        nc.scalar.copy(q_bf[:], q_raw[:].rearrange("p b j q -> p b q j"))
+
+        def gather_values(h, b, bank_index):
+            if h == 0:
+                got = shared.tile([P, 2, GROUPS, RUN], BF16, name="v_got0%d" % b, offset=2 * N * b, align_bytes=64)
             else:
-                nc.scalar.activation(stepped, v_pool_bf[:].indirect(listed(b)), ACT.Copy)
-            words = got[:].rearrange("e u s i -> e (u s i)").bitcast(F32)
+                got = sb("v_got1%d" % b, [P, 2, GROUPS, RUN], BF16)
+            dealt = got[:].rearrange("e u g x -> e g u x")
+            if h == 1:
+                nc.vector.tensor_copy(dealt, v_pool1[:].indirect(listed(b)))
+            else:
+                nc.scalar.activation(dealt, v_pool_bf[:].indirect(listed(b)), ACT.Copy)
+            words = got[:].rearrange("e u g x -> e (u g x)").bitcast(F32)
             turned = bank(bank_index, "v_turned%d%d" % (h, b))
             for u in range(2):
                 nc.tensor.transpose(turned[:, u * P : (u + 1) * P], words[:, u * P : (u + 1) * P], ident[:])
             return turned
 
-        v_bf = [sb("v_bf%d" % h, [P, B * N], BF16) for h in range(BLOCKS)]
+        v_bf = [sb("v_bf%d" % b, [P, DV * PACK], BF16) for b in range(B)]
 
         def interleave_values(h, b, turned):
             nc.scalar.copy(
-                v_bf[h][:, b * N : (b + 1) * N].bitcast(F32).rearrange("s (e u) -> s e u", u=2),
+                v_bf[b][:, h * N : (h + 1) * N].bitcast(F32).rearrange("s (e u) -> s e u", u=2),
                 turned[:, 0 : 2 * P].rearrange("s (u e) -> s e u", u=2),
             )
 
@@ -101,132 +122,108 @@ def tile_attend_sink_kernel(tc, qT, k_words, k_scales, vT, vs, sink, offs, out):
             width = values.shape[1] // PACK
             codes = sb(name + "_codes", [P, width], U32, tag)
             scales = sb(name + "_scales", [P, width], U8)
-            nc.vector.quantize_mx(out=codes[:].bitcast(FP8X4), scales=scales[:], in_=values[:])
+            nc.vector.quantize_mx(out=codes[:].bitcast(FP8X4), scales=scales[:], in_=values)
             return codes, scales
 
-        ks_got = sb("ks_got", [P, B * N], U8)
-        nc.vector.tensor_copy(ks_got[:], ks_pool[:].bitcast(U8).indirect(offsets[:]))
-        vs_got = sb("vs_got", [P, B, PACK, P], F32)
-        nc.vector.tensor_copy(
-            vs_got[:].bitcast(U32).rearrange("p b t s -> p b s t"), vs_pool[:].bitcast(U32).indirect(offsets[:])
-        )
+        vs_turned = bank(2, "vs_turned")
+        for b in range(B):
+            for u in range(2):
+                for j in range(2):
+                    col = PACK * b + 2 * u + j
+                    nc.tensor.transpose(
+                        vs_turned[:, col : col + P],
+                        vs_got[:].rearrange("p u g x -> p u (g x)")[:, u, 2 * P * b + j : 2 * P * (b + 1) : 2],
+                        ident[:],
+                    )
 
-        for cols in pieces:
-            nc.scalar.activation(v_pool_bf[:, cols], v_pool[0][:, cols], ACT.Copy)
-        v_pool.append(sb("v_pool1", [P, T], F32, "late"))
-        nc.sync.dma_start(v_pool[1][:], vT[P : 2 * P, :])
-        q_bf = sb("q_bf", [P, B, NQ, PACK], BF16, "first1")
-        nc.scalar.copy(q_bf[:], q_raw[:].rearrange("p b j q -> p b q j"))
-
-        neg = sb("neg", [P, B, N + 16], F32)
-        sink_turned = bank(4, "sink_turned")
-        nc.tensor.transpose(sink_turned[:, 0:P], sink_rows[:], ident[:])
-        neg_sink = sb("neg_sink", [P, B], F32, "third")
-        nc.scalar.activation(neg_sink[:], sink_turned[:, 0:B], ACT.Copy, scale=-1.0)
-        nc.scalar.activation(neg[:, :, N], sink_turned[:, 0:B], ACT.Copy, scale=-1.0)
-
-        turned00 = gather_values(0, 0, 6, False)
-        turned01 = gather_values(0, 1, 7, False)
+        turned00 = gather_values(0, 0, 6)
+        turned01 = gather_values(0, 1, 7)
         interleave_values(0, 0, turned00)
         interleave_values(0, 1, turned01)
+        vs_col = sb("vs_col", [P, B * PACK], F32, "first_pool")
+        nc.scalar.copy(vs_col[:], vs_turned[:, 0 : B * PACK])
 
-        q_codes = sb("q_codes", [P, B * NQ], U32, "second")
-        q_scales = sb("q_scales", [P, B * NQ], U8)
-        nc.vector.quantize_mx(
-            out=q_codes[:].bitcast(FP8X4), scales=q_scales[:], in_=q_bf[:].rearrange("p b q j -> p (b q j)")
-        )
+        q_codes, q_scales = quantize("q", q_bf[:].rearrange("p b q j -> p (b q j)"), "scale_pool")
 
-        vs_col = []
-        for b in range(B):
-            turned = bank(2 + b, "vs_turned%d" % b)
-            for t in range(PACK):
-                nc.tensor.transpose(turned[:, t * P : (t + 1) * P], vs_got[:, b, t, :], ident[:])
-            col = sb("vs_col%d" % b, [P, PACK], F32, "fourth" if b == 1 else None)
-            nc.scalar.copy(col[:], turned[:, 0 : PACK * P : P])
-            vs_col.append(col)
-
-        kw_got = [sb("kw_got%d" % b, [P, N], U32, "first%d" % b) for b in range(B)]
         scores = []
         for b in range(B):
-            nc.vector.tensor_copy(kw_got[b][:], kw_pool[:].indirect(listed(b)))
+            kw_got = sb("kw_got%d" % b, [P, N], U32)
+            nc.vector.tensor_copy(kw_got[:], kw_pool[:].indirect(listed(b)))
             acc = bank(b, "scores%d" % b)
             nc.tensor.matmul_mx(
                 out=acc[:],
                 lhsT=q_codes[:, b * NQ : (b + 1) * NQ].bitcast(FP8X4),
                 lhsT_scale=q_scales[:, b * NQ : (b + 1) * NQ],
-                rhs=kw_got[b][:].bitcast(FP8X4),
+                rhs=kw_got[:].bitcast(FP8X4),
                 rhs_scale=ks_got[:, b * N : (b + 1) * N],
                 start=True,
                 stop=True,
             )
             scores.append(acc)
 
-        totals, p_turned, maxes = [], [], []
+        total = sb("total", [P, B], F32)
+        p_turned = []
         for b in range(B):
             neg_max = sb("neg_max%d" % b, [P, 1], F32)
             nc.vector.tensor_scalar(
-                neg[:, b, 0:N].rearrange("p (t s) -> p t s", t=PACK),
-                scores[b][:].rearrange("p (s t) -> p t s", t=PACK),
+                neg[:, b, 0:N].rearrange("p (u j g r) -> p j g u r", u=2, j=2, g=GROUPS),
+                scores[b][:].rearrange("p (g u r j) -> p j g u r", u=2, j=2, g=GROUPS),
                 -1.0,
-                neg_sink[:, b : b + 1],
+                neg[:, b, N : N + 1],
                 ALU.mult,
                 ALU.min,
                 accum_out=neg_max[:],
             )
             p = sb("p%d" % b, [P, N + 1], F32)
-            total = sb("total%d" % b, [P, 1], F32)
-            nc.scalar.activation(p[:], neg[:, b, 0 : N + 1], ACT.Exp, bias=neg_max[:], scale=-1.0, accum_out=total[:])
+            nc.scalar.activation(
+                p[:], neg[:, b, 0 : N + 1], ACT.Exp, bias=neg_max[:], scale=-1.0, accum_out=total[:, b : b + 1]
+            )
             turned = bank(4 + b, "p_turned%d" % b)
             for t in range(PACK):
                 nc.tensor.transpose(turned[:, t * P : (t + 1) * P], p[:, t * P : (t + 1) * P], ident[:])
-            totals.append(total)
-            maxes.append(neg_max)
             p_turned.append(turned)
 
-        def weigh(b):
-            w_bf = sb("w_bf%d" % b, [P, NQ * PACK], BF16)
-            nc.vector.tensor_tensor(
-                w_bf[:].rearrange("s (q t) -> s q t", t=PACK),
-                p_turned[b][:].rearrange("s (t q) -> s q t", t=PACK),
-                vs_col[b][:].unsqueeze(1).to_broadcast([P, NQ, PACK]),
-                ALU.mult,
-            )
-            return w_bf
-
-        def finish(b, w, inverse):
-            acc = bank(b, "y%d" % b)
-            cols = slice(b * P, (b + 1) * P)
-            for h in range(BLOCKS):
-                nc.tensor.matmul_mx(
-                    out=acc[:, h * P : (h + 1) * P],
-                    lhsT=w[0][:].bitcast(FP8X4),
-                    lhsT_scale=w[1][:],
-                    rhs=v[h][0][:, cols].bitcast(FP8X4),
-                    rhs_scale=v[h][1][:, cols],
-                    start=True,
-                    stop=True,
-                )
-            y = sb("y_out%d" % b, [P, DV], F32)
-            if b == 1:
-                nc.vector.tensor_scalar(y[:], acc[:, 0:DV], inverse[:], None, ALU.mult)
-            else:
-                nc.scalar.activation(y[:], acc[:, 0:DV], ACT.Copy, scale=inverse[:])
-            nc.sync.dma_start(out[b], y[:])
-
-        v = [quantize("v0", v_bf[0], "first0")]
-        turned10 = gather_values(1, 0, 2, True, "third")
-        turned11 = gather_values(1, 1, 3, True, "first1")
+        turned10 = gather_values(1, 0, 3)
+        turned11 = gather_values(1, 1, 6)
         interleave_values(1, 0, turned10)
         interleave_values(1, 1, turned11)
-        inverse = []
-        for b in range(B):
-            inv = sb("inverse%d" % b, [P, 1], F32)
-            nc.vector.reciprocal(inv[:], totals[b][:])
-            inverse.append(inv)
-        w_bf0 = weigh(0)
-        w_bf1 = weigh(1)
-        w0 = quantize("w0", w_bf0)
-        v.append(quantize("v1", v_bf[1], "fourth"))
-        w1 = quantize("w1", w_bf1)
-        finish(0, w0, inverse[0])
-        finish(1, w1, inverse[1])
+
+        w_bf = sb("w_bf", [P, B, NQ * PACK], BF16, "last_pool")
+
+        def weigh(b):
+            nc.vector.tensor_tensor(
+                w_bf[:, b, :].rearrange("s (q t) -> s q t", t=PACK),
+                p_turned[b][:].rearrange("s (t q) -> s q t", t=PACK),
+                vs_col[:, b * PACK : (b + 1) * PACK].unsqueeze(1).to_broadcast([P, NQ, PACK]),
+                ALU.mult,
+            )
+
+        inverse = sb("inverse", [P, B], F32)
+
+        def finish(b, w, v):
+            acc = bank(b, "y%d" % b)
+            nc.tensor.matmul_mx(
+                out=acc[:, 0:DV],
+                lhsT=w[0][:].bitcast(FP8X4),
+                lhsT_scale=w[1][:],
+                rhs=v[0][:].bitcast(FP8X4),
+                rhs_scale=v[1][:],
+                start=True,
+                stop=True,
+            )
+            y = sb("y_out%d" % b, [P, DV], F32)
+            if b == 1:
+                nc.vector.tensor_scalar(y[:], acc[:, 0:DV], inverse[:, b : b + 1], None, ALU.mult)
+            else:
+                nc.scalar.activation(y[:], acc[:, 0:DV], ACT.Copy, scale=inverse[:, b : b + 1])
+            nc.sync.dma_start(out[b], y[:])
+
+        weigh(0)
+        v0 = quantize("v0", v_bf[0][:])
+        weigh(1)
+        w0 = quantize("w0", w_bf[:, 0, :])
+        nc.vector.reciprocal(inverse[:], total[:])
+        v1 = quantize("v1", v_bf[1][:])
+        w1 = quantize("w1", w_bf[:, 1, :])
+        finish(0, w0, v0)
+        finish(1, w1, v1)

@@ -19,16 +19,13 @@ ACT = mybir.ActivationFunctionType
 P = 128
 PACK = 4
 LIST_COLS = N // 16
-GROUPS = 16
-RUN = 16
-FIRST = 512
+BLOCKS = DV // P
 
 
 def tile_attend_sink_kernel(tc, qT, k_words, k_scales, vT, vs, sink, offs, out):
     nc = tc.nc
     with ExitStack() as ctx:
         held = ctx.enter_context(tc.tile_pool(name="held", bufs=1))
-        shared = ctx.enter_context(tc.tile_pool(name="shared", bufs=1))
         psum = ctx.enter_context(tc.psum_pool(name="psum", bufs=1))
 
         def sb(name, shape, dtype, tag=None):
@@ -45,116 +42,79 @@ def tile_attend_sink_kernel(tc, qT, k_words, k_scales, vT, vs, sink, offs, out):
 
         ks_pool = sb("ks_pool", [P, T // 4], I32)
         vs_pool = sb("vs_pool", [P, T], F32, "scale_pool")
-        nc.vector.memset(ks_pool[:, 0 : T // 8], 0)
-        nc.gpsimd.memset(ks_pool[:, T // 8 : T // 4], 0)
+        sink_rows = sb("sink_rows", [P, NQ], F32)
         seed = sb("seed", [P, 1], F32)
+        nc.vector.memset(ks_pool[:], 0)
+        nc.vector.memset(vs_pool[:], 0.0)
         nc.vector.memset(seed[:], 0.0)
-        nc.vector.memset(vs_pool[:, 0 : T // 2], 0.0)
-        nc.gpsimd.memset(vs_pool[:, T // 2 : T], 0.0)
+        nc.vector.memset(sink_rows[:], 0.0)
         ident = sb("ident", [P, P], F32)
         make_identity(nc, ident[:])
 
-        v_pool0 = sb("v_pool0", [P, T], F32)
-        pieces = [slice(0, FIRST), slice(FIRST, (FIRST + T) // 2), slice((FIRST + T) // 2, T)]
-        nc.sync.dma_start(v_pool0[:, pieces[0]], vT[0:P, pieces[0]])
+        q_raw = [sb("q_raw%d" % b, [P, PACK, NQ], F32) for b in range(B)]
+
+        def load_queries(b):
+            nc.sync.dma_start(
+                q_raw[b][:].rearrange("p j q -> p (j q)"), qT[b].rearrange("(p j) q -> p (j q)", j=PACK)
+            )
+
+        load_queries(0)
         ks_rows = k_scales[0].bitcast(I32)
         for r in range(4):
             queue = nc.sync if r < 2 else nc.scalar
             queue.dma_start(ks_pool[r:P:32, :], ks_rows[r:16:4, :])
-        for cols in pieces[1:]:
-            nc.sync.dma_start(v_pool0[:, cols], vT[0:P, cols])
-        warm = sb("warm", [P, 1], F32)
-        nc.scalar.activation(warm[:], seed[:], ACT.Exp)
-        nc.sync.dma_start(vs_pool[0:1, :], vs[0:1, :])
-        q_raw = shared.tile([P, B, PACK, NQ], F32, name="q_raw", offset=0, align_bytes=64)
-        nc.sync.dma_start(
-            q_raw[:].rearrange("p b j q -> p b (j q)"),
-            qT.rearrange("b (p j) q -> p b (j q)", j=PACK),
-        )
-        sink_cols = sb("sink_cols", [P, B], F32)
-        with nc.allow_non_contiguous_dma(reason="one logit a partition"):
-            nc.sync.dma_start(sink_cols[:], sink.rearrange("b q o -> q (b o)"))
+        nc.scalar.dma_start(vs_pool[0:1, :], vs[0:1, :])
         kw_pool = sb("kw_pool", [P, T], U32)
         nc.sync.dma_start(kw_pool[:].bitcast(I32), k_words[0].rearrange("p n r -> p (n r)").bitcast(I32))
-        v_pool1 = sb("v_pool1", [P, T], F32, "last_pool")
-        nc.sync.dma_start(v_pool1[:], vT[P : 2 * P, :])
+        load_queries(1)
+        nc.sync.dma_start(sink_rows[0:B, :], sink.rearrange("b q o -> b (q o)"))
+        v_pool = [sb("v_pool%d" % h, [P, T], F32) for h in range(BLOCKS)]
+        for h in range(BLOCKS):
+            nc.sync.dma_start(v_pool[h][:], vT[h * P : (h + 1) * P, :])
+        warm = sb("warm", [P, 1], F32)
+        nc.scalar.activation(warm[:], seed[:], ACT.Exp)
 
-        ks_got = sb("ks_got", [P, B * N], U8)
-        nc.vector.tensor_copy(ks_got[:], ks_pool[:].bitcast(U8).indirect(offsets[:]))
-        vs_got = sb("vs_got", [P, 2, B * GROUPS, RUN], F32)
-        nc.vector.tensor_copy(
-            vs_got[:].bitcast(U32).rearrange("p u g x -> p g u x"), vs_pool[:].bitcast(U32).indirect(offsets[:])
-        )
-
-        v_pool_bf = sb("v_pool_bf", [P, T], BF16, "first_pool")
-        for cols in pieces:
-            nc.scalar.activation(v_pool_bf[:, cols], v_pool0[:, cols], ACT.Copy)
-        neg = sb("neg", [P, B, N + 16], F32)
-        nc.scalar.activation(neg[:, :, N], sink_cols[:], ACT.Copy, scale=-1.0)
-        q_bf = sb("q_bf", [P, B, NQ, PACK], BF16)
-        nc.scalar.copy(q_bf[:], q_raw[:].rearrange("p b j q -> p b q j"))
-
-        def gather_values(h, b, bank_index):
-            if h == 0:
-                got = shared.tile([P, 2, GROUPS, RUN], BF16, name="v_got0%d" % b, offset=2 * N * b, align_bytes=64)
-            else:
-                got = sb("v_got1%d" % b, [P, 2, GROUPS, RUN], BF16)
-            dealt = got[:].rearrange("e u g x -> e g u x")
-            if h == 1:
-                nc.vector.tensor_copy(dealt, v_pool1[:].indirect(listed(b)))
-            else:
-                nc.scalar.activation(dealt, v_pool_bf[:].indirect(listed(b)), ACT.Copy)
-            words = got[:].rearrange("e u g x -> e (u g x)").bitcast(F32)
-            turned = bank(bank_index, "v_turned%d%d" % (h, b))
-            for u in range(2):
-                nc.tensor.transpose(turned[:, u * P : (u + 1) * P], words[:, u * P : (u + 1) * P], ident[:])
-            return turned
-
-        v_bf = [sb("v_bf%d" % b, [P, DV * PACK], BF16) for b in range(B)]
-
-        def interleave_values(h, b, turned):
-            nc.scalar.copy(
-                v_bf[b][:, h * N : (h + 1) * N].bitcast(F32).rearrange("s (e u) -> s e u", u=2),
-                turned[:, 0 : 2 * P].rearrange("s (u e) -> s e u", u=2),
-            )
-
-        def quantize(name, values, tag=None):
+        def quantize(name, values):
             width = values.shape[1] // PACK
-            codes = sb(name + "_codes", [P, width], U32, tag)
+            codes = sb(name + "_codes", [P, width], U32)
             scales = sb(name + "_scales", [P, width], U8)
             nc.vector.quantize_mx(out=codes[:].bitcast(FP8X4), scales=scales[:], in_=values)
             return codes, scales
 
-        vs_turned = bank(2, "vs_turned")
+        def round_queries(b):
+            q_bf = sb("q_bf%d" % b, [P, NQ, PACK], BF16)
+            nc.scalar.copy(q_bf[:], q_raw[b][:].rearrange("p j q -> p q j"))
+            return quantize("q%d" % b, q_bf[:].rearrange("p q j -> p (q j)"))
+
+        ks_got = sb("ks_got", [P, B * N], U8)
+        nc.vector.tensor_copy(ks_got[:], ks_pool[:].bitcast(U8).indirect(offsets[:]))
+        q = [round_queries(0)]
+        vs_got = sb("vs_got", [P, B * N], F32)
+        nc.vector.tensor_copy(vs_got[:], vs_pool[:].indirect(offsets[:]))
+
+        kw_both = sb("kw_both", [P, B * N], U32, "scale_pool")
+        kw_got = [kw_both[:, b * N : (b + 1) * N] for b in range(B)]
         for b in range(B):
-            for u in range(2):
-                for j in range(2):
-                    col = PACK * b + 2 * u + j
-                    nc.tensor.transpose(
-                        vs_turned[:, col : col + P],
-                        vs_got[:].rearrange("p u g x -> p u (g x)")[:, u, 2 * P * b + j : 2 * P * (b + 1) : 2],
-                        ident[:],
-                    )
+            nc.vector.tensor_copy(kw_got[b], kw_pool[:].indirect(listed(b)))
+        q.append(round_queries(1))
 
-        turned00 = gather_values(0, 0, 6)
-        turned01 = gather_values(0, 1, 7)
-        interleave_values(0, 0, turned00)
-        interleave_values(0, 1, turned01)
-        vs_col = sb("vs_col", [P, B * PACK], F32, "first_pool")
-        nc.scalar.copy(vs_col[:], vs_turned[:, 0 : B * PACK])
+        vs_col = [sb("vs_col%d" % b, [P, PACK], F32) for b in range(B)]
+        for b in range(B):
+            nc.scalar.dma_start(vs_col[b][:], vs_got[0:1, b * N : (b + 1) * N].rearrange("o (s t) -> o s t", t=PACK))
 
-        q_codes, q_scales = quantize("q", q_bf[:].rearrange("p b q j -> p (b q j)"), "scale_pool")
+        neg = sb("neg", [P, B, N + 16], F32)
+        sink_turned = bank(2, "sink_turned")
+        nc.tensor.transpose(sink_turned[:, 0:P], sink_rows[:], ident[:])
+        nc.scalar.activation(neg[:, :, N], sink_turned[:, 0:B], ACT.Copy, scale=-1.0)
 
         scores = []
         for b in range(B):
-            kw_got = sb("kw_got%d" % b, [P, N], U32)
-            nc.vector.tensor_copy(kw_got[:], kw_pool[:].indirect(listed(b)))
             acc = bank(b, "scores%d" % b)
             nc.tensor.matmul_mx(
                 out=acc[:],
-                lhsT=q_codes[:, b * NQ : (b + 1) * NQ].bitcast(FP8X4),
-                lhsT_scale=q_scales[:, b * NQ : (b + 1) * NQ],
-                rhs=kw_got[:].bitcast(FP8X4),
+                lhsT=q[b][0][:].bitcast(FP8X4),
+                lhsT_scale=q[b][1][:],
+                rhs=kw_got[b].bitcast(FP8X4),
                 rhs_scale=ks_got[:, b * N : (b + 1) * N],
                 start=True,
                 stop=True,
@@ -166,8 +126,8 @@ def tile_attend_sink_kernel(tc, qT, k_words, k_scales, vT, vs, sink, offs, out):
         for b in range(B):
             neg_max = sb("neg_max%d" % b, [P, 1], F32)
             nc.vector.tensor_scalar(
-                neg[:, b, 0:N].rearrange("p (u j g r) -> p j g u r", u=2, j=2, g=GROUPS),
-                scores[b][:].rearrange("p (g u r j) -> p j g u r", u=2, j=2, g=GROUPS),
+                neg[:, b, 0:N].rearrange("p (t s) -> p t s", t=PACK),
+                scores[b][:].rearrange("p (s t) -> p t s", t=PACK),
                 -1.0,
                 neg[:, b, N : N + 1],
                 ALU.mult,
@@ -183,18 +143,27 @@ def tile_attend_sink_kernel(tc, qT, k_words, k_scales, vT, vs, sink, offs, out):
                 nc.tensor.transpose(turned[:, t * P : (t + 1) * P], p[:, t * P : (t + 1) * P], ident[:])
             p_turned.append(turned)
 
-        turned10 = gather_values(1, 0, 3)
-        turned11 = gather_values(1, 1, 6)
-        interleave_values(1, 0, turned10)
-        interleave_values(1, 1, turned11)
+        v_bf = [sb("v_bf%d" % b, [P, DV * PACK], BF16) for b in range(B)]
+        for h in range(BLOCKS):
+            for b in range(B):
+                got = sb("v_got%d%d" % (h, b), [P, N], BF16)
+                nc.vector.tensor_copy(got[:], v_pool[h][:].indirect(listed(b)))
+                words = got[:].bitcast(F32)
+                turned = bank((6, 7, 2, 3)[B * h + b], "v_turned%d%d" % (h, b))
+                for u in range(2):
+                    nc.tensor.transpose(turned[:, u * P : (u + 1) * P], words[:, u : 2 * P : 2], ident[:])
+                nc.scalar.copy(
+                    v_bf[b][:, h * N : (h + 1) * N].bitcast(F32).rearrange("s (e u) -> s e u", u=2),
+                    turned[:, 0 : 2 * P].rearrange("s (u e) -> s e u", u=2),
+                )
 
-        w_bf = sb("w_bf", [P, B, NQ * PACK], BF16, "last_pool")
+        w_bf = sb("w_bf", [P, B, NQ * PACK], BF16, "v_pool1")
 
         def weigh(b):
             nc.vector.tensor_tensor(
                 w_bf[:, b, :].rearrange("s (q t) -> s q t", t=PACK),
                 p_turned[b][:].rearrange("s (t q) -> s q t", t=PACK),
-                vs_col[:, b * PACK : (b + 1) * PACK].unsqueeze(1).to_broadcast([P, NQ, PACK]),
+                vs_col[b][:].unsqueeze(1).to_broadcast([P, NQ, PACK]),
                 ALU.mult,
             )
 

@@ -26,6 +26,7 @@ def tile_attend_sink_kernel(tc, qT, k_words, k_scales, vT, vs, sink, offs, out):
     nc = tc.nc
     with ExitStack() as ctx:
         held = ctx.enter_context(tc.tile_pool(name="held", bufs=1))
+        late = ctx.enter_context(tc.tile_pool(name="late", bufs=1))
         psum = ctx.enter_context(tc.psum_pool(name="psum", bufs=1))
 
         def sb(name, shape, dtype, tag=None):
@@ -45,50 +46,49 @@ def tile_attend_sink_kernel(tc, qT, k_words, k_scales, vT, vs, sink, offs, out):
         sink_rows = sb("sink_rows", [P, NQ], F32)
         seed = sb("seed", [P, 1], F32)
         nc.vector.memset(ks_pool[:], 0)
-        nc.vector.memset(vs_pool[:], 0.0)
-        nc.vector.memset(seed[:], 0.0)
         nc.vector.memset(sink_rows[:], 0.0)
+        nc.vector.memset(seed[:], 0.0)
+        nc.vector.memset(vs_pool[:].bitcast(I32), 0)
         ident = sb("ident", [P, P], F32)
         make_identity(nc, ident[:])
 
-        q_raw = [sb("q_raw%d" % b, [P, PACK, NQ], F32) for b in range(B)]
-
-        def load_queries(b):
-            nc.sync.dma_start(
-                q_raw[b][:].rearrange("p j q -> p (j q)"), qT[b].rearrange("(p j) q -> p (j q)", j=PACK)
-            )
-
-        load_queries(0)
+        q_raw = sb("q_raw", [P, B, PACK, NQ], F32)
+        nc.sync.dma_start(
+            q_raw[:].rearrange("p b j q -> p b (j q)"),
+            qT.rearrange("b (p j) q -> p b (j q)", j=PACK),
+        )
         ks_rows = k_scales[0].bitcast(I32)
         for r in range(4):
-            queue = nc.sync if r < 2 else nc.scalar
-            queue.dma_start(ks_pool[r:P:32, :], ks_rows[r:16:4, :])
-        nc.scalar.dma_start(vs_pool[0:1, :], vs[0:1, :])
+            nc.sync.dma_start(ks_pool[r:P:32, :], ks_rows[r:16:4, :])
+        nc.sync.dma_start(sink_rows[0:B, :], sink.rearrange("b q o -> b (q o)"))
+        nc.sync.dma_start(vs_pool[0:1, :], vs[0:1, :])
         kw_pool = sb("kw_pool", [P, T], U32)
         nc.sync.dma_start(kw_pool[:].bitcast(I32), k_words[0].rearrange("p n r -> p (n r)").bitcast(I32))
-        load_queries(1)
-        nc.sync.dma_start(sink_rows[0:B, :], sink.rearrange("b q o -> b (q o)"))
-        v_pool = [sb("v_pool%d" % h, [P, T], F32) for h in range(BLOCKS)]
+        v_pool = [sb("v_pool0", [P, T], F32), late.tile([P, T], F32, name="v_pool1", offset=0, align_bytes=64)]
         for h in range(BLOCKS):
             nc.sync.dma_start(v_pool[h][:], vT[h * P : (h + 1) * P, :])
         warm = sb("warm", [P, 1], F32)
         nc.scalar.activation(warm[:], seed[:], ACT.Exp)
 
-        def quantize(name, values):
+        def quantize(name, values, offset=None):
             width = values.shape[1] // PACK
-            codes = sb(name + "_codes", [P, width], U32)
+            if offset is None:
+                codes = sb(name + "_codes", [P, width], U32)
+            else:
+                codes = late.tile([P, width], U32, name=name + "_codes", offset=offset, align_bytes=64)
             scales = sb(name + "_scales", [P, width], U8)
             nc.vector.quantize_mx(out=codes[:].bitcast(FP8X4), scales=scales[:], in_=values)
             return codes, scales
 
-        def round_queries(b):
-            q_bf = sb("q_bf%d" % b, [P, NQ, PACK], BF16)
-            nc.scalar.copy(q_bf[:], q_raw[b][:].rearrange("p j q -> p q j"))
-            return quantize("q%d" % b, q_bf[:].rearrange("p q j -> p (q j)"))
-
         ks_got = sb("ks_got", [P, B * N], U8)
         nc.vector.tensor_copy(ks_got[:], ks_pool[:].bitcast(U8).indirect(offsets[:]))
-        q = [round_queries(0)]
+        q_bf = sb("q_bf", [P, B, NQ, PACK], BF16)
+        nc.scalar.copy(q_bf[:], q_raw[:].rearrange("p b j q -> p b q j"))
+        q_codes = sb("q_codes", [P, B * NQ], U32, "ks_pool")
+        q_scales = sb("q_scales", [P, B * NQ], U8)
+        nc.vector.quantize_mx(
+            out=q_codes[:].bitcast(FP8X4), scales=q_scales[:], in_=q_bf[:].rearrange("p b q j -> p (b q j)")
+        )
         vs_got = sb("vs_got", [P, B * N], F32)
         nc.vector.tensor_copy(vs_got[:], vs_pool[:].indirect(offsets[:]))
 
@@ -96,11 +96,10 @@ def tile_attend_sink_kernel(tc, qT, k_words, k_scales, vT, vs, sink, offs, out):
         kw_got = [kw_both[:, b * N : (b + 1) * N] for b in range(B)]
         for b in range(B):
             nc.vector.tensor_copy(kw_got[b], kw_pool[:].indirect(listed(b)))
-        q.append(round_queries(1))
 
         vs_col = [sb("vs_col%d" % b, [P, PACK], F32) for b in range(B)]
         for b in range(B):
-            nc.scalar.dma_start(vs_col[b][:], vs_got[0:1, b * N : (b + 1) * N].rearrange("o (s t) -> o s t", t=PACK))
+            nc.sync.dma_start(vs_col[b][:], vs_got[0:1, b * N : (b + 1) * N].rearrange("o (s t) -> o s t", t=PACK))
 
         neg = sb("neg", [P, B, N + 16], F32)
         sink_turned = bank(2, "sink_turned")
@@ -112,8 +111,8 @@ def tile_attend_sink_kernel(tc, qT, k_words, k_scales, vT, vs, sink, offs, out):
             acc = bank(b, "scores%d" % b)
             nc.tensor.matmul_mx(
                 out=acc[:],
-                lhsT=q[b][0][:].bitcast(FP8X4),
-                lhsT_scale=q[b][1][:],
+                lhsT=q_codes[:, b * NQ : (b + 1) * NQ].bitcast(FP8X4),
+                lhsT_scale=q_scales[:, b * NQ : (b + 1) * NQ],
                 rhs=kw_got[b].bitcast(FP8X4),
                 rhs_scale=ks_got[:, b * N : (b + 1) * N],
                 start=True,
@@ -143,7 +142,7 @@ def tile_attend_sink_kernel(tc, qT, k_words, k_scales, vT, vs, sink, offs, out):
                 nc.tensor.transpose(turned[:, t * P : (t + 1) * P], p[:, t * P : (t + 1) * P], ident[:])
             p_turned.append(turned)
 
-        v_bf = [sb("v_bf%d" % b, [P, DV * PACK], BF16) for b in range(B)]
+        v_bf = [[sb("v_bf%d%d" % (h, b), [P, N], BF16) for b in range(B)] for h in range(BLOCKS)]
         for h in range(BLOCKS):
             for b in range(B):
                 got = sb("v_got%d%d" % (h, b), [P, N], BF16)
@@ -153,11 +152,11 @@ def tile_attend_sink_kernel(tc, qT, k_words, k_scales, vT, vs, sink, offs, out):
                 for u in range(2):
                     nc.tensor.transpose(turned[:, u * P : (u + 1) * P], words[:, u : 2 * P : 2], ident[:])
                 nc.scalar.copy(
-                    v_bf[b][:, h * N : (h + 1) * N].bitcast(F32).rearrange("s (e u) -> s e u", u=2),
+                    v_bf[h][b][:].bitcast(F32).rearrange("s (e u) -> s e u", u=2),
                     turned[:, 0 : 2 * P].rearrange("s (u e) -> s e u", u=2),
                 )
 
-        w_bf = sb("w_bf", [P, B, NQ * PACK], BF16, "v_pool1")
+        w_bf = late.tile([P, B, NQ * PACK], BF16, name="w_bf", offset=0, align_bytes=64)
 
         def weigh(b):
             nc.vector.tensor_tensor(
@@ -169,10 +168,9 @@ def tile_attend_sink_kernel(tc, qT, k_words, k_scales, vT, vs, sink, offs, out):
 
         inverse = sb("inverse", [P, B], F32)
 
-        def finish(b, w, v):
-            acc = bank(b, "y%d" % b)
+        def multiply(acc, w, v):
             nc.tensor.matmul_mx(
-                out=acc[:, 0:DV],
+                out=acc,
                 lhsT=w[0][:].bitcast(FP8X4),
                 lhsT_scale=w[1][:],
                 rhs=v[0][:].bitcast(FP8X4),
@@ -180,19 +178,28 @@ def tile_attend_sink_kernel(tc, qT, k_words, k_scales, vT, vs, sink, offs, out):
                 start=True,
                 stop=True,
             )
-            y = sb("y_out%d" % b, [P, DV], F32)
-            if b == 1:
-                nc.vector.tensor_scalar(y[:], acc[:, 0:DV], inverse[:, b : b + 1], None, ALU.mult)
-            else:
-                nc.scalar.activation(y[:], acc[:, 0:DV], ACT.Copy, scale=inverse[:, b : b + 1])
-            nc.sync.dma_start(out[b], y[:])
 
         weigh(0)
-        v0 = quantize("v0", v_bf[0][:])
+        v00 = quantize("v00", v_bf[0][0][:], 2048)
         weigh(1)
         w0 = quantize("w0", w_bf[:, 0, :])
+        v01 = quantize("v01", v_bf[0][1][:], 2560)
+        v10 = quantize("v10", v_bf[1][0][:])
         nc.vector.reciprocal(inverse[:], total[:])
-        v1 = quantize("v1", v_bf[1][:])
         w1 = quantize("w1", w_bf[:, 1, :])
-        finish(0, w0, v0)
-        finish(1, w1, v1)
+        v11 = quantize("v11", v_bf[1][1][:])
+
+        acc0 = bank(0, "y0")
+        multiply(acc0[:, 0:P], w0, v00)
+        multiply(acc0[:, P:DV], w0, v10)
+        y0 = sb("y_out0", [P, DV], F32)
+        nc.scalar.activation(y0[:], acc0[:, 0:DV], ACT.Copy, scale=inverse[:, 0:1])
+        nc.sync.dma_start(out[0], y0[:])
+        acc1 = [bank(1, "y01"), bank(7, "y11")]
+        multiply(acc1[0][:, 0:P], w1, v01)
+        multiply(acc1[1][:, 0:P], w1, v11)
+        y1 = [sb("y_out%d1" % h, [P, P], F32) for h in range(BLOCKS)]
+        nc.scalar.activation(y1[0][:], acc1[0][:, 0:P], ACT.Copy, scale=inverse[:, 1:2])
+        nc.scalar.dma_start(out[1][:, 0:P], y1[0][:])
+        nc.vector.tensor_scalar(y1[1][:], acc1[1][:, 0:P], inverse[:, 1:2], None, ALU.mult)
+        nc.sync.dma_start(out[1][:, P:DV], y1[1][:])

@@ -27,6 +27,7 @@ def tile_attend_sink_kernel(tc, qT, k_words, k_scales, vT, vs, sink, offs, out):
     with ExitStack() as ctx:
         held = ctx.enter_context(tc.tile_pool(name="held", bufs=1))
         late = ctx.enter_context(tc.tile_pool(name="late", bufs=1))
+        early = ctx.enter_context(tc.tile_pool(name="early", bufs=1))
         psum = ctx.enter_context(tc.psum_pool(name="psum", bufs=1))
 
         def sb(name, shape, dtype, tag=None):
@@ -64,9 +65,12 @@ def tile_attend_sink_kernel(tc, qT, k_words, k_scales, vT, vs, sink, offs, out):
         nc.sync.dma_start(vs_pool[0:1, :], vs[0:1, :])
         kw_pool = sb("kw_pool", [P, T], U32)
         nc.sync.dma_start(kw_pool[:].bitcast(I32), k_words[0].rearrange("p n r -> p (n r)").bitcast(I32))
-        v_pool = [sb("v_pool0", [P, T], F32), late.tile([P, T], F32, name="v_pool1", offset=0, align_bytes=64)]
-        for h in range(BLOCKS):
-            nc.sync.dma_start(v_pool[h][:], vT[h * P : (h + 1) * P, :])
+        v_pool0 = early.tile([P, T], F32, name="v_pool0", offset=0, align_bytes=64)
+        pieces = [slice(0, 768), slice(768, 1536), slice(1536, T)]
+        for cols in pieces:
+            nc.sync.dma_start(v_pool0[:, cols], vT[0:P, cols])
+        v_pool1 = late.tile([P, T], F32, name="v_pool1", offset=0, align_bytes=64)
+        nc.sync.dma_start(v_pool1[:], vT[P : 2 * P, :])
         warm = sb("warm", [P, 1], F32)
         nc.scalar.activation(warm[:], seed[:], ACT.Exp)
 
@@ -106,6 +110,32 @@ def tile_attend_sink_kernel(tc, qT, k_words, k_scales, vT, vs, sink, offs, out):
         nc.tensor.transpose(sink_turned[:, 0:P], sink_rows[:], ident[:])
         nc.scalar.activation(neg[:, :, N], sink_turned[:, 0:B], ACT.Copy, scale=-1.0)
 
+        v_pool_bf = sb("v_pool_bf", [P, T], BF16)
+        for cols in pieces:
+            nc.scalar.activation(v_pool_bf[:, cols], v_pool0[:, cols], ACT.Copy)
+
+        def gather_values(h, b):
+            got = sb("v_got%d%d" % (h, b), [P, N], BF16)
+            if h == 0:
+                nc.scalar.activation(got[:], v_pool_bf[:].indirect(listed(b)), ACT.Copy)
+            else:
+                nc.vector.tensor_copy(got[:], v_pool1[:].indirect(listed(b)))
+            return got
+
+        v_bf = [[sb("v_bf%d%d" % (h, b), [P, N], BF16) for b in range(B)] for h in range(BLOCKS)]
+
+        def turn_values(h, b, got, index):
+            words = got[:].bitcast(F32)
+            turned = bank(index, "v_turned%d%d" % (h, b))
+            for u in range(2):
+                nc.tensor.transpose(turned[:, u * P : (u + 1) * P], words[:, u : 2 * P : 2], ident[:])
+            nc.scalar.copy(
+                v_bf[h][b][:].bitcast(F32).rearrange("s (e u) -> s e u", u=2),
+                turned[:, 0 : 2 * P].rearrange("s (u e) -> s e u", u=2),
+            )
+
+        got00 = gather_values(0, 0)
+
         scores = []
         for b in range(B):
             acc = bank(b, "scores%d" % b)
@@ -133,7 +163,7 @@ def tile_attend_sink_kernel(tc, qT, k_words, k_scales, vT, vs, sink, offs, out):
                 ALU.min,
                 accum_out=neg_max[:],
             )
-            p = sb("p%d" % b, [P, N + 1], F32)
+            p = early.tile([P, N + 1], F32, name="p%d" % b, offset=4 * T // B * b, align_bytes=64)
             nc.scalar.activation(
                 p[:], neg[:, b, 0 : N + 1], ACT.Exp, bias=neg_max[:], scale=-1.0, accum_out=total[:, b : b + 1]
             )
@@ -142,19 +172,11 @@ def tile_attend_sink_kernel(tc, qT, k_words, k_scales, vT, vs, sink, offs, out):
                 nc.tensor.transpose(turned[:, t * P : (t + 1) * P], p[:, t * P : (t + 1) * P], ident[:])
             p_turned.append(turned)
 
-        v_bf = [[sb("v_bf%d%d" % (h, b), [P, N], BF16) for b in range(B)] for h in range(BLOCKS)]
-        for h in range(BLOCKS):
-            for b in range(B):
-                got = sb("v_got%d%d" % (h, b), [P, N], BF16)
-                nc.vector.tensor_copy(got[:], v_pool[h][:].indirect(listed(b)))
-                words = got[:].bitcast(F32)
-                turned = bank((6, 7, 2, 3)[B * h + b], "v_turned%d%d" % (h, b))
-                for u in range(2):
-                    nc.tensor.transpose(turned[:, u * P : (u + 1) * P], words[:, u : 2 * P : 2], ident[:])
-                nc.scalar.copy(
-                    v_bf[h][b][:].bitcast(F32).rearrange("s (e u) -> s e u", u=2),
-                    turned[:, 0 : 2 * P].rearrange("s (u e) -> s e u", u=2),
-                )
+        got01 = gather_values(0, 1)
+        turn_values(0, 0, got00, 6)
+        turn_values(1, 0, gather_values(1, 0), 2)
+        turn_values(1, 1, gather_values(1, 1), 3)
+        turn_values(0, 1, got01, 2)
 
         w_bf = late.tile([P, B, NQ * PACK], BF16, name="w_bf", offset=0, align_bytes=64)
 
@@ -183,11 +205,11 @@ def tile_attend_sink_kernel(tc, qT, k_words, k_scales, vT, vs, sink, offs, out):
         v00 = quantize("v00", v_bf[0][0][:], 2048)
         weigh(1)
         w0 = quantize("w0", w_bf[:, 0, :])
-        v01 = quantize("v01", v_bf[0][1][:], 2560)
         v10 = quantize("v10", v_bf[1][0][:])
         nc.vector.reciprocal(inverse[:], total[:])
         w1 = quantize("w1", w_bf[:, 1, :])
         v11 = quantize("v11", v_bf[1][1][:])
+        v01 = quantize("v01", v_bf[0][1][:])
 
         acc0 = bank(0, "y0")
         multiply(acc0[:, 0:P], w0, v00)
@@ -196,10 +218,10 @@ def tile_attend_sink_kernel(tc, qT, k_words, k_scales, vT, vs, sink, offs, out):
         nc.scalar.activation(y0[:], acc0[:, 0:DV], ACT.Copy, scale=inverse[:, 0:1])
         nc.sync.dma_start(out[0], y0[:])
         acc1 = [bank(1, "y01"), bank(7, "y11")]
-        multiply(acc1[0][:, 0:P], w1, v01)
         multiply(acc1[1][:, 0:P], w1, v11)
+        multiply(acc1[0][:, 0:P], w1, v01)
         y1 = [sb("y_out%d1" % h, [P, P], F32) for h in range(BLOCKS)]
-        nc.scalar.activation(y1[0][:], acc1[0][:, 0:P], ACT.Copy, scale=inverse[:, 1:2])
-        nc.scalar.dma_start(out[1][:, 0:P], y1[0][:])
-        nc.vector.tensor_scalar(y1[1][:], acc1[1][:, 0:P], inverse[:, 1:2], None, ALU.mult)
-        nc.sync.dma_start(out[1][:, P:DV], y1[1][:])
+        nc.scalar.activation(y1[1][:], acc1[1][:, 0:P], ACT.Copy, scale=inverse[:, 1:2])
+        nc.scalar.dma_start(out[1][:, P:DV], y1[1][:])
+        nc.vector.tensor_scalar(y1[0][:], acc1[0][:, 0:P], inverse[:, 1:2], None, ALU.mult)
+        nc.sync.dma_start(out[1][:, 0:P], y1[0][:])

@@ -19,22 +19,24 @@ ACT = mybir.ActivationFunctionType
 P = 128
 PACK = 4
 LIST_COLS = N // 16
-BLOCKS = DV // P
+HALVES = DV // P
+BANK = 512
+LINE = 16
+CUTS = (0, 1280, 1792, T)
 
 
 def tile_attend_sink_kernel(tc, qT, k_words, k_scales, vT, vs, sink, offs, out):
     nc = tc.nc
     with ExitStack() as ctx:
         held = ctx.enter_context(tc.tile_pool(name="held", bufs=1))
-        late = ctx.enter_context(tc.tile_pool(name="late", bufs=1))
-        early = ctx.enter_context(tc.tile_pool(name="early", bufs=1))
+        half0_bytes = ctx.enter_context(tc.tile_pool(name="half0_bytes", bufs=1))
         psum = ctx.enter_context(tc.psum_pool(name="psum", bufs=1))
 
         def sb(name, shape, dtype, tag=None):
             return held.tile(shape, dtype, name=name, tag=tag or name, align_bytes=64)
 
         def bank(index, name):
-            return psum.tile([P, 512], F32, name=name, tag="bank%d" % index)
+            return psum.tile([P, BANK], F32, name=name, tag="bank%d" % index)
 
         offsets = held.tile([P, B * LIST_COLS], U16, name="offsets")
         nc.sync.dma_start(offsets[:], offs)
@@ -43,76 +45,94 @@ def tile_attend_sink_kernel(tc, qT, k_words, k_scales, vT, vs, sink, offs, out):
             return offsets[:, b * LIST_COLS : (b + 1) * LIST_COLS]
 
         ks_pool = sb("ks_pool", [P, T // 4], I32)
-        vs_pool = sb("vs_pool", [P, T], F32, "scale_pool")
+        vs_pool = sb("vs_pool", [P, T], F32)
         sink_rows = sb("sink_rows", [P, NQ], F32)
-        seed = sb("seed", [P, 1], F32)
         nc.vector.memset(ks_pool[:], 0)
         nc.vector.memset(sink_rows[:], 0.0)
-        nc.vector.memset(seed[:], 0.0)
         nc.vector.memset(vs_pool[:].bitcast(I32), 0)
         ident = sb("ident", [P, P], F32)
         make_identity(nc, ident[:])
 
-        q_raw = sb("q_raw", [P, B, PACK, NQ], F32)
-        nc.sync.dma_start(
-            q_raw[:].rearrange("p b j q -> p b (j q)"),
-            qT.rearrange("b (p j) q -> p b (j q)", j=PACK),
-        )
+        q_raw = [sb("q_raw%d" % b, [P, PACK, NQ], F32) for b in range(B)]
+
+        def load_queries(b):
+            nc.sync.dma_start(
+                q_raw[b][:].rearrange("p j q -> p (j q)"), qT[b].rearrange("(p j) q -> p (j q)", j=PACK)
+            )
+
+        load_queries(0)
         ks_rows = k_scales[0].bitcast(I32)
         for r in range(4):
-            nc.sync.dma_start(ks_pool[r:P:32, :], ks_rows[r:16:4, :])
+            queue = nc.sync if r < 2 else nc.scalar
+            queue.dma_start(ks_pool[r:P:32, :], ks_rows[r:16:4, :])
         nc.sync.dma_start(sink_rows[0:B, :], sink.rearrange("b q o -> b (q o)"))
+        v_pool0 = half0_bytes.tile([P, T], F32, name="v_pool0", offset=0, align_bytes=64)
+        pieces = [slice(lo, hi) for lo, hi in zip(CUTS, CUTS[1:])]
+        nc.sync.dma_start(v_pool0[:, pieces[0]], vT[0:P, pieces[0]])
         nc.sync.dma_start(vs_pool[0:1, :], vs[0:1, :])
         kw_pool = sb("kw_pool", [P, T], U32)
         nc.sync.dma_start(kw_pool[:].bitcast(I32), k_words[0].rearrange("p n r -> p (n r)").bitcast(I32))
-        v_pool0 = early.tile([P, T], F32, name="v_pool0", offset=0, align_bytes=64)
-        pieces = [slice(0, 768), slice(768, 1536), slice(1536, T)]
-        for cols in pieces:
+        load_queries(1)
+        for cols in pieces[1:]:
             nc.sync.dma_start(v_pool0[:, cols], vT[0:P, cols])
-        v_pool1 = late.tile([P, T], F32, name="v_pool1", offset=0, align_bytes=64)
+        v_pool1 = sb("v_pool1", [P, T], F32)
         nc.sync.dma_start(v_pool1[:], vT[P : 2 * P, :])
-        warm = sb("warm", [P, 1], F32)
-        nc.scalar.activation(warm[:], seed[:], ACT.Exp)
 
-        def quantize(name, values, offset=None):
-            width = values.shape[1] // PACK
-            if offset is None:
-                codes = sb(name + "_codes", [P, width], U32)
-            else:
-                codes = late.tile([P, width], U32, name=name + "_codes", offset=offset, align_bytes=64)
-            scales = sb(name + "_scales", [P, width], U8)
+        def quantize(name, values, codes):
+            scales = sb(name + "_scales", [P, P], U8)
             nc.vector.quantize_mx(out=codes[:].bitcast(FP8X4), scales=scales[:], in_=values)
             return codes, scales
 
+        def own_codes(name, tag=None):
+            return sb(name + "_codes", [P, P], U32, tag)
+
+        def multiply(acc, stationary, moving):
+            nc.tensor.matmul_mx(
+                out=acc,
+                lhsT=stationary[0][:].bitcast(FP8X4),
+                lhsT_scale=stationary[1][:],
+                rhs=moving[0].bitcast(FP8X4),
+                rhs_scale=moving[1],
+                start=True,
+                stop=True,
+            )
+
+        def quantize_queries(b, tag):
+            q_bf = sb("q_bf%d" % b, [P, NQ, PACK], BF16)
+            nc.scalar.copy(q_bf[:], q_raw[b][:].rearrange("p j q -> p q j"))
+            return quantize("q%d" % b, q_bf[:].rearrange("p q j -> p (q j)"), own_codes("q%d" % b, tag))
+
         ks_got = sb("ks_got", [P, B * N], U8)
         nc.vector.tensor_copy(ks_got[:], ks_pool[:].bitcast(U8).indirect(offsets[:]))
-        q_bf = sb("q_bf", [P, B, NQ, PACK], BF16)
-        nc.scalar.copy(q_bf[:], q_raw[:].rearrange("p b j q -> p b q j"))
-        q_codes = sb("q_codes", [P, B * NQ], U32, "ks_pool")
-        q_scales = sb("q_scales", [P, B * NQ], U8)
-        nc.vector.quantize_mx(
-            out=q_codes[:].bitcast(FP8X4), scales=q_scales[:], in_=q_bf[:].rearrange("p b q j -> p (b q j)")
-        )
         vs_got = sb("vs_got", [P, B * N], F32)
         nc.vector.tensor_copy(vs_got[:], vs_pool[:].indirect(offsets[:]))
+        q = [quantize_queries(0, "vs_pool")]
 
-        kw_both = sb("kw_both", [P, B * N], U32, "scale_pool")
+        v_pool_bf = sb("v_pool_bf", [P, T], BF16)
+
+        def round_values(cols):
+            nc.scalar.activation(v_pool_bf[:, cols], v_pool0[:, cols], ACT.Copy)
+
+        round_values(pieces[0])
+
+        kw_both = sb("kw_both", [P, B * N], U32)
         kw_got = [kw_both[:, b * N : (b + 1) * N] for b in range(B)]
         for b in range(B):
             nc.vector.tensor_copy(kw_got[b], kw_pool[:].indirect(listed(b)))
+
+        q.append(quantize_queries(1, None))
 
         vs_col = [sb("vs_col%d" % b, [P, PACK], F32) for b in range(B)]
         for b in range(B):
             nc.sync.dma_start(vs_col[b][:], vs_got[0:1, b * N : (b + 1) * N].rearrange("o (s t) -> o s t", t=PACK))
 
-        neg = sb("neg", [P, B, N + 16], F32)
+        neg = sb("neg", [P, B, N + LINE], F32)
         sink_turned = bank(2, "sink_turned")
         nc.tensor.transpose(sink_turned[:, 0:P], sink_rows[:], ident[:])
         nc.scalar.activation(neg[:, :, N], sink_turned[:, 0:B], ACT.Copy, scale=-1.0)
 
-        v_pool_bf = sb("v_pool_bf", [P, T], BF16)
-        for cols in pieces:
-            nc.scalar.activation(v_pool_bf[:, cols], v_pool0[:, cols], ACT.Copy)
+        for cols in pieces[1:]:
+            round_values(cols)
 
         def gather_values(h, b):
             got = sb("v_got%d%d" % (h, b), [P, N], BF16)
@@ -122,11 +142,11 @@ def tile_attend_sink_kernel(tc, qT, k_words, k_scales, vT, vs, sink, offs, out):
                 nc.vector.tensor_copy(got[:], v_pool1[:].indirect(listed(b)))
             return got
 
-        v_bf = [[sb("v_bf%d%d" % (h, b), [P, N], BF16) for b in range(B)] for h in range(BLOCKS)]
+        v_bf = [[sb("v_bf%d%d" % (h, b), [P, N], BF16) for b in range(B)] for h in range(HALVES)]
 
-        def turn_values(h, b, got, index):
+        def turn_values(h, b, got, bank_index):
             words = got[:].bitcast(F32)
-            turned = bank(index, "v_turned%d%d" % (h, b))
+            turned = bank(bank_index, "v_turned%d%d" % (h, b))
             for u in range(2):
                 nc.tensor.transpose(turned[:, u * P : (u + 1) * P], words[:, u : 2 * P : 2], ident[:])
             nc.scalar.copy(
@@ -139,21 +159,13 @@ def tile_attend_sink_kernel(tc, qT, k_words, k_scales, vT, vs, sink, offs, out):
         scores = []
         for b in range(B):
             acc = bank(b, "scores%d" % b)
-            nc.tensor.matmul_mx(
-                out=acc[:],
-                lhsT=q_codes[:, b * NQ : (b + 1) * NQ].bitcast(FP8X4),
-                lhsT_scale=q_scales[:, b * NQ : (b + 1) * NQ],
-                rhs=kw_got[b].bitcast(FP8X4),
-                rhs_scale=ks_got[:, b * N : (b + 1) * N],
-                start=True,
-                stop=True,
-            )
+            multiply(acc[:], q[b], (kw_got[b], ks_got[:, b * N : (b + 1) * N]))
             scores.append(acc)
 
         total = sb("total", [P, B], F32)
         p_turned = []
         for b in range(B):
-            neg_max = sb("neg_max%d" % b, [P, 1], F32)
+            neg_max = sb("neg_max%d" % b, [P, 1], F32, "q_raw1" if b == 0 else None)
             nc.vector.tensor_scalar(
                 neg[:, b, 0:N].rearrange("p (t s) -> p t s", t=PACK),
                 scores[b][:].rearrange("p (s t) -> p t s", t=PACK),
@@ -163,7 +175,7 @@ def tile_attend_sink_kernel(tc, qT, k_words, k_scales, vT, vs, sink, offs, out):
                 ALU.min,
                 accum_out=neg_max[:],
             )
-            p = early.tile([P, N + 1], F32, name="p%d" % b, offset=4 * T // B * b, align_bytes=64)
+            p = half0_bytes.tile([P, N + 1], F32, name="p%d" % b, offset=4 * T // B * b, align_bytes=64)
             nc.scalar.activation(
                 p[:], neg[:, b, 0 : N + 1], ACT.Exp, bias=neg_max[:], scale=-1.0, accum_out=total[:, b : b + 1]
             )
@@ -178,7 +190,7 @@ def tile_attend_sink_kernel(tc, qT, k_words, k_scales, vT, vs, sink, offs, out):
         turn_values(1, 1, gather_values(1, 1), 3)
         turn_values(0, 1, got01, 2)
 
-        w_bf = late.tile([P, B, NQ * PACK], BF16, name="w_bf", offset=0, align_bytes=64)
+        w_bf = sb("w_bf", [P, B, NQ * PACK], BF16)
 
         def weigh(b):
             nc.vector.tensor_tensor(
@@ -188,40 +200,34 @@ def tile_attend_sink_kernel(tc, qT, k_words, k_scales, vT, vs, sink, offs, out):
                 ALU.mult,
             )
 
+        def quantize_values(h, b, codes):
+            codes, scales = quantize("v%d%d" % (h, b), v_bf[h][b][:], codes)
+            return codes[:], scales[:]
+
         inverse = sb("inverse", [P, B], F32)
 
-        def multiply(acc, w, v):
-            nc.tensor.matmul_mx(
-                out=acc,
-                lhsT=w[0][:].bitcast(FP8X4),
-                lhsT_scale=w[1][:],
-                rhs=v[0][:].bitcast(FP8X4),
-                rhs_scale=v[1][:],
-                start=True,
-                stop=True,
-            )
-
         weigh(0)
-        v00 = quantize("v00", v_bf[0][0][:], 2048)
         weigh(1)
-        w0 = quantize("w0", w_bf[:, 0, :])
-        v10 = quantize("v10", v_bf[1][0][:])
+        v00 = quantize_values(0, 0, own_codes("v00", "vs_col0"))
+        w0 = quantize("w0", w_bf[:, 0, :], own_codes("w0"))
+        v10 = quantize_values(1, 0, own_codes("v10"))
         nc.vector.reciprocal(inverse[:], total[:])
-        w1 = quantize("w1", w_bf[:, 1, :])
-        v11 = quantize("v11", v_bf[1][1][:])
-        v01 = quantize("v01", v_bf[0][1][:])
+        w1 = quantize("w1", w_bf[:, 1, :], own_codes("w1"))
+        v11 = quantize_values(1, 1, own_codes("v11"))
+        v01 = quantize_values(0, 1, own_codes("v01"))
 
-        acc0 = bank(0, "y0")
-        multiply(acc0[:, 0:P], w0, v00)
-        multiply(acc0[:, P:DV], w0, v10)
-        y0 = sb("y_out0", [P, DV], F32)
-        nc.scalar.activation(y0[:], acc0[:, 0:DV], ACT.Copy, scale=inverse[:, 0:1])
+        y0_sums = bank(0, "y0_sums")
+        multiply(y0_sums[:, 0:P], w0, v00)
+        multiply(y0_sums[:, P:DV], w0, v10)
+        y0 = sb("y0", [P, DV], F32)
+        nc.scalar.activation(y0[:], y0_sums[:, 0:DV], ACT.Copy, scale=inverse[:, 0:1])
         nc.sync.dma_start(out[0], y0[:])
-        acc1 = [bank(1, "y01"), bank(7, "y11")]
-        multiply(acc1[1][:, 0:P], w1, v11)
-        multiply(acc1[0][:, 0:P], w1, v01)
-        y1 = [sb("y_out%d1" % h, [P, P], F32) for h in range(BLOCKS)]
-        nc.scalar.activation(y1[1][:], acc1[1][:, 0:P], ACT.Copy, scale=inverse[:, 1:2])
+
+        y1_sums = [bank(1, "y1_sums0"), bank(7, "y1_sums1")]
+        multiply(y1_sums[1][:, 0:P], w1, v11)
+        multiply(y1_sums[0][:, 0:P], w1, v01)
+        y1 = [sb("y1_half%d" % h, [P, P], F32) for h in range(HALVES)]
+        nc.scalar.activation(y1[1][:], y1_sums[1][:, 0:P], ACT.Copy, scale=inverse[:, 1:2])
         nc.scalar.dma_start(out[1][:, P:DV], y1[1][:])
-        nc.vector.tensor_scalar(y1[0][:], acc1[0][:, 0:P], inverse[:, 1:2], None, ALU.mult)
+        nc.vector.tensor_scalar(y1[0][:], y1_sums[0][:, 0:P], inverse[:, 1:2], None, ALU.mult)
         nc.sync.dma_start(out[1][:, 0:P], y1[0][:])

@@ -50,8 +50,11 @@ def tile_attend_sink_kernel(tc, qT, k_words, k_scales, vT, vs, sink, offs, out):
         nc.vector.memset(ks_pool[:], 0)
         nc.vector.memset(sink_rows[:], 0.0)
         nc.vector.memset(vs_pool[:].bitcast(I32), 0)
+        ks_plane = sb("ks_plane", [P, B * N // 4], I32)
+        nc.vector.memset(ks_plane[:], 0)
         ident = sb("ident", [P, P], F32)
-        make_identity(nc, ident[:])
+        nc.vector.memset(ident[:], 0.0)
+        make_identity(nc, ident[:], nomemset=True)
 
         q_raw = [sb("q_raw%d" % b, [P, PACK, NQ], F32) for b in range(B)]
 
@@ -62,17 +65,19 @@ def tile_attend_sink_kernel(tc, qT, k_words, k_scales, vT, vs, sink, offs, out):
 
         load_queries(0)
         ks_rows = k_scales[0].bitcast(I32)
-        for r in range(4):
-            queue = nc.sync if r < 2 else nc.scalar
-            queue.dma_start(ks_pool[r:P:32, :], ks_rows[r:16:4, :])
+        nc.sync.dma_start(ks_pool[0:P:8, :], ks_rows)
         nc.sync.dma_start(sink_rows[0:B, :], sink.rearrange("b q o -> b (q o)"))
         v_pool0 = half0_bytes.tile([P, T], F32, name="v_pool0", offset=0, align_bytes=64)
         pieces = [slice(lo, hi) for lo, hi in zip(CUTS, CUTS[1:])]
         nc.sync.dma_start(v_pool0[:, pieces[0]], vT[0:P, pieces[0]])
-        nc.sync.dma_start(vs_pool[0:1, :], vs[0:1, :])
+        nc.sync.dma_start(vs_pool[4:5, :], vs[0:1, :])
         kw_pool = sb("kw_pool", [P, T], U32)
         nc.sync.dma_start(kw_pool[:].bitcast(I32), k_words[0].rearrange("p n r -> p (n r)").bitcast(I32))
         load_queries(1)
+        ks_got = sb("ks_got", [P, B * N], U8)
+        nc.vector.tensor_copy(ks_got[:], ks_pool[:].bitcast(U8).indirect(offsets[:]))
+        for r in range(4):
+            nc.sync.dma_start(ks_plane[r:P:32, :], ks_got[:].bitcast(I32)[8 * r : P : 32, :])
         for cols in pieces[1:]:
             nc.sync.dma_start(v_pool0[:, cols], vT[0:P, cols])
         v_pool1 = sb("v_pool1", [P, T], F32)
@@ -102,8 +107,6 @@ def tile_attend_sink_kernel(tc, qT, k_words, k_scales, vT, vs, sink, offs, out):
             nc.scalar.copy(q_bf[:], q_raw[b][:].rearrange("p j q -> p q j"))
             return quantize("q%d" % b, q_bf[:].rearrange("p q j -> p (q j)"), own_codes("q%d" % b, tag))
 
-        ks_got = sb("ks_got", [P, B * N], U8)
-        nc.vector.tensor_copy(ks_got[:], ks_pool[:].bitcast(U8).indirect(offsets[:]))
         vs_got = sb("vs_got", [P, B * N], F32)
         nc.vector.tensor_copy(vs_got[:], vs_pool[:].indirect(offsets[:]))
         q = [quantize_queries(0, "vs_pool")]
@@ -124,7 +127,7 @@ def tile_attend_sink_kernel(tc, qT, k_words, k_scales, vT, vs, sink, offs, out):
 
         vs_col = [sb("vs_col%d" % b, [P, PACK], F32) for b in range(B)]
         for b in range(B):
-            nc.sync.dma_start(vs_col[b][:], vs_got[0:1, b * N : (b + 1) * N].rearrange("o (s t) -> o s t", t=PACK))
+            nc.sync.dma_start(vs_col[b][:], vs_got[4:5, b * N : (b + 1) * N].rearrange("o (s t) -> o s t", t=PACK))
 
         neg = sb("neg", [P, B, N + LINE], F32)
         sink_turned = bank(2, "sink_turned")
@@ -159,7 +162,7 @@ def tile_attend_sink_kernel(tc, qT, k_words, k_scales, vT, vs, sink, offs, out):
         scores = []
         for b in range(B):
             acc = bank(b, "scores%d" % b)
-            multiply(acc[:], q[b], (kw_got[b], ks_got[:, b * N : (b + 1) * N]))
+            multiply(acc[:], q[b], (kw_got[b], ks_plane[:].bitcast(U8)[:, b * N : (b + 1) * N]))
             scores.append(acc)
 
         total = sb("total", [P, B], F32)

@@ -22,7 +22,7 @@ LIST_COLS = N // 16
 HALVES = DV // P
 BANK = 512
 LINE = 16
-CUTS = (0, 1280, 1792, T)
+CUTS = (0, 768, 1408, T)
 
 
 def tile_attend_sink_kernel(tc, qT, k_words, k_scales, vT, vs, sink, offs, out):
@@ -39,7 +39,6 @@ def tile_attend_sink_kernel(tc, qT, k_words, k_scales, vT, vs, sink, offs, out):
             return psum.tile([P, BANK], F32, name=name, tag="bank%d" % index)
 
         offsets = held.tile([P, B * LIST_COLS], U16, name="offsets")
-        nc.sync.dma_start(offsets[:], offs)
 
         def listed(b):
             return offsets[:, b * LIST_COLS : (b + 1) * LIST_COLS]
@@ -64,8 +63,10 @@ def tile_attend_sink_kernel(tc, qT, k_words, k_scales, vT, vs, sink, offs, out):
             )
 
         load_queries(0)
+        nc.sync.dma_start(offsets[:], offs)
         ks_rows = k_scales[0].bitcast(I32)
         nc.sync.dma_start(ks_pool[0:P:8, :], ks_rows)
+        load_queries(1)
         nc.sync.dma_start(sink_rows[0:B, :], sink.rearrange("b q o -> b (q o)"))
         v_pool0 = half0_bytes.tile([P, T], F32, name="v_pool0", offset=0, align_bytes=64)
         pieces = [slice(lo, hi) for lo, hi in zip(CUTS, CUTS[1:])]
@@ -73,7 +74,6 @@ def tile_attend_sink_kernel(tc, qT, k_words, k_scales, vT, vs, sink, offs, out):
         nc.sync.dma_start(vs_pool[4:5, :], vs[0:1, :])
         kw_pool = sb("kw_pool", [P, T], U32)
         nc.sync.dma_start(kw_pool[:].bitcast(I32), k_words[0].rearrange("p n r -> p (n r)").bitcast(I32))
-        load_queries(1)
         ks_got = sb("ks_got", [P, B * N], U8)
         nc.vector.tensor_copy(ks_got[:], ks_pool[:].bitcast(U8).indirect(offsets[:]))
         for r in range(4):
@@ -86,7 +86,7 @@ def tile_attend_sink_kernel(tc, qT, k_words, k_scales, vT, vs, sink, offs, out):
         def quantize(name, values, codes):
             scales = sb(name + "_scales", [P, P], U8)
             nc.vector.quantize_mx(out=codes[:].bitcast(FP8X4), scales=scales[:], in_=values)
-            return codes, scales
+            return codes[:], scales[:]
 
         def own_codes(name, tag=None):
             return sb(name + "_codes", [P, P], U32, tag)
@@ -94,22 +94,29 @@ def tile_attend_sink_kernel(tc, qT, k_words, k_scales, vT, vs, sink, offs, out):
         def multiply(acc, stationary, moving):
             nc.tensor.matmul_mx(
                 out=acc,
-                lhsT=stationary[0][:].bitcast(FP8X4),
-                lhsT_scale=stationary[1][:],
+                lhsT=stationary[0].bitcast(FP8X4),
+                lhsT_scale=stationary[1],
                 rhs=moving[0].bitcast(FP8X4),
                 rhs_scale=moving[1],
                 start=True,
                 stop=True,
             )
 
-        def quantize_queries(b, tag):
-            q_bf = sb("q_bf%d" % b, [P, NQ, PACK], BF16)
-            nc.scalar.copy(q_bf[:], q_raw[b][:].rearrange("p j q -> p q j"))
-            return quantize("q%d" % b, q_bf[:].rearrange("p q j -> p (q j)"), own_codes("q%d" % b, tag))
+        q_bf = sb("q_bf", [P, B, NQ, PACK], BF16)
+        for b in range(B):
+            nc.scalar.copy(
+                q_bf[:, b].rearrange("p (c i) j -> p c j i", i=PACK),
+                q_raw[b][:].rearrange("p j (c i) -> p c j i", i=PACK),
+            )
+        q_codes = sb("q_codes", [P, B * NQ], U32)
+        q_scales = sb("q_scales", [P, B * NQ], U8)
+        nc.vector.quantize_mx(
+            out=q_codes[:].bitcast(FP8X4), scales=q_scales[:], in_=q_bf[:].rearrange("p b q j -> p (b q j)")
+        )
+        q = [(q_codes[:, b * NQ : (b + 1) * NQ], q_scales[:, b * NQ : (b + 1) * NQ]) for b in range(B)]
 
         vs_got = sb("vs_got", [P, B * N], F32)
         nc.vector.tensor_copy(vs_got[:], vs_pool[:].indirect(offsets[:]))
-        q = [quantize_queries(0, "vs_pool")]
 
         v_pool_bf = sb("v_pool_bf", [P, T], BF16)
 
@@ -122,8 +129,6 @@ def tile_attend_sink_kernel(tc, qT, k_words, k_scales, vT, vs, sink, offs, out):
         kw_got = [kw_both[:, b * N : (b + 1) * N] for b in range(B)]
         for b in range(B):
             nc.vector.tensor_copy(kw_got[b], kw_pool[:].indirect(listed(b)))
-
-        q.append(quantize_queries(1, None))
 
         vs_col = [sb("vs_col%d" % b, [P, PACK], F32) for b in range(B)]
         for b in range(B):
@@ -168,7 +173,7 @@ def tile_attend_sink_kernel(tc, qT, k_words, k_scales, vT, vs, sink, offs, out):
         total = sb("total", [P, B], F32)
         p_turned = []
         for b in range(B):
-            neg_max = sb("neg_max%d" % b, [P, 1], F32, "q_raw1" if b == 0 else None)
+            neg_max = sb("neg_max%d" % b, [P, 1], F32)
             nc.vector.tensor_scalar(
                 neg[:, b, 0:N].rearrange("p (t s) -> p t s", t=PACK),
                 scores[b][:].rearrange("p (s t) -> p t s", t=PACK),
@@ -204,8 +209,7 @@ def tile_attend_sink_kernel(tc, qT, k_words, k_scales, vT, vs, sink, offs, out):
             )
 
         def quantize_values(h, b, codes):
-            codes, scales = quantize("v%d%d" % (h, b), v_bf[h][b][:], codes)
-            return codes[:], scales[:]
+            return quantize("v%d%d" % (h, b), v_bf[h][b][:], codes)
 
         inverse = sb("inverse", [P, B], F32)
 

@@ -19,10 +19,11 @@ ACT = mybir.ActivationFunctionType
 P = 128
 PACK = 4
 LIST_COLS = N // 16
-HALVES = DV // P
 BANK = 512
 LINE = 16
-CUTS = (0, 768, 1408, T)
+QUADRANT = 32
+KS_ROW, KS_STEP, VS_ROW = 4, 8, 8
+CUTS = (0, 512, 1152, 1664, T)
 
 
 def tile_attend_sink_kernel(tc, qT, k_words, k_scales, vT, vs, sink, offs, out):
@@ -65,31 +66,32 @@ def tile_attend_sink_kernel(tc, qT, k_words, k_scales, vT, vs, sink, offs, out):
         load_queries(0)
         nc.sync.dma_start(offsets[:], offs)
         ks_rows = k_scales[0].bitcast(I32)
-        nc.sync.dma_start(ks_pool[0:P:8, :], ks_rows)
+        nc.sync.dma_start(ks_pool[KS_ROW:P:KS_STEP, :], ks_rows)
         load_queries(1)
         nc.sync.dma_start(sink_rows[0:B, :], sink.rearrange("b q o -> b (q o)"))
         v_pool0 = half0_bytes.tile([P, T], F32, name="v_pool0", offset=0, align_bytes=64)
         pieces = [slice(lo, hi) for lo, hi in zip(CUTS, CUTS[1:])]
         nc.sync.dma_start(v_pool0[:, pieces[0]], vT[0:P, pieces[0]])
-        nc.sync.dma_start(vs_pool[4:5, :], vs[0:1, :])
+        nc.sync.dma_start(vs_pool[VS_ROW : VS_ROW + 1, :], vs[0:1, :])
         kw_pool = sb("kw_pool", [P, T], U32)
         nc.sync.dma_start(kw_pool[:].bitcast(I32), k_words[0].rearrange("p n r -> p (n r)").bitcast(I32))
+        nc.sync.dma_start(v_pool0[:, pieces[1]], vT[0:P, pieces[1]])
         ks_got = sb("ks_got", [P, B * N], U8)
         nc.vector.tensor_copy(ks_got[:], ks_pool[:].bitcast(U8).indirect(offsets[:]))
         for r in range(4):
-            nc.sync.dma_start(ks_plane[r:P:32, :], ks_got[:].bitcast(I32)[8 * r : P : 32, :])
-        for cols in pieces[1:]:
+            nc.sync.dma_start(
+                ks_plane[r:P:QUADRANT, :], ks_got[:].bitcast(I32)[KS_ROW + KS_STEP * r : P : QUADRANT, :]
+            )
+        for cols in pieces[2:]:
             nc.sync.dma_start(v_pool0[:, cols], vT[0:P, cols])
         v_pool1 = sb("v_pool1", [P, T], F32)
         nc.sync.dma_start(v_pool1[:], vT[P : 2 * P, :])
 
-        def quantize(name, values, codes):
+        def quantize(name, values, tag=None):
+            codes = sb(name + "_codes", [P, P], U32, tag)
             scales = sb(name + "_scales", [P, P], U8)
             nc.vector.quantize_mx(out=codes[:].bitcast(FP8X4), scales=scales[:], in_=values)
             return codes[:], scales[:]
-
-        def own_codes(name, tag=None):
-            return sb(name + "_codes", [P, P], U32, tag)
 
         def multiply(acc, stationary, moving):
             nc.tensor.matmul_mx(
@@ -132,7 +134,10 @@ def tile_attend_sink_kernel(tc, qT, k_words, k_scales, vT, vs, sink, offs, out):
 
         vs_col = [sb("vs_col%d" % b, [P, PACK], F32) for b in range(B)]
         for b in range(B):
-            nc.sync.dma_start(vs_col[b][:], vs_got[4:5, b * N : (b + 1) * N].rearrange("o (s t) -> o s t", t=PACK))
+            nc.sync.dma_start(
+                vs_col[b][:],
+                vs_got[VS_ROW : VS_ROW + 1, b * N : (b + 1) * N].rearrange("o (s t) -> o s t", t=PACK),
+            )
 
         neg = sb("neg", [P, B, N + LINE], F32)
         sink_turned = bank(2, "sink_turned")
@@ -141,28 +146,6 @@ def tile_attend_sink_kernel(tc, qT, k_words, k_scales, vT, vs, sink, offs, out):
 
         for cols in pieces[1:]:
             round_values(cols)
-
-        def gather_values(h, b):
-            got = sb("v_got%d%d" % (h, b), [P, N], BF16)
-            if h == 0:
-                nc.scalar.activation(got[:], v_pool_bf[:].indirect(listed(b)), ACT.Copy)
-            else:
-                nc.vector.tensor_copy(got[:], v_pool1[:].indirect(listed(b)))
-            return got
-
-        v_bf = [[sb("v_bf%d%d" % (h, b), [P, N], BF16) for b in range(B)] for h in range(HALVES)]
-
-        def turn_values(h, b, got, bank_index):
-            words = got[:].bitcast(F32)
-            turned = bank(bank_index, "v_turned%d%d" % (h, b))
-            for u in range(2):
-                nc.tensor.transpose(turned[:, u * P : (u + 1) * P], words[:, u : 2 * P : 2], ident[:])
-            nc.scalar.copy(
-                v_bf[h][b][:].bitcast(F32).rearrange("s (e u) -> s e u", u=2),
-                turned[:, 0 : 2 * P].rearrange("s (u e) -> s e u", u=2),
-            )
-
-        got00 = gather_values(0, 0)
 
         scores = []
         for b in range(B):
@@ -192,49 +175,71 @@ def tile_attend_sink_kernel(tc, qT, k_words, k_scales, vT, vs, sink, offs, out):
                 nc.tensor.transpose(turned[:, t * P : (t + 1) * P], p[:, t * P : (t + 1) * P], ident[:])
             p_turned.append(turned)
 
-        got01 = gather_values(0, 1)
-        turn_values(0, 0, got00, 6)
-        turn_values(1, 0, gather_values(1, 0), 2)
-        turn_values(1, 1, gather_values(1, 1), 3)
-        turn_values(0, 1, got01, 2)
+        got01 = sb("v_got01", [P, N], BF16, "neg_max0")
+        nc.vector.tensor_copy(got01[:], v_pool_bf[:].indirect(listed(1)))
+        got00 = sb("v_got00", [P, N], BF16)
+        nc.scalar.activation(got00[:], v_pool_bf[:].indirect(listed(0)), ACT.Copy)
 
-        w_bf = sb("w_bf", [P, B, NQ * PACK], BF16)
-
-        def weigh(b):
-            nc.vector.tensor_tensor(
-                w_bf[:, b, :].rearrange("s (q t) -> s q t", t=PACK),
-                p_turned[b][:].rearrange("s (t q) -> s q t", t=PACK),
-                vs_col[b][:].unsqueeze(1).to_broadcast([P, NQ, PACK]),
-                ALU.mult,
+        w0_planes = sb("w0_planes", [P, PACK, NQ], BF16)
+        for t in range(PACK):
+            nc.scalar.activation(
+                w0_planes[:, t, :], p_turned[0][:, t * P : (t + 1) * P], ACT.Copy, scale=vs_col[0][:, t : t + 1]
             )
 
-        def quantize_values(h, b, codes):
-            return quantize("v%d%d" % (h, b), v_bf[h][b][:], codes)
+        def gather_half1(b):
+            got = sb("v_got1%d" % b, [P, N], BF16)
+            nc.vector.tensor_copy(got[:], v_pool1[:].indirect(listed(b)))
+            return got
 
+        v_bf = [[sb("v_bf%d%d" % (h, b), [P, N], BF16) for b in range(B)] for h in range(DV // P)]
+
+        def turn_values(h, b, got, bank_index):
+            words = got[:].bitcast(F32)
+            turned = bank(bank_index, "v_turned%d%d" % (h, b))
+            for u in range(2):
+                nc.tensor.transpose(turned[:, u * P : (u + 1) * P], words[:, u : 2 * P : 2], ident[:])
+            nc.scalar.copy(
+                v_bf[h][b][:].bitcast(F32).rearrange("s (e u) -> s e u", u=2),
+                turned[:, 0 : 2 * P].rearrange("s (u e) -> s e u", u=2),
+            )
+
+        turn_values(0, 1, got01, 7)
+        turn_values(0, 0, got00, 6)
+        turn_values(1, 0, gather_half1(0), 2)
+        turn_values(1, 1, gather_half1(1), 3)
+
+        w_bf = sb("w_bf", [P, B, NQ * PACK], BF16)
         inverse = sb("inverse", [P, B], F32)
+        nc.vector.tensor_tensor(
+            w_bf[:, 1, :].rearrange("s (q t) -> s q t", t=PACK),
+            p_turned[1][:].rearrange("s (t q) -> s q t", t=PACK),
+            vs_col[1][:].unsqueeze(1).to_broadcast([P, NQ, PACK]),
+            ALU.mult,
+        )
+        nc.vector.tensor_copy(
+            w_bf[:, 0, :].rearrange("s (c i t) -> s c t i", i=PACK, t=PACK),
+            w0_planes[:].rearrange("s t (c i) -> s c t i", i=PACK),
+        )
 
-        weigh(0)
-        weigh(1)
-        v00 = quantize_values(0, 0, own_codes("v00", "vs_col0"))
-        w0 = quantize("w0", w_bf[:, 0, :], own_codes("w0"))
-        v10 = quantize_values(1, 0, own_codes("v10"))
+        w1 = quantize("w1", w_bf[:, 1, :])
+        v01 = quantize("v01", v_bf[0][1][:], "vs_col1")
+        w0 = quantize("w0", w_bf[:, 0, :])
+        v00 = quantize("v00", v_bf[0][0][:], "vs_col0")
         nc.vector.reciprocal(inverse[:], total[:])
-        w1 = quantize("w1", w_bf[:, 1, :], own_codes("w1"))
-        v11 = quantize_values(1, 1, own_codes("v11"))
-        v01 = quantize_values(0, 1, own_codes("v01"))
+        v10 = quantize("v10", v_bf[1][0][:])
+        v11 = quantize("v11", v_bf[1][1][:])
 
-        y0_sums = bank(0, "y0_sums")
-        multiply(y0_sums[:, 0:P], w0, v00)
-        multiply(y0_sums[:, P:DV], w0, v10)
-        y0 = sb("y0", [P, DV], F32)
-        nc.scalar.activation(y0[:], y0_sums[:, 0:DV], ACT.Copy, scale=inverse[:, 0:1])
-        nc.sync.dma_start(out[0], y0[:])
+        def finish(b, h, w, v, bank_index, on_vector, queue):
+            sums = bank(bank_index, "y_sums%d%d" % (b, h))
+            multiply(sums[:, 0:P], w, v)
+            y = sb("y%d%d" % (b, h), [P, P], F32)
+            if on_vector:
+                nc.vector.tensor_scalar(y[:], sums[:, 0:P], inverse[:, b : b + 1], None, ALU.mult)
+            else:
+                nc.scalar.activation(y[:], sums[:, 0:P], ACT.Copy, scale=inverse[:, b : b + 1])
+            queue.dma_start(out[b][:, h * P : (h + 1) * P], y[:])
 
-        y1_sums = [bank(1, "y1_sums0"), bank(7, "y1_sums1")]
-        multiply(y1_sums[1][:, 0:P], w1, v11)
-        multiply(y1_sums[0][:, 0:P], w1, v01)
-        y1 = [sb("y1_half%d" % h, [P, P], F32) for h in range(HALVES)]
-        nc.scalar.activation(y1[1][:], y1_sums[1][:, 0:P], ACT.Copy, scale=inverse[:, 1:2])
-        nc.scalar.dma_start(out[1][:, P:DV], y1[1][:])
-        nc.vector.tensor_scalar(y1[0][:], y1_sums[0][:, 0:P], inverse[:, 1:2], None, ALU.mult)
-        nc.sync.dma_start(out[1][:, 0:P], y1[0][:])
+        finish(1, 0, w1, v01, 1, False, nc.sync)
+        finish(0, 0, w0, v00, 0, False, nc.sync)
+        finish(0, 1, w0, v10, 6, False, nc.scalar)
+        finish(1, 1, w1, v11, 7, True, nc.sync)

@@ -22,19 +22,21 @@ LIST_COLS = N // 16
 BANK = 512
 LINE = 16
 QUADRANT = 32
-KS_ROW, KS_STEP, VS_ROW = 4, 8, 8
-CUTS = (0, 512, 1152, 1664, T)
+VS_ROW = 8
 
 
 def tile_attend_sink_kernel(tc, qT, k_words, k_scales, vT, vs, sink, offs, out):
     nc = tc.nc
     with ExitStack() as ctx:
         held = ctx.enter_context(tc.tile_pool(name="held", bufs=1))
-        half0_bytes = ctx.enter_context(tc.tile_pool(name="half0_bytes", bufs=1))
+        last = ctx.enter_context(tc.tile_pool(name="last", bufs=1))
         psum = ctx.enter_context(tc.psum_pool(name="psum", bufs=1))
 
-        def sb(name, shape, dtype, tag=None):
-            return held.tile(shape, dtype, name=name, tag=tag or name, align_bytes=64)
+        def sb(name, shape, dtype):
+            return held.tile(shape, dtype, name=name, align_bytes=64)
+
+        def late(name, shape, dtype, offset):
+            return last.tile(shape, dtype, name=name, offset=offset, align_bytes=64)
 
         def bank(index, name):
             return psum.tile([P, BANK], F32, name=name, tag="bank%d" % index)
@@ -47,12 +49,10 @@ def tile_attend_sink_kernel(tc, qT, k_words, k_scales, vT, vs, sink, offs, out):
         ks_pool = sb("ks_pool", [P, T // 4], I32)
         vs_pool = sb("vs_pool", [P, T], F32)
         sink_rows = sb("sink_rows", [P, NQ], F32)
-        nc.vector.memset(ks_pool[:], 0)
-        nc.vector.memset(sink_rows[:], 0.0)
-        nc.vector.memset(vs_pool[:].bitcast(I32), 0)
-        ks_plane = sb("ks_plane", [P, B * N // 4], I32)
-        nc.vector.memset(ks_plane[:], 0)
         ident = sb("ident", [P, P], F32)
+        nc.vector.memset(ks_pool[:], 0)
+        nc.vector.memset(vs_pool[:].bitcast(I32), 0)
+        nc.vector.memset(sink_rows[:], 0.0)
         nc.vector.memset(ident[:], 0.0)
         make_identity(nc, ident[:], nomemset=True)
 
@@ -63,35 +63,21 @@ def tile_attend_sink_kernel(tc, qT, k_words, k_scales, vT, vs, sink, offs, out):
                 q_raw[b][:].rearrange("p j q -> p (j q)"), qT[b].rearrange("(p j) q -> p (j q)", j=PACK)
             )
 
-        load_queries(0)
         nc.sync.dma_start(offsets[:], offs)
+        load_queries(0)
         ks_rows = k_scales[0].bitcast(I32)
-        nc.sync.dma_start(ks_pool[KS_ROW:P:KS_STEP, :], ks_rows)
+        for r in range(4):
+            nc.sync.dma_start(ks_pool[r:P:QUADRANT, :], ks_rows[r:16:4, :])
         load_queries(1)
-        nc.sync.dma_start(sink_rows[0:B, :], sink.rearrange("b q o -> b (q o)"))
-        v_pool0 = half0_bytes.tile([P, T], F32, name="v_pool0", offset=0, align_bytes=64)
-        pieces = [slice(lo, hi) for lo, hi in zip(CUTS, CUTS[1:])]
-        nc.sync.dma_start(v_pool0[:, pieces[0]], vT[0:P, pieces[0]])
         nc.sync.dma_start(vs_pool[VS_ROW : VS_ROW + 1, :], vs[0:1, :])
+        nc.sync.dma_start(sink_rows[0:B, :], sink.rearrange("b q o -> b (q o)"))
         kw_pool = sb("kw_pool", [P, T], U32)
         nc.sync.dma_start(kw_pool[:].bitcast(I32), k_words[0].rearrange("p n r -> p (n r)").bitcast(I32))
-        nc.sync.dma_start(v_pool0[:, pieces[1]], vT[0:P, pieces[1]])
-        ks_got = sb("ks_got", [P, B * N], U8)
-        nc.vector.tensor_copy(ks_got[:], ks_pool[:].bitcast(U8).indirect(offsets[:]))
-        for r in range(4):
-            nc.sync.dma_start(
-                ks_plane[r:P:QUADRANT, :], ks_got[:].bitcast(I32)[KS_ROW + KS_STEP * r : P : QUADRANT, :]
-            )
-        for cols in pieces[2:]:
-            nc.sync.dma_start(v_pool0[:, cols], vT[0:P, cols])
-        v_pool1 = sb("v_pool1", [P, T], F32)
-        nc.sync.dma_start(v_pool1[:], vT[P : 2 * P, :])
+        v_pool0 = sb("v_pool0", [P, T], F32)
+        nc.sync.dma_start(v_pool0[:], vT[0:P, :])
 
-        def quantize(name, values, tag=None):
-            codes = sb(name + "_codes", [P, P], U32, tag)
-            scales = sb(name + "_scales", [P, P], U8)
-            nc.vector.quantize_mx(out=codes[:].bitcast(FP8X4), scales=scales[:], in_=values)
-            return codes[:], scales[:]
+        def quantize(codes, scales, values):
+            nc.vector.quantize_mx(out=codes.bitcast(FP8X4), scales=scales, in_=values)
 
         def multiply(acc, stationary, moving):
             nc.tensor.matmul_mx(
@@ -104,33 +90,22 @@ def tile_attend_sink_kernel(tc, qT, k_words, k_scales, vT, vs, sink, offs, out):
                 stop=True,
             )
 
-        q_bf = sb("q_bf", [P, B, NQ, PACK], BF16)
-        for b in range(B):
+        def prepare_queries(b):
+            q_bf = sb("q_bf%d" % b, [P, NQ, PACK], BF16)
             nc.scalar.copy(
-                q_bf[:, b].rearrange("p (c i) j -> p c j i", i=PACK),
+                q_bf[:].rearrange("p (c i) j -> p c j i", i=PACK),
                 q_raw[b][:].rearrange("p j (c i) -> p c j i", i=PACK),
             )
-        q_codes = sb("q_codes", [P, B * NQ], U32)
-        q_scales = sb("q_scales", [P, B * NQ], U8)
-        nc.vector.quantize_mx(
-            out=q_codes[:].bitcast(FP8X4), scales=q_scales[:], in_=q_bf[:].rearrange("p b q j -> p (b q j)")
-        )
-        q = [(q_codes[:, b * NQ : (b + 1) * NQ], q_scales[:, b * NQ : (b + 1) * NQ]) for b in range(B)]
+            codes = sb("q_codes%d" % b, [P, NQ], U32)
+            scales = sb("q_scales%d" % b, [P, NQ], U8)
+            quantize(codes[:], scales[:], q_bf[:].rearrange("p q j -> p (q j)"))
+            return codes[:], scales[:]
 
+        q = [prepare_queries(b) for b in range(B)]
+        ks_got = sb("ks_got", [P, B * N], U8)
+        nc.vector.tensor_copy(ks_got[:], ks_pool[:].bitcast(U8).indirect(offsets[:]))
         vs_got = sb("vs_got", [P, B * N], F32)
-        nc.vector.tensor_copy(vs_got[:], vs_pool[:].indirect(offsets[:]))
-
-        v_pool_bf = sb("v_pool_bf", [P, T], BF16)
-
-        def round_values(cols):
-            nc.scalar.activation(v_pool_bf[:, cols], v_pool0[:, cols], ACT.Copy)
-
-        round_values(pieces[0])
-
-        kw_both = sb("kw_both", [P, B * N], U32)
-        kw_got = [kw_both[:, b * N : (b + 1) * N] for b in range(B)]
-        for b in range(B):
-            nc.vector.tensor_copy(kw_got[b], kw_pool[:].indirect(listed(b)))
+        nc.scalar.activation(vs_got[:], vs_pool[:].indirect(offsets[:]), ACT.Copy)
 
         vs_col = [sb("vs_col%d" % b, [P, PACK], F32) for b in range(B)]
         for b in range(B):
@@ -138,19 +113,23 @@ def tile_attend_sink_kernel(tc, qT, k_words, k_scales, vT, vs, sink, offs, out):
                 vs_col[b][:],
                 vs_got[VS_ROW : VS_ROW + 1, b * N : (b + 1) * N].rearrange("o (s t) -> o s t", t=PACK),
             )
+        v_pool1 = late("v_pool1", [P, T], F32, 0)
+        nc.sync.dma_start(v_pool1[:], vT[P : 2 * P, :])
+
+        kw_both = sb("kw_both", [P, B * N], U32)
+        kw_got = [kw_both[:, b * N : (b + 1) * N] for b in range(B)]
+        for b in range(B):
+            nc.vector.tensor_copy(kw_got[b], kw_pool[:].indirect(listed(b)))
 
         neg = sb("neg", [P, B, N + LINE], F32)
         sink_turned = bank(2, "sink_turned")
         nc.tensor.transpose(sink_turned[:, 0:P], sink_rows[:], ident[:])
         nc.scalar.activation(neg[:, :, N], sink_turned[:, 0:B], ACT.Copy, scale=-1.0)
 
-        for cols in pieces[1:]:
-            round_values(cols)
-
         scores = []
         for b in range(B):
             acc = bank(b, "scores%d" % b)
-            multiply(acc[:], q[b], (kw_got[b], ks_plane[:].bitcast(U8)[:, b * N : (b + 1) * N]))
+            multiply(acc[:], q[b], (kw_got[b], ks_got[:, b * N : (b + 1) * N]))
             scores.append(acc)
 
         total = sb("total", [P, B], F32)
@@ -166,7 +145,7 @@ def tile_attend_sink_kernel(tc, qT, k_words, k_scales, vT, vs, sink, offs, out):
                 ALU.min,
                 accum_out=neg_max[:],
             )
-            p = half0_bytes.tile([P, N + 1], F32, name="p%d" % b, offset=4 * T // B * b, align_bytes=64)
+            p = sb("p%d" % b, [P, N + 1], F32)
             nc.scalar.activation(
                 p[:], neg[:, b, 0 : N + 1], ACT.Exp, bias=neg_max[:], scale=-1.0, accum_out=total[:, b : b + 1]
             )
@@ -175,63 +154,56 @@ def tile_attend_sink_kernel(tc, qT, k_words, k_scales, vT, vs, sink, offs, out):
                 nc.tensor.transpose(turned[:, t * P : (t + 1) * P], p[:, t * P : (t + 1) * P], ident[:])
             p_turned.append(turned)
 
-        got01 = sb("v_got01", [P, N], BF16, "neg_max0")
-        nc.vector.tensor_copy(got01[:], v_pool_bf[:].indirect(listed(1)))
-        got00 = sb("v_got00", [P, N], BF16)
-        nc.scalar.activation(got00[:], v_pool_bf[:].indirect(listed(0)), ACT.Copy)
-
-        w0_planes = sb("w0_planes", [P, PACK, NQ], BF16)
-        for t in range(PACK):
-            nc.scalar.activation(
-                w0_planes[:, t, :], p_turned[0][:, t * P : (t + 1) * P], ACT.Copy, scale=vs_col[0][:, t : t + 1]
-            )
-
-        def gather_half1(b):
-            got = sb("v_got1%d" % b, [P, N], BF16)
-            nc.vector.tensor_copy(got[:], v_pool1[:].indirect(listed(b)))
+        def gather_values(h, pool):
+            got = [sb("v_got%d%d" % (h, b), [P, N], BF16) for b in range(B)]
+            nc.vector.tensor_copy(got[1][:], pool[:].indirect(listed(1)))
+            nc.scalar.activation(got[0][:], pool[:].indirect(listed(0)), ACT.Copy)
             return got
 
-        v_bf = [[sb("v_bf%d%d" % (h, b), [P, N], BF16) for b in range(B)] for h in range(DV // P)]
-
-        def turn_values(h, b, got, bank_index):
+        def turn_values(got, v_bf, turned):
             words = got[:].bitcast(F32)
-            turned = bank(bank_index, "v_turned%d%d" % (h, b))
             for u in range(2):
                 nc.tensor.transpose(turned[:, u * P : (u + 1) * P], words[:, u : 2 * P : 2], ident[:])
             nc.scalar.copy(
-                v_bf[h][b][:].bitcast(F32).rearrange("s (e u) -> s e u", u=2),
+                v_bf.bitcast(F32).rearrange("s (e u) -> s e u", u=2),
                 turned[:, 0 : 2 * P].rearrange("s (u e) -> s e u", u=2),
             )
 
-        turn_values(0, 1, got01, 7)
-        turn_values(0, 0, got00, 6)
-        turn_values(1, 0, gather_half1(0), 2)
-        turn_values(1, 1, gather_half1(1), 3)
+        got0 = gather_values(0, v_pool0)
+        v_bf01 = sb("v_bf01", [P, N], BF16)
+        turn_values(got0[1], v_bf01[:], bank(7, "v_turned01"))
 
         w_bf = sb("w_bf", [P, B, NQ * PACK], BF16)
-        inverse = sb("inverse", [P, B], F32)
-        nc.vector.tensor_tensor(
-            w_bf[:, 1, :].rearrange("s (q t) -> s q t", t=PACK),
-            p_turned[1][:].rearrange("s (t q) -> s q t", t=PACK),
-            vs_col[1][:].unsqueeze(1).to_broadcast([P, NQ, PACK]),
-            ALU.mult,
-        )
-        nc.vector.tensor_copy(
-            w_bf[:, 0, :].rearrange("s (c i t) -> s c t i", i=PACK, t=PACK),
-            w0_planes[:].rearrange("s t (c i) -> s c t i", i=PACK),
-        )
+        for b in range(B):
+            nc.vector.tensor_tensor(
+                w_bf[:, b, :].rearrange("s (q t) -> s q t", t=PACK),
+                p_turned[b][:].rearrange("s (t q) -> s q t", t=PACK),
+                vs_col[b][:].unsqueeze(1).to_broadcast([P, NQ, PACK]),
+                ALU.mult,
+            )
 
-        w1 = quantize("w1", w_bf[:, 1, :])
-        v01 = quantize("v01", v_bf[0][1][:], "vs_col1")
-        w0 = quantize("w0", w_bf[:, 0, :])
-        v00 = quantize("v00", v_bf[0][0][:], "vs_col0")
+        got1 = gather_values(1, v_pool1)
+
+        v_bf00 = late("v_bf00", [P, N], BF16, 0)
+        turn_values(got0[0], v_bf00[:], bank(6, "v_turned00"))
+        inverse = late("inverse", [P, B], F32, 1024)
         nc.vector.reciprocal(inverse[:], total[:])
-        v10 = quantize("v10", v_bf[1][0][:])
-        v11 = quantize("v11", v_bf[1][1][:])
+        w_codes = late("w_codes", [P, B * NQ], U32, 2048)
+        w_scales = sb("w_scales", [P, B * NQ], U8)
+        quantize(w_codes[:], w_scales[:], w_bf[:].rearrange("s b c -> s (b c)"))
+        w = [(w_codes[:, b * NQ : (b + 1) * NQ], w_scales[:, b * NQ : (b + 1) * NQ]) for b in range(B)]
 
-        def finish(b, h, w, v, bank_index, on_vector, queue):
+        v_bf11 = sb("v_bf11", [P, N], BF16)
+        turn_values(got1[1], v_bf11[:], bank(3, "v_turned11"))
+        v_bf10 = sb("v_bf10", [P, N], BF16)
+        turn_values(got1[0], v_bf10[:], bank(2, "v_turned10"))
+
+        def finish(b, h, v_bf, bank_index, on_vector, queue):
+            codes = late("v_codes%d%d" % (h, b), [P, P], U32, 4096 + 512 * (2 * h + b))
+            scales = sb("v_scales%d%d" % (h, b), [P, P], U8)
+            quantize(codes[:], scales[:], v_bf[:])
             sums = bank(bank_index, "y_sums%d%d" % (b, h))
-            multiply(sums[:, 0:P], w, v)
+            multiply(sums[:, 0:P], w[b], (codes[:], scales[:]))
             y = sb("y%d%d" % (b, h), [P, P], F32)
             if on_vector:
                 nc.vector.tensor_scalar(y[:], sums[:, 0:P], inverse[:, b : b + 1], None, ALU.mult)
@@ -239,7 +211,7 @@ def tile_attend_sink_kernel(tc, qT, k_words, k_scales, vT, vs, sink, offs, out):
                 nc.scalar.activation(y[:], sums[:, 0:P], ACT.Copy, scale=inverse[:, b : b + 1])
             queue.dma_start(out[b][:, h * P : (h + 1) * P], y[:])
 
-        finish(1, 0, w1, v01, 1, False, nc.sync)
-        finish(0, 0, w0, v00, 0, False, nc.sync)
-        finish(0, 1, w0, v10, 6, False, nc.scalar)
-        finish(1, 1, w1, v11, 7, True, nc.sync)
+        finish(1, 0, v_bf01, 1, False, nc.sync)
+        finish(0, 0, v_bf00, 0, False, nc.sync)
+        finish(1, 1, v_bf11, 4, False, nc.scalar)
+        finish(0, 1, v_bf10, 5, True, nc.sync)

@@ -22,7 +22,10 @@ LIST_COLS = N // 16
 BANK = 512
 LINE = 16
 QUADRANT = 32
-VS_ROW = 8
+KS_ROW, KS_STEP, VS_ROW = 4, 8, 8
+V_AHEAD = 384
+SHARE = 128
+KEYS_AHEAD = 768
 
 
 def tile_attend_sink_kernel(tc, qT, k_words, k_scales, vT, vs, sink, offs, out):
@@ -30,10 +33,11 @@ def tile_attend_sink_kernel(tc, qT, k_words, k_scales, vT, vs, sink, offs, out):
     with ExitStack() as ctx:
         held = ctx.enter_context(tc.tile_pool(name="held", bufs=1))
         last = ctx.enter_context(tc.tile_pool(name="last", bufs=1))
+        first = ctx.enter_context(tc.tile_pool(name="first", bufs=1))
         psum = ctx.enter_context(tc.psum_pool(name="psum", bufs=1))
 
-        def sb(name, shape, dtype):
-            return held.tile(shape, dtype, name=name, align_bytes=64)
+        def sb(name, shape, dtype, tag=None):
+            return held.tile(shape, dtype, name=name, tag=tag or name, align_bytes=64)
 
         def late(name, shape, dtype, offset):
             return last.tile(shape, dtype, name=name, offset=offset, align_bytes=64)
@@ -47,12 +51,14 @@ def tile_attend_sink_kernel(tc, qT, k_words, k_scales, vT, vs, sink, offs, out):
             return offsets[:, b * LIST_COLS : (b + 1) * LIST_COLS]
 
         ks_pool = sb("ks_pool", [P, T // 4], I32)
-        vs_pool = sb("vs_pool", [P, T], F32)
+        vs_pool = late("vs_pool", [P, T], F32, 0)
         sink_rows = sb("sink_rows", [P, NQ], F32)
         ident = sb("ident", [P, P], F32)
         nc.vector.memset(ks_pool[:], 0)
-        nc.vector.memset(vs_pool[:].bitcast(I32), 0)
         nc.vector.memset(sink_rows[:], 0.0)
+        nc.vector.memset(vs_pool[:].bitcast(I32), 0)
+        ks_plane = sb("ks_plane", [P, B * N // 4], I32)
+        nc.vector.memset(ks_plane[:], 0)
         nc.vector.memset(ident[:], 0.0)
         make_identity(nc, ident[:], nomemset=True)
 
@@ -66,15 +72,23 @@ def tile_attend_sink_kernel(tc, qT, k_words, k_scales, vT, vs, sink, offs, out):
         nc.sync.dma_start(offsets[:], offs)
         load_queries(0)
         ks_rows = k_scales[0].bitcast(I32)
-        for r in range(4):
-            nc.sync.dma_start(ks_pool[r:P:QUADRANT, :], ks_rows[r:16:4, :])
-        load_queries(1)
-        nc.sync.dma_start(vs_pool[VS_ROW : VS_ROW + 1, :], vs[0:1, :])
+        nc.sync.dma_start(ks_pool[KS_ROW:P:KS_STEP, :], ks_rows)
         nc.sync.dma_start(sink_rows[0:B, :], sink.rearrange("b q o -> b (q o)"))
         kw_pool = sb("kw_pool", [P, T], U32)
-        nc.sync.dma_start(kw_pool[:].bitcast(I32), k_words[0].rearrange("p n r -> p (n r)").bitcast(I32))
+        kw_rows = k_words[0].rearrange("p n r -> p (n r)").bitcast(I32)
+        nc.sync.dma_start(kw_pool[:].bitcast(I32)[:, 0:KEYS_AHEAD], kw_rows[:, 0:KEYS_AHEAD])
+        nc.sync.dma_start(vs_pool[VS_ROW : VS_ROW + 1, :], vs[0:1, :])
+        nc.sync.dma_start(kw_pool[:].bitcast(I32)[:, KEYS_AHEAD:T], kw_rows[:, KEYS_AHEAD:T])
+        load_queries(1)
         v_pool0 = sb("v_pool0", [P, T], F32)
-        nc.sync.dma_start(v_pool0[:], vT[0:P, :])
+        nc.sync.dma_start(v_pool0[:, 0:V_AHEAD], vT[0:P, 0:V_AHEAD])
+        ks_got = sb("ks_got", [P, B * N], U8)
+        nc.vector.tensor_copy(ks_got[:], ks_pool[:].bitcast(U8).indirect(offsets[:]))
+        for r in range(4):
+            nc.sync.dma_start(
+                ks_plane[r:P:QUADRANT, :], ks_got[:].bitcast(I32)[KS_ROW + KS_STEP * r : P : QUADRANT, :]
+            )
+        nc.sync.dma_start(v_pool0[:, V_AHEAD:T], vT[0:P, V_AHEAD:T])
 
         def quantize(codes, scales, values):
             nc.vector.quantize_mx(out=codes.bitcast(FP8X4), scales=scales, in_=values)
@@ -91,7 +105,7 @@ def tile_attend_sink_kernel(tc, qT, k_words, k_scales, vT, vs, sink, offs, out):
             )
 
         def prepare_queries(b):
-            q_bf = sb("q_bf%d" % b, [P, NQ, PACK], BF16)
+            q_bf = first.tile([P, NQ, PACK], BF16, name="q_bf%d" % b, offset=2048 + 4096 * b, align_bytes=64)
             nc.scalar.copy(
                 q_bf[:].rearrange("p (c i) j -> p c j i", i=PACK),
                 q_raw[b][:].rearrange("p j (c i) -> p c j i", i=PACK),
@@ -101,35 +115,37 @@ def tile_attend_sink_kernel(tc, qT, k_words, k_scales, vT, vs, sink, offs, out):
             quantize(codes[:], scales[:], q_bf[:].rearrange("p q j -> p (q j)"))
             return codes[:], scales[:]
 
-        q = [prepare_queries(b) for b in range(B)]
-        ks_got = sb("ks_got", [P, B * N], U8)
-        nc.vector.tensor_copy(ks_got[:], ks_pool[:].bitcast(U8).indirect(offsets[:]))
-        vs_got = sb("vs_got", [P, B * N], F32)
-        nc.scalar.activation(vs_got[:], vs_pool[:].indirect(offsets[:]), ACT.Copy)
-
-        vs_col = [sb("vs_col%d" % b, [P, PACK], F32) for b in range(B)]
-        for b in range(B):
-            nc.sync.dma_start(
-                vs_col[b][:],
-                vs_got[VS_ROW : VS_ROW + 1, b * N : (b + 1) * N].rearrange("o (s t) -> o s t", t=PACK),
-            )
-        v_pool1 = late("v_pool1", [P, T], F32, 0)
-        nc.sync.dma_start(v_pool1[:], vT[P : 2 * P, :])
-
-        kw_both = sb("kw_both", [P, B * N], U32)
-        kw_got = [kw_both[:, b * N : (b + 1) * N] for b in range(B)]
-        for b in range(B):
-            nc.vector.tensor_copy(kw_got[b], kw_pool[:].indirect(listed(b)))
-
+        q = [prepare_queries(0)]
         neg = sb("neg", [P, B, N + LINE], F32)
         sink_turned = bank(2, "sink_turned")
         nc.tensor.transpose(sink_turned[:, 0:P], sink_rows[:], ident[:])
         nc.scalar.activation(neg[:, :, N], sink_turned[:, 0:B], ACT.Copy, scale=-1.0)
 
+        vs_got = [sb("vs_got%d" % b, [P, N], F32) for b in range(B)]
+        nc.vector.tensor_copy(vs_got[0][:], vs_pool[:].indirect(listed(0)))
+        nc.scalar.activation(vs_got[1][:], vs_pool[:].indirect(listed(1)), ACT.Copy)
+
+        def turn_vs(b, column, bank_index):
+            turned = bank(bank_index, "vs_turned%d" % b)
+            for t in range(PACK):
+                nc.tensor.transpose(turned[:, t * P : (t + 1) * P], vs_got[b][:, t:N:PACK], ident[:])
+            nc.scalar.copy(column, turned[:, VS_ROW:BANK:P])
+
+        v_pool1 = late("v_pool1", [P, T], F32, 0)
+        nc.sync.dma_start(v_pool1[:], vT[P : 2 * P, :])
+
+        kw_got = [first.tile([P, N], U32, name="kw_got%d" % b, offset=2560 - 2048 * b, align_bytes=64)[:] for b in range(B)]
+        for b in range(B):
+            nc.vector.tensor_copy(kw_got[b], kw_pool[:].indirect(listed(b)))
+
+        q.append(prepare_queries(1))
+        vs_col = [sb("vs_col0", [P, PACK], F32, "q_raw1"), None]
+        turn_vs(0, vs_col[0][:], 7)
+
         scores = []
         for b in range(B):
             acc = bank(b, "scores%d" % b)
-            multiply(acc[:], q[b], (kw_got[b], ks_got[:, b * N : (b + 1) * N]))
+            multiply(acc[:], q[b], (kw_got[b], ks_plane[:].bitcast(U8)[:, b * N : (b + 1) * N]))
             scores.append(acc)
 
         total = sb("total", [P, B], F32)
@@ -154,10 +170,18 @@ def tile_attend_sink_kernel(tc, qT, k_words, k_scales, vT, vs, sink, offs, out):
                 nc.tensor.transpose(turned[:, t * P : (t + 1) * P], p[:, t * P : (t + 1) * P], ident[:])
             p_turned.append(turned)
 
+        vs_col[1] = sb("vs_col1", [P, PACK], F32, "neg_max1")
+        turn_vs(1, vs_col[1][:], 0)
+
         def gather_values(h, pool):
-            got = [sb("v_got%d%d" % (h, b), [P, N], BF16) for b in range(B)]
+            got = [sb("v_got%d0" % h, [P, N], BF16, None if h else "neg"), sb("v_got%d1" % h, [P, N], BF16)]
             nc.vector.tensor_copy(got[1][:], pool[:].indirect(listed(1)))
-            nc.scalar.activation(got[0][:], pool[:].indirect(listed(0)), ACT.Copy)
+            if h == 0:
+                nc.scalar.activation(got[0][:], pool[:].indirect(listed(0)), ACT.Copy)
+            else:
+                cut = (N - SHARE) // 16
+                nc.scalar.activation(got[0][:, N - SHARE : N], pool[:].indirect(listed(0)[:, cut:]), ACT.Copy)
+                nc.vector.tensor_copy(got[0][:, 0 : N - SHARE], pool[:].indirect(listed(0)[:, 0:cut]))
             return got
 
         def turn_values(got, v_bf, turned):
@@ -171,8 +195,6 @@ def tile_attend_sink_kernel(tc, qT, k_words, k_scales, vT, vs, sink, offs, out):
 
         got0 = gather_values(0, v_pool0)
         v_bf01 = sb("v_bf01", [P, N], BF16)
-        turn_values(got0[1], v_bf01[:], bank(7, "v_turned01"))
-
         w_bf = sb("w_bf", [P, B, NQ * PACK], BF16)
         for b in range(B):
             nc.vector.tensor_tensor(
@@ -182,6 +204,7 @@ def tile_attend_sink_kernel(tc, qT, k_words, k_scales, vT, vs, sink, offs, out):
                 ALU.mult,
             )
 
+        turn_values(got0[1], v_bf01[:], bank(4, "v_turned01"))
         got1 = gather_values(1, v_pool1)
 
         v_bf00 = late("v_bf00", [P, N], BF16, 0)
@@ -212,6 +235,6 @@ def tile_attend_sink_kernel(tc, qT, k_words, k_scales, vT, vs, sink, offs, out):
             queue.dma_start(out[b][:, h * P : (h + 1) * P], y[:])
 
         finish(1, 0, v_bf01, 1, False, nc.sync)
-        finish(0, 0, v_bf00, 0, False, nc.sync)
-        finish(1, 1, v_bf11, 4, False, nc.scalar)
+        finish(0, 0, v_bf00, 4, False, nc.sync)
+        finish(1, 1, v_bf11, 7, False, nc.scalar)
         finish(0, 1, v_bf10, 5, True, nc.sync)

@@ -23,7 +23,7 @@ BANK = 512
 LINE = 16
 QUADRANT = 32
 KS_ROW, KS_STEP, VS_ROW = 4, 8, 8
-V_AHEAD = 384
+CUTS = (0, 384, 896, 1536, T)
 SHARE = 128
 KEYS_AHEAD = 768
 
@@ -81,14 +81,16 @@ def tile_attend_sink_kernel(tc, qT, k_words, k_scales, vT, vs, sink, offs, out):
         nc.sync.dma_start(kw_pool[:].bitcast(I32)[:, KEYS_AHEAD:T], kw_rows[:, KEYS_AHEAD:T])
         load_queries(1)
         v_pool0 = sb("v_pool0", [P, T], F32)
-        nc.sync.dma_start(v_pool0[:, 0:V_AHEAD], vT[0:P, 0:V_AHEAD])
+        pieces = [slice(lo, hi) for lo, hi in zip(CUTS, CUTS[1:])]
+        nc.sync.dma_start(v_pool0[:, pieces[0]], vT[0:P, pieces[0]])
         ks_got = sb("ks_got", [P, B * N], U8)
         nc.vector.tensor_copy(ks_got[:], ks_pool[:].bitcast(U8).indirect(offsets[:]))
         for r in range(4):
             nc.sync.dma_start(
                 ks_plane[r:P:QUADRANT, :], ks_got[:].bitcast(I32)[KS_ROW + KS_STEP * r : P : QUADRANT, :]
             )
-        nc.sync.dma_start(v_pool0[:, V_AHEAD:T], vT[0:P, V_AHEAD:T])
+        for cols in pieces[1:]:
+            nc.sync.dma_start(v_pool0[:, cols], vT[0:P, cols])
 
         def quantize(codes, scales, values):
             nc.vector.quantize_mx(out=codes.bitcast(FP8X4), scales=scales, in_=values)
@@ -125,22 +127,22 @@ def tile_attend_sink_kernel(tc, qT, k_words, k_scales, vT, vs, sink, offs, out):
         nc.vector.tensor_copy(vs_got[0][:], vs_pool[:].indirect(listed(0)))
         nc.scalar.activation(vs_got[1][:], vs_pool[:].indirect(listed(1)), ACT.Copy)
 
-        def turn_vs(b, column, bank_index):
-            turned = bank(bank_index, "vs_turned%d" % b)
-            for t in range(PACK):
-                nc.tensor.transpose(turned[:, t * P : (t + 1) * P], vs_got[b][:, t:N:PACK], ident[:])
-            nc.scalar.copy(column, turned[:, VS_ROW:BANK:P])
-
         v_pool1 = late("v_pool1", [P, T], F32, 0)
         nc.sync.dma_start(v_pool1[:], vT[P : 2 * P, :])
+        vs_col1 = sb("vs_col1", [P, PACK], F32)
+        nc.sync.dma_start(vs_col1[:], vs_got[1][VS_ROW : VS_ROW + 1, :].rearrange("o (s t) -> o s t", t=PACK))
 
         kw_got = [first.tile([P, N], U32, name="kw_got%d" % b, offset=2560 - 2048 * b, align_bytes=64)[:] for b in range(B)]
         for b in range(B):
             nc.vector.tensor_copy(kw_got[b], kw_pool[:].indirect(listed(b)))
 
         q.append(prepare_queries(1))
-        vs_col = [sb("vs_col0", [P, PACK], F32, "q_raw1"), None]
-        turn_vs(0, vs_col[0][:], 7)
+
+        v_pool_bf = sb("v_pool_bf", [P, T], BF16)
+        for cols in pieces[:2]:
+            nc.scalar.activation(v_pool_bf[:, cols], v_pool0[:, cols], ACT.Copy)
+        for cols in pieces[2:]:
+            nc.gpsimd.tensor_copy(v_pool_bf[:, cols], v_pool0[:, cols])
 
         scores = []
         for b in range(B):
@@ -161,6 +163,10 @@ def tile_attend_sink_kernel(tc, qT, k_words, k_scales, vT, vs, sink, offs, out):
                 ALU.min,
                 accum_out=neg_max[:],
             )
+            if b == 0:
+                vs_turned = bank(0, "vs_turned")
+                for t in range(PACK):
+                    nc.tensor.transpose(vs_turned[:, t * P : (t + 1) * P], vs_got[0][:, t:N:PACK], ident[:])
             p = sb("p%d" % b, [P, N + 1], F32)
             nc.scalar.activation(
                 p[:], neg[:, b, 0 : N + 1], ACT.Exp, bias=neg_max[:], scale=-1.0, accum_out=total[:, b : b + 1]
@@ -170,61 +176,66 @@ def tile_attend_sink_kernel(tc, qT, k_words, k_scales, vT, vs, sink, offs, out):
                 nc.tensor.transpose(turned[:, t * P : (t + 1) * P], p[:, t * P : (t + 1) * P], ident[:])
             p_turned.append(turned)
 
-        vs_col[1] = sb("vs_col1", [P, PACK], F32, "neg_max1")
-        turn_vs(1, vs_col[1][:], 0)
+        vs_col0 = sb("vs_col0", [P, PACK], F32, "neg_max1")
+        nc.scalar.copy(vs_col0[:], vs_turned[:, VS_ROW:BANK:P])
 
-        def gather_values(h, pool):
+        def gather_values(h):
             got = [sb("v_got%d0" % h, [P, N], BF16, None if h else "neg"), sb("v_got%d1" % h, [P, N], BF16)]
+            pool = v_pool1 if h else v_pool0
             nc.vector.tensor_copy(got[1][:], pool[:].indirect(listed(1)))
             if h == 0:
-                nc.scalar.activation(got[0][:], pool[:].indirect(listed(0)), ACT.Copy)
+                nc.scalar.activation(got[0][:], v_pool_bf[:].indirect(listed(0)), ACT.Copy)
             else:
                 cut = (N - SHARE) // 16
                 nc.scalar.activation(got[0][:, N - SHARE : N], pool[:].indirect(listed(0)[:, cut:]), ACT.Copy)
                 nc.vector.tensor_copy(got[0][:, 0 : N - SHARE], pool[:].indirect(listed(0)[:, 0:cut]))
             return got
 
-        def turn_values(got, v_bf, turned):
+        def turn_values(got, values, turned):
             words = got[:].bitcast(F32)
             for u in range(2):
                 nc.tensor.transpose(turned[:, u * P : (u + 1) * P], words[:, u : 2 * P : 2], ident[:])
             nc.scalar.copy(
-                v_bf.bitcast(F32).rearrange("s (e u) -> s e u", u=2),
+                values.bitcast(F32).rearrange("s (e u) -> s e u", u=2),
                 turned[:, 0 : 2 * P].rearrange("s (u e) -> s e u", u=2),
             )
 
-        got0 = gather_values(0, v_pool0)
-        v_bf01 = sb("v_bf01", [P, N], BF16)
-        w_bf = sb("w_bf", [P, B, NQ * PACK], BF16)
-        for b in range(B):
+        def weigh(b, vs_col):
+            w_bf = sb("w_bf%d" % b, [P, NQ * PACK], BF16)
             nc.vector.tensor_tensor(
-                w_bf[:, b, :].rearrange("s (q t) -> s q t", t=PACK),
+                w_bf[:].rearrange("s (q t) -> s q t", t=PACK),
                 p_turned[b][:].rearrange("s (t q) -> s q t", t=PACK),
-                vs_col[b][:].unsqueeze(1).to_broadcast([P, NQ, PACK]),
+                vs_col[:].unsqueeze(1).to_broadcast([P, NQ, PACK]),
                 ALU.mult,
             )
+            return w_bf
 
+        v_bf01, v_bf11, v_bf10 = (sb(name, [P, N], BF16) for name in ("v_bf01", "v_bf11", "v_bf10"))
+        got0 = gather_values(0)
+        w_bf = [weigh(0, vs_col0)]
         turn_values(got0[1], v_bf01[:], bank(4, "v_turned01"))
-        got1 = gather_values(1, v_pool1)
-
+        got1 = gather_values(1)
         v_bf00 = late("v_bf00", [P, N], BF16, 0)
         turn_values(got0[0], v_bf00[:], bank(6, "v_turned00"))
-        inverse = late("inverse", [P, B], F32, 1024)
-        nc.vector.reciprocal(inverse[:], total[:])
-        w_codes = late("w_codes", [P, B * NQ], U32, 2048)
-        w_scales = sb("w_scales", [P, B * NQ], U8)
-        quantize(w_codes[:], w_scales[:], w_bf[:].rearrange("s b c -> s (b c)"))
-        w = [(w_codes[:, b * NQ : (b + 1) * NQ], w_scales[:, b * NQ : (b + 1) * NQ]) for b in range(B)]
-
-        v_bf11 = sb("v_bf11", [P, N], BF16)
         turn_values(got1[1], v_bf11[:], bank(3, "v_turned11"))
-        v_bf10 = sb("v_bf10", [P, N], BF16)
         turn_values(got1[0], v_bf10[:], bank(2, "v_turned10"))
+        w_bf.append(weigh(1, vs_col1))
 
-        def finish(b, h, v_bf, bank_index, on_vector, queue):
+        def quantize_weights(b):
+            codes = late("w_codes%d" % b, [P, NQ], U32, 2048 + 512 * b)
+            scales = sb("w_scales%d" % b, [P, NQ], U8)
+            quantize(codes[:], scales[:], w_bf[b][:])
+            return codes[:], scales[:]
+
+        inverse = late("inverse", [P, B], F32, 1024)
+        w = [quantize_weights(0)]
+        nc.vector.reciprocal(inverse[:], total[:])
+        w.append(quantize_weights(1))
+
+        def finish(b, h, values, bank_index, on_vector, queue):
             codes = late("v_codes%d%d" % (h, b), [P, P], U32, 4096 + 512 * (2 * h + b))
             scales = sb("v_scales%d%d" % (h, b), [P, P], U8)
-            quantize(codes[:], scales[:], v_bf[:])
+            quantize(codes[:], scales[:], values[:])
             sums = bank(bank_index, "y_sums%d%d" % (b, h))
             multiply(sums[:, 0:P], w[b], (codes[:], scales[:]))
             y = sb("y%d%d" % (b, h), [P, P], F32)
@@ -235,6 +246,6 @@ def tile_attend_sink_kernel(tc, qT, k_words, k_scales, vT, vs, sink, offs, out):
             queue.dma_start(out[b][:, h * P : (h + 1) * P], y[:])
 
         finish(1, 0, v_bf01, 1, False, nc.sync)
-        finish(0, 0, v_bf00, 4, False, nc.sync)
+        finish(0, 0, v_bf00, 0, False, nc.sync)
         finish(1, 1, v_bf11, 7, False, nc.scalar)
-        finish(0, 1, v_bf10, 5, True, nc.sync)
+        finish(0, 1, v_bf10, 4, True, nc.sync)

@@ -24,6 +24,7 @@ LINE = 16
 QUADRANT = 32
 KS_ROW, KS_STEP, VS_ROW = 4, 8, 8
 CUTS = (0, 384, 896, 1536, T)
+VS_SHARE = 384
 SHARE = 128
 KEYS_AHEAD = 768
 
@@ -124,8 +125,18 @@ def tile_attend_sink_kernel(tc, qT, k_words, k_scales, vT, vs, sink, offs, out):
         nc.scalar.activation(neg[:, :, N], sink_turned[:, 0:B], ACT.Copy, scale=-1.0)
 
         vs_got = [sb("vs_got%d" % b, [P, N], F32) for b in range(B)]
-        nc.vector.tensor_copy(vs_got[0][:], vs_pool[:].indirect(listed(0)))
+        vs_cut = VS_SHARE // 16
+        nc.scalar.activation(vs_got[0][:, VS_SHARE:N], vs_pool[:].indirect(listed(0)[:, vs_cut:]), ACT.Copy)
         nc.scalar.activation(vs_got[1][:], vs_pool[:].indirect(listed(1)), ACT.Copy)
+        nc.vector.tensor_copy(vs_got[0][:, 0:VS_SHARE], vs_pool[:].indirect(listed(0)[:, 0:vs_cut]))
+
+        def turn_vs(pair, bank_index):
+            turned = bank(bank_index, "vs_turned%d" % pair)
+            for u in range(2):
+                nc.tensor.transpose(turned[:, u * P : (u + 1) * P], vs_got[0][:, 2 * pair + u : N : PACK], ident[:])
+            return turned[:, VS_ROW : 2 * P : P]
+
+        vs_places01 = turn_vs(0, 7)
 
         v_pool1 = late("v_pool1", [P, T], F32, 0)
         nc.sync.dma_start(v_pool1[:], vT[P : 2 * P, :])
@@ -137,6 +148,9 @@ def tile_attend_sink_kernel(tc, qT, k_words, k_scales, vT, vs, sink, offs, out):
             nc.vector.tensor_copy(kw_got[b], kw_pool[:].indirect(listed(b)))
 
         q.append(prepare_queries(1))
+
+        vs_col0 = sb("vs_col0", [P, PACK], F32, "q_raw1")
+        nc.scalar.copy(vs_col0[:, 0:2], vs_places01)
 
         v_pool_bf = sb("v_pool_bf", [P, T], BF16)
         for cols in pieces[:2]:
@@ -164,23 +178,20 @@ def tile_attend_sink_kernel(tc, qT, k_words, k_scales, vT, vs, sink, offs, out):
                 accum_out=neg_max[:],
             )
             if b == 0:
-                vs_turned = bank(0, "vs_turned")
-                for t in range(PACK):
-                    nc.tensor.transpose(vs_turned[:, t * P : (t + 1) * P], vs_got[0][:, t:N:PACK], ident[:])
+                vs_places23 = turn_vs(1, 0)
             p = sb("p%d" % b, [P, N + 1], F32)
             nc.scalar.activation(
                 p[:], neg[:, b, 0 : N + 1], ACT.Exp, bias=neg_max[:], scale=-1.0, accum_out=total[:, b : b + 1]
             )
+            if b == 0:
+                nc.scalar.copy(vs_col0[:, 2:PACK], vs_places23)
             turned = bank(4 + b, "p_turned%d" % b)
             for t in range(PACK):
                 nc.tensor.transpose(turned[:, t * P : (t + 1) * P], p[:, t * P : (t + 1) * P], ident[:])
             p_turned.append(turned)
 
-        vs_col0 = sb("vs_col0", [P, PACK], F32, "neg_max1")
-        nc.scalar.copy(vs_col0[:], vs_turned[:, VS_ROW:BANK:P])
-
         def gather_values(h):
-            got = [sb("v_got%d0" % h, [P, N], BF16, None if h else "neg"), sb("v_got%d1" % h, [P, N], BF16)]
+            got = [sb("v_got%d%d" % (h, b), [P, N], BF16) for b in range(B)]
             pool = v_pool1 if h else v_pool0
             nc.vector.tensor_copy(got[1][:], pool[:].indirect(listed(1)))
             if h == 0:
@@ -200,44 +211,49 @@ def tile_attend_sink_kernel(tc, qT, k_words, k_scales, vT, vs, sink, offs, out):
                 turned[:, 0 : 2 * P].rearrange("s (u e) -> s e u", u=2),
             )
 
-        def weigh(b, vs_col):
-            w_bf = sb("w_bf%d" % b, [P, NQ * PACK], BF16)
+        def weigh(b, vs_col, w_bf):
             nc.vector.tensor_tensor(
                 w_bf[:].rearrange("s (q t) -> s q t", t=PACK),
                 p_turned[b][:].rearrange("s (t q) -> s q t", t=PACK),
                 vs_col[:].unsqueeze(1).to_broadcast([P, NQ, PACK]),
                 ALU.mult,
             )
-            return w_bf
+
+        def quantize_weights(b, codes):
+            scales = sb("w_scales%d" % b, [P, NQ], U8)
+            quantize(codes[:], scales[:], w_bf[b][:])
+            return codes[:], scales[:]
 
         v_bf01, v_bf11, v_bf10 = (sb(name, [P, N], BF16) for name in ("v_bf01", "v_bf11", "v_bf10"))
         got0 = gather_values(0)
-        w_bf = [weigh(0, vs_col0)]
+        w_bf = [sb("w_bf%d" % b, [P, NQ * PACK], BF16) for b in range(B)]
+        weigh(0, vs_col0, w_bf[0])
         turn_values(got0[1], v_bf01[:], bank(4, "v_turned01"))
         got1 = gather_values(1)
         v_bf00 = late("v_bf00", [P, N], BF16, 0)
         turn_values(got0[0], v_bf00[:], bank(6, "v_turned00"))
         turn_values(got1[1], v_bf11[:], bank(3, "v_turned11"))
         turn_values(got1[0], v_bf10[:], bank(2, "v_turned10"))
-        w_bf.append(weigh(1, vs_col1))
+        weigh(1, vs_col1, w_bf[1])
 
-        def quantize_weights(b):
-            codes = late("w_codes%d" % b, [P, NQ], U32, 2048 + 512 * b)
-            scales = sb("w_scales%d" % b, [P, NQ], U8)
-            quantize(codes[:], scales[:], w_bf[b][:])
-            return codes[:], scales[:]
-
-        inverse = late("inverse", [P, B], F32, 1024)
-        w = [quantize_weights(0)]
-        nc.vector.reciprocal(inverse[:], total[:])
-        w.append(quantize_weights(1))
-
-        def finish(b, h, values, bank_index, on_vector, queue):
+        def quantize_values(h, b, values):
             codes = late("v_codes%d%d" % (h, b), [P, P], U32, 4096 + 512 * (2 * h + b))
             scales = sb("v_scales%d%d" % (h, b), [P, P], U8)
             quantize(codes[:], scales[:], values[:])
+            return codes[:], scales[:]
+
+        w = [quantize_weights(0, late("w_codes0", [P, NQ], U32, 2048))]
+        inverse = late("inverse", [P, B], F32, 1024)
+        nc.vector.reciprocal(inverse[:], total[:])
+        v01 = quantize_values(0, 1, v_bf01)
+        w.append(quantize_weights(1, sb("w_codes1", [P, NQ], U32)))
+        v00 = quantize_values(0, 0, v_bf00)
+        v11 = quantize_values(1, 1, v_bf11)
+        v10 = quantize_values(1, 0, v_bf10)
+
+        def finish(b, h, v, bank_index, on_vector, queue):
             sums = bank(bank_index, "y_sums%d%d" % (b, h))
-            multiply(sums[:, 0:P], w[b], (codes[:], scales[:]))
+            multiply(sums[:, 0:P], w[b], v)
             y = sb("y%d%d" % (b, h), [P, P], F32)
             if on_vector:
                 nc.vector.tensor_scalar(y[:], sums[:, 0:P], inverse[:, b : b + 1], None, ALU.mult)
@@ -245,7 +261,7 @@ def tile_attend_sink_kernel(tc, qT, k_words, k_scales, vT, vs, sink, offs, out):
                 nc.scalar.activation(y[:], sums[:, 0:P], ACT.Copy, scale=inverse[:, b : b + 1])
             queue.dma_start(out[b][:, h * P : (h + 1) * P], y[:])
 
-        finish(1, 0, v_bf01, 1, False, nc.sync)
-        finish(0, 0, v_bf00, 0, False, nc.sync)
-        finish(1, 1, v_bf11, 7, False, nc.scalar)
-        finish(0, 1, v_bf10, 4, True, nc.sync)
+        finish(1, 0, v01, 1, False, nc.sync)
+        finish(0, 0, v00, 0, False, nc.sync)
+        finish(1, 1, v11, 7, False, nc.scalar)
+        finish(0, 1, v10, 4, True, nc.sync)

@@ -24,7 +24,7 @@ LINE = 16
 QUADRANT = 32
 KS_ROW, KS_STEP, VS_ROW = 4, 8, 8
 CUTS = (0, 384, 896, 1536, T)
-VS_SHARE = 384
+VS_SHARE = 448
 SHARE = 128
 KEYS_AHEAD = 768
 
@@ -149,9 +149,6 @@ def tile_attend_sink_kernel(tc, qT, k_words, k_scales, vT, vs, sink, offs, out):
 
         q.append(prepare_queries(1))
 
-        vs_col0 = sb("vs_col0", [P, PACK], F32, "q_raw1")
-        nc.scalar.copy(vs_col0[:, 0:2], vs_places01)
-
         v_pool_bf = sb("v_pool_bf", [P, T], BF16)
         for cols in pieces[:2]:
             nc.scalar.activation(v_pool_bf[:, cols], v_pool0[:, cols], ACT.Copy)
@@ -184,6 +181,8 @@ def tile_attend_sink_kernel(tc, qT, k_words, k_scales, vT, vs, sink, offs, out):
                 p[:], neg[:, b, 0 : N + 1], ACT.Exp, bias=neg_max[:], scale=-1.0, accum_out=total[:, b : b + 1]
             )
             if b == 0:
+                vs_col0 = sb("vs_col0", [P, PACK], F32, "neg_max0")
+                nc.scalar.copy(vs_col0[:, 0:2], vs_places01)
                 nc.scalar.copy(vs_col0[:, 2:PACK], vs_places23)
             turned = bank(4 + b, "p_turned%d" % b)
             for t in range(PACK):

@@ -25,7 +25,6 @@ QUADRANT = 32
 KS_ROW, KS_STEP, VS_ROW = 4, 8, 8
 CUTS = (0, 384, 896, 1536, T)
 VS_SHARE = 448
-SHARE = 128
 KEYS_AHEAD = 768
 
 
@@ -196,9 +195,7 @@ def tile_attend_sink_kernel(tc, qT, k_words, k_scales, vT, vs, sink, offs, out):
             if h == 0:
                 nc.scalar.activation(got[0][:], v_pool_bf[:].indirect(listed(0)), ACT.Copy)
             else:
-                cut = (N - SHARE) // 16
-                nc.scalar.activation(got[0][:, N - SHARE : N], pool[:].indirect(listed(0)[:, cut:]), ACT.Copy)
-                nc.vector.tensor_copy(got[0][:, 0 : N - SHARE], pool[:].indirect(listed(0)[:, 0:cut]))
+                nc.vector.tensor_copy(got[0][:], pool[:].indirect(listed(0)))
             return got
 
         def turn_values(got, values, turned):
@@ -228,9 +225,9 @@ def tile_attend_sink_kernel(tc, qT, k_words, k_scales, vT, vs, sink, offs, out):
         w_bf = [sb("w_bf%d" % b, [P, NQ * PACK], BF16) for b in range(B)]
         weigh(0, vs_col0, w_bf[0])
         turn_values(got0[1], v_bf01[:], bank(4, "v_turned01"))
-        got1 = gather_values(1)
-        v_bf00 = late("v_bf00", [P, N], BF16, 0)
+        v_bf00 = sb("v_bf00", [P, N], BF16)
         turn_values(got0[0], v_bf00[:], bank(6, "v_turned00"))
+        got1 = gather_values(1)
         turn_values(got1[1], v_bf11[:], bank(3, "v_turned11"))
         turn_values(got1[0], v_bf10[:], bank(2, "v_turned10"))
         weigh(1, vs_col1, w_bf[1])

@@ -25,7 +25,8 @@ QUADRANT = 32
 KS_ROW, KS_STEP, VS_ROW = 4, 8, 8
 CUTS = (0, 384, 896, 1536, T)
 VS_SHARE = 448
-KEYS_AHEAD = 768
+KEYS_AHEAD = 896
+LAST_SHARE = 128
 
 
 def tile_attend_sink_kernel(tc, qT, k_words, k_scales, vT, vs, sink, offs, out):
@@ -51,14 +52,13 @@ def tile_attend_sink_kernel(tc, qT, k_words, k_scales, vT, vs, sink, offs, out):
             return offsets[:, b * LIST_COLS : (b + 1) * LIST_COLS]
 
         ks_pool = sb("ks_pool", [P, T // 4], I32)
-        vs_pool = late("vs_pool", [P, T], F32, 0)
+        vs_pool = sb("vs_pool", [P, T], F32)
         sink_rows = sb("sink_rows", [P, NQ], F32)
         ident = sb("ident", [P, P], F32)
         nc.vector.memset(ks_pool[:], 0)
         nc.vector.memset(sink_rows[:], 0.0)
         nc.vector.memset(vs_pool[:].bitcast(I32), 0)
         ks_plane = sb("ks_plane", [P, B * N // 4], I32)
-        nc.vector.memset(ks_plane[:], 0)
         nc.vector.memset(ident[:], 0.0)
         make_identity(nc, ident[:], nomemset=True)
 
@@ -69,8 +69,8 @@ def tile_attend_sink_kernel(tc, qT, k_words, k_scales, vT, vs, sink, offs, out):
                 q_raw[b][:].rearrange("p j q -> p (j q)"), qT[b].rearrange("(p j) q -> p (j q)", j=PACK)
             )
 
-        nc.sync.dma_start(offsets[:], offs)
         load_queries(0)
+        nc.sync.dma_start(offsets[:], offs)
         ks_rows = k_scales[0].bitcast(I32)
         nc.sync.dma_start(ks_pool[KS_ROW:P:KS_STEP, :], ks_rows)
         nc.sync.dma_start(sink_rows[0:B, :], sink.rearrange("b q o -> b (q o)"))
@@ -123,7 +123,7 @@ def tile_attend_sink_kernel(tc, qT, k_words, k_scales, vT, vs, sink, offs, out):
         nc.tensor.transpose(sink_turned[:, 0:P], sink_rows[:], ident[:])
         nc.scalar.activation(neg[:, :, N], sink_turned[:, 0:B], ACT.Copy, scale=-1.0)
 
-        vs_got = [sb("vs_got%d" % b, [P, N], F32) for b in range(B)]
+        vs_got = [sb("vs_got0", [P, N], F32), first.tile([P, N], F32, name="vs_got1", offset=8192, align_bytes=64)]
         vs_cut = VS_SHARE // 16
         nc.scalar.activation(vs_got[0][:, VS_SHARE:N], vs_pool[:].indirect(listed(0)[:, vs_cut:]), ACT.Copy)
         nc.scalar.activation(vs_got[1][:], vs_pool[:].indirect(listed(1)), ACT.Copy)
@@ -193,15 +193,18 @@ def tile_attend_sink_kernel(tc, qT, k_words, k_scales, vT, vs, sink, offs, out):
             pool = v_pool1 if h else v_pool0
             nc.vector.tensor_copy(got[1][:], pool[:].indirect(listed(1)))
             if h == 0:
-                nc.scalar.activation(got[0][:], v_pool_bf[:].indirect(listed(0)), ACT.Copy)
+                dealt = got[0][:].rearrange("p (u s e) -> p s u e", u=2, e=2)
+                nc.scalar.activation(dealt, v_pool_bf[:].indirect(listed(0)), ACT.Copy)
             else:
-                nc.vector.tensor_copy(got[0][:], pool[:].indirect(listed(0)))
+                cut = N - LAST_SHARE
+                nc.vector.tensor_copy(got[0][:, 0:cut], pool[:].indirect(listed(0)[:, 0 : cut // 16]))
+                nc.scalar.activation(got[0][:, cut:N], pool[:].indirect(listed(0)[:, cut // 16 :]), ACT.Copy)
             return got
 
-        def turn_values(got, values, turned):
+        def turn_values(got, values, turned, dealt=False):
             words = got[:].bitcast(F32)
             for u in range(2):
-                nc.tensor.transpose(turned[:, u * P : (u + 1) * P], words[:, u : 2 * P : 2], ident[:])
+                nc.tensor.transpose(turned[:, u * P : (u + 1) * P], words[:, u * P : (u + 1) * P] if dealt else words[:, u : 2 * P : 2], ident[:])
             nc.scalar.copy(
                 values.bitcast(F32).rearrange("s (e u) -> s e u", u=2),
                 turned[:, 0 : 2 * P].rearrange("s (u e) -> s e u", u=2),
@@ -220,13 +223,15 @@ def tile_attend_sink_kernel(tc, qT, k_words, k_scales, vT, vs, sink, offs, out):
             quantize(codes[:], scales[:], w_bf[b][:])
             return codes[:], scales[:]
 
-        v_bf01, v_bf11, v_bf10 = (sb(name, [P, N], BF16) for name in ("v_bf01", "v_bf11", "v_bf10"))
+        v_bf11, v_bf10 = (sb(name, [P, N], BF16) for name in ("v_bf11", "v_bf10"))
+        v_bf00, v_bf01 = (
+            first.tile([P, N], BF16, name="v_bf0%d" % b, offset=8192 + 1024 * b, align_bytes=64) for b in range(B)
+        )
         got0 = gather_values(0)
         w_bf = [sb("w_bf%d" % b, [P, NQ * PACK], BF16) for b in range(B)]
         weigh(0, vs_col0, w_bf[0])
         turn_values(got0[1], v_bf01[:], bank(4, "v_turned01"))
-        v_bf00 = sb("v_bf00", [P, N], BF16)
-        turn_values(got0[0], v_bf00[:], bank(6, "v_turned00"))
+        turn_values(got0[0], v_bf00[:], bank(6, "v_turned00"), dealt=True)
         got1 = gather_values(1)
         turn_values(got1[1], v_bf11[:], bank(3, "v_turned11"))
         turn_values(got1[0], v_bf10[:], bank(2, "v_turned10"))

@@ -62,7 +62,9 @@ def tile_attend_sink_kernel(tc, qT, k_words, k_scales, vT, vs, sink, offs, out):
         nc.vector.memset(ident[:], 0.0)
         make_identity(nc, ident[:], nomemset=True)
 
-        q_raw = [sb("q_raw%d" % b, [P, PACK, NQ], F32) for b in range(B)]
+        q_raw = [
+            first.tile([P, PACK, NQ], F32, name="q_raw%d" % b, offset=12288 + 2048 * b, align_bytes=64) for b in range(B)
+        ]
 
         def load_queries(b):
             nc.sync.dma_start(
@@ -124,18 +126,11 @@ def tile_attend_sink_kernel(tc, qT, k_words, k_scales, vT, vs, sink, offs, out):
         nc.scalar.activation(neg[:, :, N], sink_turned[:, 0:B], ACT.Copy, scale=-1.0)
 
         vs_got = [sb("vs_got0", [P, N], F32), first.tile([P, N], F32, name="vs_got1", offset=8192, align_bytes=64)]
-        vs_cut = VS_SHARE // 16
-        nc.scalar.activation(vs_got[0][:, VS_SHARE:N], vs_pool[:].indirect(listed(0)[:, vs_cut:]), ACT.Copy)
         nc.scalar.activation(vs_got[1][:], vs_pool[:].indirect(listed(1)), ACT.Copy)
-        nc.vector.tensor_copy(vs_got[0][:, 0:VS_SHARE], vs_pool[:].indirect(listed(0)[:, 0:vs_cut]))
-
-        def turn_vs(pair, bank_index):
-            turned = bank(bank_index, "vs_turned%d" % pair)
-            for u in range(2):
-                nc.tensor.transpose(turned[:, u * P : (u + 1) * P], vs_got[0][:, 2 * pair + u : N : PACK], ident[:])
-            return turned[:, VS_ROW : 2 * P : P]
-
-        vs_places01 = turn_vs(0, 7)
+        nc.vector.tensor_copy(vs_got[0][:].rearrange("p (t s) -> p s t", t=PACK), vs_pool[:].indirect(listed(0)))
+        vs_turned = bank(7, "vs_turned")
+        for t in range(PACK):
+            nc.tensor.transpose(vs_turned[:, t * P : (t + 1) * P], vs_got[0][:, t * P : (t + 1) * P], ident[:])
 
         v_pool1 = late("v_pool1", [P, T], F32, 0)
         nc.sync.dma_start(v_pool1[:], vT[P : 2 * P, :])
@@ -147,6 +142,8 @@ def tile_attend_sink_kernel(tc, qT, k_words, k_scales, vT, vs, sink, offs, out):
             nc.vector.tensor_copy(kw_got[b], kw_pool[:].indirect(listed(b)))
 
         q.append(prepare_queries(1))
+        vs_col0 = first.tile([P, PACK], F32, name="vs_col0", offset=12288 + 2048, align_bytes=64)
+        nc.scalar.copy(vs_col0[:], vs_turned[:, VS_ROW : PACK * P : P])
 
         v_pool_bf = sb("v_pool_bf", [P, T], BF16)
         for cols in pieces[:2]:
@@ -173,16 +170,10 @@ def tile_attend_sink_kernel(tc, qT, k_words, k_scales, vT, vs, sink, offs, out):
                 ALU.min,
                 accum_out=neg_max[:],
             )
-            if b == 0:
-                vs_places23 = turn_vs(1, 0)
             p = sb("p%d" % b, [P, N + 1], F32)
             nc.scalar.activation(
                 p[:], neg[:, b, 0 : N + 1], ACT.Exp, bias=neg_max[:], scale=-1.0, accum_out=total[:, b : b + 1]
             )
-            if b == 0:
-                vs_col0 = sb("vs_col0", [P, PACK], F32, "neg_max0")
-                nc.scalar.copy(vs_col0[:, 0:2], vs_places01)
-                nc.scalar.copy(vs_col0[:, 2:PACK], vs_places23)
             turned = bank(4 + b, "p_turned%d" % b)
             for t in range(PACK):
                 nc.tensor.transpose(turned[:, t * P : (t + 1) * P], p[:, t * P : (t + 1) * P], ident[:])
@@ -191,14 +182,15 @@ def tile_attend_sink_kernel(tc, qT, k_words, k_scales, vT, vs, sink, offs, out):
         def gather_values(h):
             got = [sb("v_got%d%d" % (h, b), [P, N], BF16) for b in range(B)]
             pool = v_pool1 if h else v_pool0
-            nc.vector.tensor_copy(got[1][:], pool[:].indirect(listed(1)))
             if h == 0:
-                dealt = got[0][:].rearrange("p (u s e) -> p s u e", u=2, e=2)
-                nc.scalar.activation(dealt, v_pool_bf[:].indirect(listed(0)), ACT.Copy)
+                nc.vector.tensor_copy(got[1][:], pool[:].indirect(listed(1)))
+                nc.scalar.activation(got[0][:], v_pool_bf[:].indirect(listed(0)), ACT.Copy)
             else:
                 cut = N - LAST_SHARE
-                nc.vector.tensor_copy(got[0][:, 0:cut], pool[:].indirect(listed(0)[:, 0 : cut // 16]))
-                nc.scalar.activation(got[0][:, cut:N], pool[:].indirect(listed(0)[:, cut // 16 :]), ACT.Copy)
+                nc.vector.tensor_copy(got[1][:, 0:cut], pool[:].indirect(listed(1)[:, 0 : cut // 16]))
+                nc.scalar.activation(got[1][:, cut:N], pool[:].indirect(listed(1)[:, cut // 16 :]), ACT.Copy)
+                dealt = got[0][:].rearrange("p (u s e) -> p s u e", u=2, e=2)
+                nc.vector.tensor_copy(dealt, pool[:].indirect(listed(0)))
             return got
 
         def turn_values(got, values, turned, dealt=False):
@@ -231,10 +223,10 @@ def tile_attend_sink_kernel(tc, qT, k_words, k_scales, vT, vs, sink, offs, out):
         w_bf = [sb("w_bf%d" % b, [P, NQ * PACK], BF16) for b in range(B)]
         weigh(0, vs_col0, w_bf[0])
         turn_values(got0[1], v_bf01[:], bank(4, "v_turned01"))
-        turn_values(got0[0], v_bf00[:], bank(6, "v_turned00"), dealt=True)
+        turn_values(got0[0], v_bf00[:], bank(6, "v_turned00"))
         got1 = gather_values(1)
         turn_values(got1[1], v_bf11[:], bank(3, "v_turned11"))
-        turn_values(got1[0], v_bf10[:], bank(2, "v_turned10"))
+        turn_values(got1[0], v_bf10[:], bank(2, "v_turned10"), dealt=True)
         weigh(1, vs_col1, w_bf[1])
 
         def quantize_values(h, b, values):

from contextlib import ExitStack

import concourse.mybir as mybir
from concourse.masks import make_identity

B, N, T, D, DV, NQ = 2, 512, 2048, 512, 256, 128
FLOPS = 2 * B * NQ * N * (D + DV)

F32 = mybir.dt.float32
BF16 = mybir.dt.bfloat16
I32 = mybir.dt.int32
U32 = mybir.dt.uint32
U16 = mybir.dt.uint16
U8 = mybir.dt.uint8
FP8X4 = mybir.dt.float8_e4m3fn_x4
ALU = mybir.AluOpType
ACT = mybir.ActivationFunctionType

P = 128
PACK = 4
LIST_COLS = N // 16
BANK = 512
LINE = 16
QUADRANT = 32
KS_ROW, KS_STEP, VS_ROW = 4, 8, 8
CUTS = (0, 384, 896, 1536, T)
VS_SHARE = 448
KEYS_AHEAD = 896
LAST_SHARE = 128


def tile_attend_sink_kernel(tc, qT, k_words, k_scales, vT, vs, sink, offs, out):
    nc = tc.nc
    with ExitStack() as ctx:
        held = ctx.enter_context(tc.tile_pool(name="held", bufs=1))
        last = ctx.enter_context(tc.tile_pool(name="last", bufs=1))
        first = ctx.enter_context(tc.tile_pool(name="first", bufs=1))
        psum = ctx.enter_context(tc.psum_pool(name="psum", bufs=1))

        def sb(name, shape, dtype, tag=None):
            return held.tile(shape, dtype, name=name, tag=tag or name, align_bytes=64)

        def late(name, shape, dtype, offset):
            return last.tile(shape, dtype, name=name, offset=offset, align_bytes=64)

        def bank(index, name):
            return psum.tile([P, BANK], F32, name=name, tag="bank%d" % index)

        offsets = held.tile([P, B * LIST_COLS], U16, name="offsets")

        def listed(b):
            return offsets[:, b * LIST_COLS : (b + 1) * LIST_COLS]

        ks_pool = sb("ks_pool", [P, T // 4], I32)
        vs_pool = sb("vs_pool", [P, T], F32)
        sink_rows = sb("sink_rows", [P, NQ], F32)
        ident = sb("ident", [P, P], F32)
        nc.vector.memset(ks_pool[:], 0)
        nc.vector.memset(sink_rows[:], 0.0)
        nc.vector.memset(vs_pool[:].bitcast(I32), 0)
        ks_plane = sb("ks_plane", [P, B * N // 4], I32)
        nc.vector.memset(ident[:], 0.0)
        make_identity(nc, ident[:], nomemset=True)

        q_raw = [
            first.tile([P, PACK, NQ], F32, name="q_raw%d" % b, offset=12288 + 2048 * b, align_bytes=64) for b in range(B)
        ]

        def load_queries(b):
            nc.sync.dma_start(
                q_raw[b][:].rearrange("p j q -> p (j q)"), qT[b].rearrange("(p j) q -> p (j q)", j=PACK)
            )

        load_queries(0)
        nc.sync.dma_start(offsets[:], offs)
        ks_rows = k_scales[0].bitcast(I32)
        nc.sync.dma_start(ks_pool[KS_ROW:P:KS_STEP, :], ks_rows)
        nc.sync.dma_start(sink_rows[0:B, :], sink.rearrange("b q o -> b (q o)"))
        kw_pool = sb("kw_pool", [P, T], U32)
        kw_rows = k_words[0].rearrange("p n r -> p (n r)").bitcast(I32)
        nc.sync.dma_start(kw_pool[:].bitcast(I32)[:, 0:KEYS_AHEAD], kw_rows[:, 0:KEYS_AHEAD])
        nc.sync.dma_start(vs_pool[VS_ROW : VS_ROW + 1, :], vs[0:1, :])
        nc.sync.dma_start(kw_pool[:].bitcast(I32)[:, KEYS_AHEAD:T], kw_rows[:, KEYS_AHEAD:T])
        load_queries(1)
        v_pool0 = sb("v_pool0", [P, T], F32)
        pieces = [slice(lo, hi) for lo, hi in zip(CUTS, CUTS[1:])]
        nc.sync.dma_start(v_pool0[:, pieces[0]], vT[0:P, pieces[0]])
        ks_got = sb("ks_got", [P, B * N], U8)
        nc.vector.tensor_copy(ks_got[:], ks_pool[:].bitcast(U8).indirect(offsets[:]))
        for r in range(4):
            nc.sync.dma_start(
                ks_plane[r:P:QUADRANT, :], ks_got[:].bitcast(I32)[KS_ROW + KS_STEP * r : P : QUADRANT, :]
            )
        for cols in pieces[1:]:
            nc.sync.dma_start(v_pool0[:, cols], vT[0:P, cols])

        def quantize(codes, scales, values):
            nc.vector.quantize_mx(out=codes.bitcast(FP8X4), scales=scales, in_=values)

        def multiply(acc, stationary, moving):
            nc.tensor.matmul_mx(
                out=acc,
                lhsT=stationary[0].bitcast(FP8X4),
                lhsT_scale=stationary[1],
                rhs=moving[0].bitcast(FP8X4),
                rhs_scale=moving[1],
                start=True,
                stop=True,
            )

        def prepare_queries(b):
            q_bf = first.tile([P, NQ, PACK], BF16, name="q_bf%d" % b, offset=2048 + 4096 * b, align_bytes=64)
            nc.scalar.copy(
                q_bf[:].rearrange("p (c i) j -> p c j i", i=PACK),
                q_raw[b][:].rearrange("p j (c i) -> p c j i", i=PACK),
            )
            codes = sb("q_codes%d" % b, [P, NQ], U32)
            scales = sb("q_scales%d" % b, [P, NQ], U8)
            quantize(codes[:], scales[:], q_bf[:].rearrange("p q j -> p (q j)"))
            return codes[:], scales[:]

        q = [prepare_queries(0)]
        neg = sb("neg", [P, B, N + LINE], F32)
        sink_turned = bank(2, "sink_turned")
        nc.tensor.transpose(sink_turned[:, 0:P], sink_rows[:], ident[:])
        nc.scalar.activation(neg[:, :, N], sink_turned[:, 0:B], ACT.Copy, scale=-1.0)

        vs_got = [sb("vs_got0", [P, N], F32), first.tile([P, N], F32, name="vs_got1", offset=8192, align_bytes=64)]
        nc.scalar.activation(vs_got[1][:], vs_pool[:].indirect(listed(1)), ACT.Copy)
        nc.vector.tensor_copy(vs_got[0][:].rearrange("p (t s) -> p s t", t=PACK), vs_pool[:].indirect(listed(0)))
        vs_turned = bank(7, "vs_turned")
        for t in range(PACK):
            nc.tensor.transpose(vs_turned[:, t * P : (t + 1) * P], vs_got[0][:, t * P : (t + 1) * P], ident[:])

        v_pool1 = late("v_pool1", [P, T], F32, 0)
        nc.sync.dma_start(v_pool1[:], vT[P : 2 * P, :])
        vs_col1 = sb("vs_col1", [P, PACK], F32)
        nc.sync.dma_start(vs_col1[:], vs_got[1][VS_ROW : VS_ROW + 1, :].rearrange("o (s t) -> o s t", t=PACK))

        kw_got = [first.tile([P, N], U32, name="kw_got%d" % b, offset=2560 - 2048 * b, align_bytes=64)[:] for b in range(B)]
        for b in range(B):
            nc.vector.tensor_copy(kw_got[b], kw_pool[:].indirect(listed(b)))

        q.append(prepare_queries(1))
        vs_col0 = first.tile([P, PACK], F32, name="vs_col0", offset=12288 + 2048, align_bytes=64)
        nc.scalar.copy(vs_col0[:], vs_turned[:, VS_ROW : PACK * P : P])

        v_pool_bf = sb("v_pool_bf", [P, T], BF16)
        for cols in pieces[:2]:
            nc.scalar.activation(v_pool_bf[:, cols], v_pool0[:, cols], ACT.Copy)
        for cols in pieces[2:]:
            nc.gpsimd.tensor_copy(v_pool_bf[:, cols], v_pool0[:, cols])

        scores = []
        for b in range(B):
            acc = bank(b, "scores%d" % b)
            multiply(acc[:], q[b], (kw_got[b], ks_plane[:].bitcast(U8)[:, b * N : (b + 1) * N]))
            scores.append(acc)

        total = sb("total", [P, B], F32)
        p_turned = []
        for b in range(B):
            neg_max = sb("neg_max%d" % b, [P, 1], F32)
            nc.vector.tensor_scalar(
                neg[:, b, 0:N].rearrange("p (t s) -> p t s", t=PACK),
                scores[b][:].rearrange("p (s t) -> p t s", t=PACK),
                -1.0,
                neg[:, b, N : N + 1],
                ALU.mult,
                ALU.min,
                accum_out=neg_max[:],
            )
            p = sb("p%d" % b, [P, N + 1], F32)
            nc.scalar.activation(
                p[:], neg[:, b, 0 : N + 1], ACT.Exp, bias=neg_max[:], scale=-1.0, accum_out=total[:, b : b + 1]
            )
            turned = bank(4 + b, "p_turned%d" % b)
            for t in range(PACK):
                nc.tensor.transpose(turned[:, t * P : (t + 1) * P], p[:, t * P : (t + 1) * P], ident[:])
            p_turned.append(turned)

        def gather_values(h):
            got = [sb("v_got%d%d" % (h, b), [P, N], BF16) for b in range(B)]
            pool = v_pool1 if h else v_pool0
            if h == 0:
                nc.vector.tensor_copy(got[1][:], pool[:].indirect(listed(1)))
                nc.scalar.activation(got[0][:], v_pool_bf[:].indirect(listed(0)), ACT.Copy)
            else:
                cut = N - LAST_SHARE
                nc.vector.tensor_copy(got[1][:, 0:cut], pool[:].indirect(listed(1)[:, 0 : cut // 16]))
                nc.scalar.activation(got[1][:, cut:N], pool[:].indirect(listed(1)[:, cut // 16 :]), ACT.Copy)
                dealt = got[0][:].rearrange("p (u s e) -> p s u e", u=2, e=2)
                nc.vector.tensor_copy(dealt, pool[:].indirect(listed(0)))
            return got

        def turn_values(got, values, turned, dealt=False):
            words = got[:].bitcast(F32)
            for u in range(2):
                nc.tensor.transpose(turned[:, u * P : (u + 1) * P], words[:, u * P : (u + 1) * P] if dealt else words[:, u : 2 * P : 2], ident[:])
            nc.scalar.copy(
                values.bitcast(F32).rearrange("s (e u) -> s e u", u=2),
                turned[:, 0 : 2 * P].rearrange("s (u e) -> s e u", u=2),
            )

        def weigh(b, vs_col, w_bf):
            nc.vector.tensor_tensor(
                w_bf[:].rearrange("s (q t) -> s q t", t=PACK),
                p_turned[b][:].rearrange("s (t q) -> s q t", t=PACK),
                vs_col[:].unsqueeze(1).to_broadcast([P, NQ, PACK]),
                ALU.mult,
            )

        def quantize_weights(b, codes):
            scales = sb("w_scales%d" % b, [P, NQ], U8)
            quantize(codes[:], scales[:], w_bf[b][:])
            return codes[:], scales[:]

        v_bf11, v_bf10 = (sb(name, [P, N], BF16) for name in ("v_bf11", "v_bf10"))
        v_bf00, v_bf01 = (
            first.tile([P, N], BF16, name="v_bf0%d" % b, offset=8192 + 1024 * b, align_bytes=64) for b in range(B)
        )
        got0 = gather_values(0)
        w_bf = [sb("w_bf%d" % b, [P, NQ * PACK], BF16) for b in range(B)]
        weigh(0, vs_col0, w_bf[0])
        turn_values(got0[1], v_bf01[:], bank(4, "v_turned01"))
        turn_values(got0[0], v_bf00[:], bank(6, "v_turned00"))
        got1 = gather_values(1)
        turn_values(got1[1], v_bf11[:], bank(3, "v_turned11"))
        turn_values(got1[0], v_bf10[:], bank(2, "v_turned10"), dealt=True)
        weigh(1, vs_col1, w_bf[1])

        def quantize_values(h, b, values):
            codes = late("v_codes%d%d" % (h, b), [P, P], U32, 4096 + 512 * (2 * h + b))
            scales = sb("v_scales%d%d" % (h, b), [P, P], U8)
            quantize(codes[:], scales[:], values[:])
            return codes[:], scales[:]

        w = [quantize_weights(0, late("w_codes0", [P, NQ], U32, 2048))]
        inverse = late("inverse", [P, B], F32, 1024)
        nc.vector.reciprocal(inverse[:], total[:])
        v01 = quantize_values(0, 1, v_bf01)
        w.append(quantize_weights(1, sb("w_codes1", [P, NQ], U32)))
        v00 = quantize_values(0, 0, v_bf00)
        v11 = quantize_values(1, 1, v_bf11)
        v10 = quantize_values(1, 0, v_bf10)

        def finish(b, h, v, bank_index, on_vector, queue):
            sums = bank(bank_index, "y_sums%d%d" % (b, h))
            multiply(sums[:, 0:P], w[b], v)
            y = sb("y%d%d" % (b, h), [P, P], F32)
            if on_vector:
                nc.vector.tensor_scalar(y[:], sums[:, 0:P], inverse[:, b : b + 1], None, ALU.mult)
            else:
                nc.scalar.activation(y[:], sums[:, 0:P], ACT.Copy, scale=inverse[:, b : b + 1])
            queue.dma_start(out[b][:, h * P : (h + 1) * P], y[:])

        finish(1, 0, v01, 1, False, nc.sync)
        finish(0, 0, v00, 0, False, nc.sync)
        finish(1, 1, v11, 7, False, nc.scalar)
        finish(0, 1, v10, 4, True, nc.sync)
